import numpy as np, ml_dtypes
CORES = [8,136,40,168]
N = 4
BF = ml_dtypes.bfloat16
W, LN, HO, TH = 2048, 256, 7, 67
def spot(a, s, k):
    return ((a * s >> 5) + a + 37 * s + k) & (W - 1)
def parts(rng):
    return (rng.integers(0, 16, (N, 8, 16, W)), rng.integers(0, W, (N, 8, 16, LN)), rng.integers(0, 16, (N, 8, 16, LN)), rng.integers(0, 16, (N, 8, 16, LN)),
            rng.integers(0, W, (N, 8, LN)), rng.integers(0, W, (N, 8, 16)))
def pack(X, P, A, R, s, K):
    b = lambda v, n: np.ascontiguousarray(np.reshape(v, (N, 128, n))).astype(np.float32).astype(BF)
    return {"x": b(X, W), "pn": np.ascontiguousarray(P.reshape(N, 128, LN)).astype(np.int32), "a0": b(A, LN), "r0": b(R, LN),
            "s0": np.ascontiguousarray(s).astype(np.int32), "kap": np.ascontiguousarray(K.reshape(N, 128, 1)).astype(np.int32)}
def setup_inputs(rng):
    return pack(*parts(rng))
def setup_inputs_spread(rng):
    X, P, A, R, s, K = parts(rng); lg = W.bit_length() - 1
    def small(n):
        top = rng.integers(0, 16, (N, 8, 1, n)); return np.minimum((rng.random((N, 8, 16, n)) * (top + 1)).astype(np.int64), top)
    def skew(*sh):
        v = np.minimum(np.exp2(lg * rng.random(sh)).astype(np.int64) - 1, W - 1); return np.where(rng.random(sh) < 0.5, v, W - 1 - v)
    X, P, A, R, s, K = small(W), skew(N, 8, 16, LN), small(LN), small(LN), skew(N, 8, LN), skew(N, 8, 16)
    pairs = ((3, 21), (21, 3), (5, 19), (19, 5), (7, 9), (9, 7))
    for q in range(N):
        for g in range(0, 8, 2):
            u, v = pairs[int(rng.integers(0, 6))]; l = int(rng.integers(0, LN))
            s[q, g, l] = W - u; K[q, g] = (W - v - spot(P[q, g, :, l], W - u, 0)) & (W - 1)
    return pack(X, P, A, R, s, K)
def setup_inputs_ends(rng):
    e = W - 1; bit = lambda *sh: rng.integers(0, 2, sh)
    def ends(n):
        v = 15 * bit(N, 8, 16, n); return np.where(rng.random((N, 8, 1, n)) < 0.5, v[:, :, :1], v)
    X, A, R = ends(W), ends(LN), ends(LN); P, s, K = e * bit(N, 8, 16, LN), e * bit(N, 8, LN), e * bit(N, 8, 16)
    K[:, :, 15] = 0; K[:, :, 14] = e
    for l in (0, 1, 6, LN - 2, LN - 1): P[..., l] = e; s[..., l] = e
    s[..., 3] = 0; s[..., LN - 3] = 0
    lo = sorted(set(spot(a, 0, k) for a in (0, e) for k in (0, e))); hi = sorted(set(spot(a, e, k) for a in (0, e) for k in (0, e)))
    w = bit(N, 8, 1, 1); o = rng.permutation(N - 1)
    for q, far in ((N - 1, 1), (int(o[0]), 0), (int(o[1]), 1)):
        X[q][:, :, lo] = 15 * w[q]; X[q][:, :, hi] = 15 * (1 - w[q])
        A[q] = 15 * ((w[q] + (s[q][:, None, :] > 0) + far) & 1)
    c = int(o[1]); A[c, 7, :, LN - 1] = 15 - A[c, 7, :, LN - 1]
    return pack(X, P, A, R, s, K)
def setup_inputs_corners(rng):
    X, P, A, R, s, K = parts(rng); off = int(rng.integers(0, 4)); H = W // 2; row = np.arange(16)[:, None]
    for q in range(N):
        for g in range(8):
            m = (q + g + off) % 4
            if m == 0:
                c = rng.integers(0, 16, (16, 1)); X[q, g] = c; A[q, g] = c; R[q, g] = c
            elif m == 1:
                c = 15 * int(rng.integers(0, 2)); X[q, g] = c; A[q, g] = 15 - c; R[q, g] = 15 - c
                if g >= 4:
                    s[q, g] = int(rng.integers(0, 32)); P[q, g, 0] = rng.permutation(H)[:LN]
            elif m == 2:
                c = 15 * int(rng.integers(0, 2)); X[q, g, :, :H] = c; X[q, g, :, H:] = 15 - c; A[q, g] = c; R[q, g] = np.where(rng.random(LN) < 0.5, c, 15 - c)
                kind = rng.integers(0, 8, LN); kind[:8] = np.arange(8); kind[LN - 8:] = rng.permutation(8)
                rows = row + np.zeros((1, LN), np.int64)
                mk = np.stack([rows < 0, rows == 0, rows == 15, (rows == 0) | (rows == 15), rows < 15, rows == rng.integers(0, 16, (1, LN)), rows >= 0, rows == 14])
                near = mk[kind, :, np.arange(LN)].T
                site = np.where(rng.random((16, LN)) < 0.3, (H - 1) * rng.integers(0, 2, (16, LN)), rng.integers(0, H, (16, LN))) + np.where(near, 0, H)
                s[q, g] = 0; P[q, g] = (site - K[q, g][:, None]) & (W - 1)
            else:
                s[q, g] = rng.choice(np.array([0, 1, H, W - 1]), LN); K[q, g] = (W - 1) * rng.integers(0, 2, 16)
                P[q, g] = np.where(rng.random((16, LN)) < 0.4, s[q, g][None, :], (W - 1) * rng.integers(0, 2, (16, LN)))
    return pack(X, P, A, R, s, K)
def setup_inputs_crowd(rng):
    X, P, A, R, s, K = parts(rng); h = LN // 2
    P[:, 3] = P[:, 3, :1]
    P[:, ::2] = P[:, ::2, :, :1].copy(); s[:, ::2] = s[:, ::2, :1].copy()
    P[:, 1:7:2, :, h:] = P[:, 1:7:2, :, :h][..., ::-1].copy(); s[:, 1:7:2, h:] = s[:, 1:7:2, :h][..., ::-1].copy()
    P[:, 7, :, 1::2] = P[:, 7, :, ::2].copy(); s[:, 7, 1::2] = s[:, 7, ::2].copy()
    for g in (0, 6):
        A[:, g] = rng.integers(8, 16, (N, 16, LN))
        for q in range(N): X[q, g][:, spot(P[q, g, :, 0], s[q, g, 0], K[q, g])] = 0
    return pack(X, P, A, R, s, K)
def gaps(rng):
    n = np.where(rng.random((N, 8, 1, LN)) < 0.4, TH - 1, TH + rng.integers(0, 17, (N, 8, 1, LN))); n[..., 0] = TH; n[..., LN - 1] = TH - 1
    return n
def dist(rng, z, n):
    i = np.argsort(rng.random((N, 8, 16, LN)), axis=2)
    return np.abs(z - ((n + i) >> 4))
def setup_inputs_ties(rng):
    X, P, A, R, s, K = parts(rng)
    z = 15 * rng.integers(0, 2, (N, 8, 1, W)); z[:, ::2] = z[:, ::2, :, :1].copy()
    zl = 15 * rng.integers(0, 2, (N, 8, 1, LN)); zl[:, ::2] = z[:, ::2, :, :1]
    c = int(rng.integers(0, N)); b = (c - 1) % N; a = (c - 2) % N
    zc = 15 * ((np.arange(8) // 2 + int(rng.integers(0, 2))) & 1)[:, None, None]
    z[c] = zc
    for q in (a, b): z[q, ::2] = zc[::2]
    for q in (a, b, c): zl[q] = zc
    na, nr = gaps(rng), gaps(rng)
    na[b] = TH - 1; nr[b] = TH - 1; na[c] = TH - 1; na[c, :, 0, 0] = TH
    e = int(rng.integers(1, 8)); gs = rng.integers(0, 8, e); ls = 1 + rng.permutation(LN - 2)[:e]
    na[c, gs, 0, ls] = TH + rng.integers(0, 17, e)
    X[:] = z
    return pack(X, P, dist(rng, zl, na), dist(rng, zl, nr), s, K)
def check_inputs(d):
    bad = []
    for k, lo, hi in (("x", 0, 15), ("pn", 0, W - 1), ("a0", 0, 15), ("r0", 0, 15), ("s0", 0, W - 1), ("kap", 0, W - 1)):
        v = np.asarray(d[k]).astype(np.float64)
        if not np.all((v >= lo) & (v <= hi) & (v == np.floor(v))): bad.append("range of " + k)
    return bad
def reference(x, pn, a0, r0, s0, kap):
    X = x.astype(np.float32).astype(np.int64).reshape(N, 8, 16, W); P = pn.astype(np.int64).reshape(N, 8, 16, LN)
    A = a0.astype(np.float32).astype(np.int64).reshape(N, 8, 16, LN); R = r0.astype(np.float32).astype(np.int64).reshape(N, 8, 16, LN)
    s = s0.astype(np.int64); K = kap.astype(np.int64).reshape(N, 8, 16, 1)
    p = np.zeros((N, 8, LN), np.int64); ex = np.zeros((N, 8, LN), np.int64); missed = np.zeros(N, np.int64); row = np.arange(16)[:, None]
    for t in range(HO):
        last = missed; missed = np.zeros(N, np.int64)
        for r in range(N):
            q = (r + t) % N
            h = spot(P[r], s[r][:, None, :], K[q])
            v = np.take_along_axis(X[q], h.reshape(8, 1, 16 * LN), 2).reshape(8, 16, 16, LN)
            dd = np.add.reduce(np.abs(v - A[r][:, :, None, :]), axis=1)
            near = (dd < TH + (last[q] & 15)) & (row >= p[r][:, None, :]); hit = np.any(near, axis=1)
            k = np.where(hit, 15 - np.argmax(near[:, ::-1], axis=1), p[r])
            hk = np.take_along_axis(h, k[:, None, :], 1)[:, 0]
            back = ((s[r] * hk >> 5) + s[r] + 811 * t) & (W - 1)
            new = np.where((row >= p[r][:, None, :]) & (row <= k[:, None, :]), back[:, None, :], P[r])
            turn = ~hit | (k == 15); tu = turn[:, None, :]
            for g in range(8):
                m = np.flatnonzero(~hit[g]); place, first = np.unique(hk[g][m], return_index=True); lane = m[first]
                X[q, g][:, place] = (X[q, g][:, place] + A[r, g][:, lane]) >> 1
            missed[q] = np.count_nonzero(~hit)
            P[r] = np.where(tu, new[:, ::-1], new); p[r] = np.where(turn, 15 - k, k + 1); s[r] = hk; ex[r] = ex[r] ^ turn
            A[r], R[r] = np.where(tu, R[r], A[r]), np.where(tu, A[r], R[r])
    at = [(q - (HO - 1)) % N for q in range(N)]
    return {"yn": P[at].reshape(N, 128, LN).astype(np.float32), "ys": s[at].astype(np.float32), "yp": (p[at] + 16 * ex[at]).astype(np.float32),
            "yx": X.reshape(N, 128, W).astype(np.float32).astype(BF)}

@@ -1,0 +1,474 @@
+from concourse.mybir import AluOpType, AxisListType, ActivationFunctionType
+
+A_ = AluOpType
+F_ = ActivationFunctionType
+HOPS = 7
+NX = 2080
+RELU = 1
+
+SCRATCH = {}
+PART = {}
+for _b, _d, _w, _ns in (("f32s", "float32", 16, ("so", "y1", "po", "jk", "ge", "pa", "pb", "G", "Fv", "hg", "tt", "sC", "U2", "KD")),
+                        ("i32s", "int32", 16, ("ip", "inn", "il", "irv", "idl", "CI", "li", "rvi", "kl", "hs", "W2", "v2", "tb", "qq", "bb", "pq"))):
+    SCRATCH[_b] = ("sbuf", [128, _w * len(_ns)], _d)
+    for _k, _n in enumerate(_ns):
+        PART[_n] = (_b, _w * _k, 8 if _n in ("ge", "pa", "pb", "idl") else _w)
+
+
+def _sb(n, w, d):
+    if n not in PART:
+        SCRATCH[n] = ("sbuf", [128, w], d)
+
+
+for _n, _w, _d in (
+    ("X", NX, "bfloat16"), ("AR", 2048, "bfloat16"), ("DR", 4096, "bfloat16"), ("DA", 4096, "bfloat16"),
+    ("LE", 2048, "bfloat16"), ("LP", 2048, "bfloat16"), ("L2", 2048, "bfloat16"), ("KI", 2048, "bfloat16"), ("KU", 256, "bfloat16"), ("DG", 2048, "float16"),
+    ("MC", 48 * HOPS, "float16"), ("MP", 256 * HOPS, "float16"), ("CO", 48 * HOPS, "float16"), ("PO", 256 * HOPS, "float16"),
+    ("PI", 256, "int32"), ("SI", 16, "int32"), ("KA", 1, "int32"),
+    ("ia", 128, "int32"), ("ib", 128, "int32"), ("ip", 16, "int32"), ("inn", 16, "int32"), ("il", 16, "int32"),
+    ("idl", 8, "int32"), ("irv", 16, "int32"), ("DUM", 16, "int32"), ("bmi", 128, "int32"), ("CI", 16, "int32"),
+    ("li", 16, "int32"), ("ge", 8, "float32"), ("pa", 8, "float32"), ("pb", 8, "float32"), ("rvi", 16, "int32"),
+    ("Ib", 128, "bfloat16"), ("NI", 128, "bfloat16"), ("I4k", 128, "bfloat16"), ("N4k", 128, "bfloat16"),
+    ("NB", 128, "bfloat16"), ("N128", 128, "bfloat16"), ("N2k", 128, "bfloat16"), ("If", 128, "float16"),
+    ("I16", 128, "float16"), ("I32", 128, "float16"), ("I1184", 128, "float16"), ("BM", 128, "bfloat16"), ("BMf", 128, "float16"),
+    ("B8", 8, "bfloat16"), ("ONE", 512, "bfloat16"), ("Z0", 128, "bfloat16"), ("F25", 128, "bfloat16"), ("F376", 128, "bfloat16"),
+    ("Fm256", 128, "bfloat16"), ("Fm", 128, "bfloat16"), ("F16", 128, "bfloat16"),
+    ("REP", 16, "uint16"), ("RK", 16, "uint16"), ("RVK", 16, "uint16"), ("RVP", 16, "uint16"), ("PRE", 8, "uint16"), ("PRL", 8, "uint16"),
+    ("SEL", 16, "float16"), ("LT", 16, "float16"), ("kf", 1, "float32"), ("rk", 16, "float16"), ("KC", 16, "float32"),
+    ("KTa", 256, "float16"), ("KTb", 256, "float16"), ("KD", 16, "float32"),
+    ("TH", 128, "bfloat16"), ("AO", 16, "uint16"), ("AC", 256, "bfloat16"), ("T1", 256, "bfloat16"), ("I64k", 128, "bfloat16"),
+    ("Z", 256, "float32"), ("ZI", 256, "int32"), ("HI", 256, "int32"), ("H16", 256, "uint16"), ("HK", 256, "float32"), ("FL", 256, "float32"),
+    ("M", 64, "float32"), ("M2", 32, "float32"), ("Wv", 16, "int32"), ("kl", 16, "int32"), ("kc", 16, "float16"), ("hs", 16, "int32"),
+    ("W2", 16, "int32"), ("tt", 16, "float32"), ("v2", 16, "int32"), ("hg", 16, "float32"), ("tb", 16, "int32"), ("qq", 16, "int32"),
+    ("bb", 16, "int32"), ("b16", 16, "float16"), ("pq", 16, "int32"), ("sC", 16, "float32"), ("U2", 16, "float32"),
+    ("hu", 16, "uint16"), ("hit", 16, "bfloat16"), ("key", 16, "float32"), ("KL", 128, "float32"), ("eq", 128, "bfloat16"),
+    ("G", 16, "float32"), ("Fv", 16, "float32"), ("FT", 128, "float16"), ("fo", 32, "uint16"), ("old", 256, "bfloat16"),
+    ("nv", 256, "int32"), ("R2", 256, "bfloat16"), ("tP", 256, "float16"), ("jk", 16, "float32"), ("mc", 1, "float32"),
+    ("mi", 1, "int32"), ("mj", 1, "int32"), ("mt", 1, "float32"),
+    ("Pf", 256, "float32"), ("Pv", 256, "float32"), ("ya", 256, "float32"), ("yb", 256, "float32"), ("yo", 256, "float32"),
+    ("so", 16, "float32"), ("y1", 16, "float32"), ("po", 16, "float32"),
+):
+    _sb(_n, _w, _d)
+PS = ("E0", "E1", "Q0", "Q1", "SK", "CC", "RG", "OB")
+for _n in PS:
+    SCRATCH[_n] = ("psum", [128, 512], "float32")
+
+SEMAPHORES = (["qv", "qs", "qp", "qg", "snd", "lx", "la", "lr", "lk", "lz", "lpy", "lps", "oy", "oz"]
+              + ["mc%d" % t for t in range(1, HOPS)] + ["mp%d" % t for t in range(1, HOPS)] + ["ar%d" % d for d in (1, 2, 3)])
+
+
+def rank_program(g, core, T, topo):
+    rank = T.rank_of(core)
+    if rank is None:
+        return
+    n = len(T.cores)
+    nxt, prv = T.cores[(rank + 1) % n], T.cores[(rank - 1) % n]
+    Q = {"v": g.vector, "s": g.scalar, "p": g.tensor, "g": g, "y": g.sync}
+    QS = {"v": "qv", "s": "qs", "p": "qp", "g": "qg"}
+    cnt = {q: 0 for q in Q}
+    seen = {q: {} for q in Q}
+    log = {}
+    sent = [0]
+
+    def view(name, a=0, b=None, st=1):
+        if name in PART:
+            name, o, w = PART[name]
+            a, b = o + a, o + (w if b is None else b)
+        b = SCRATCH[name][1][1] if b is None else b
+        ap = T[name][:, a:b] if st == 1 else T[name][:, a:b:st]
+        return (ap, name, a, b)
+
+    def need(q, ev):
+        if seen[q].get(ev[0], 0) < ev[1]:
+            seen[q][ev[0]] = ev[1]
+            Q[q].wait_ge(T.sem[ev[0]], ev[1])
+
+    def order(q, outs, ins):
+        todo = {}
+        for vs, wr in ((ins, False), (outs, True)):
+            for _, nm, a, b in vs:
+                ps = nm in PS
+                for (q2, a2, b2, w2), ev in log.get(nm, {}).items():
+                    hitx = a < b2 and a2 < b
+                    dep = (hitx and w2 and not (wr and ps)) or (q2 != q and ((hitx and (wr or w2)) or ps))
+                    if dep and todo.get(ev[0], 0) < ev[1]:
+                        todo[ev[0]] = ev[1]
+        for k in sorted(todo):
+            need(q, (k, todo[k]))
+
+    def note(q, outs, ins, ev):
+        for vs, wr in ((ins, False), (outs, True)):
+            for _, nm, a, b in vs:
+                d = log.setdefault(nm, {})
+                if wr and nm not in PS:
+                    for k in [k for k in d if a <= k[1] and k[2] <= b]:
+                        del d[k]
+                d[(q, a, b, wr)] = ev
+
+    def emit(q, fn, outs, ins):
+        order(q, outs, ins)
+        cnt[q] += 1
+        fn().then_inc(T.sem[QS[q]], 1)
+        note(q, outs, ins, (QS[q], cnt[q]))
+
+    def tt(o, a, b, op):
+        emit("v", lambda: g.vector.tensor_tensor(o[0], a[0], b[0], op), [o], [a, b])
+
+    def tti(o, win, off, b, op):
+        emit("v", lambda: g.vector.tensor_tensor(o[0], win[0].indirect(off[0]), b[0], op), [o], [win, off, b])
+
+    def ts(o, a, s1, op0, s2=None, op1=None):
+        col = isinstance(s1, tuple)
+        sc = s1[0] if col else s1
+        if op1 is None:
+            f = lambda: g.vector.tensor_scalar(o[0], a[0], sc, None, op0)
+        else:
+            f = lambda: g.vector.tensor_scalar(o[0], a[0], sc, s2, op0, op1)
+        emit("v", f, [o], [a] + ([s1] if col else []))
+
+    def cp(o, a):
+        emit("v", lambda: g.vector.tensor_copy(o[0], a[0]), [o], [a])
+
+    def cpi(o, win, off):
+        emit("v", lambda: g.vector.tensor_copy(o[0], win[0].indirect(off[0])), [o], [win, off])
+
+    def scat(win, off, a):
+        emit("v", lambda: g.vector.tensor_copy(win[0].indirect(off[0]), a[0]), [win], [off, a])
+
+    def ms(o, c):
+        emit("v", lambda: g.vector.memset(o[0], c), [o], [])
+
+    def act(o, a, f=F_.Copy, scale=1.0):
+        if isinstance(scale, tuple):
+            emit("s", lambda: g.scalar.activation(o[0], a[0], f, scale=scale[0]), [o], [a, scale])
+        else:
+            emit("s", lambda: g.scalar.activation(o[0], a[0], f, scale=scale), [o], [a])
+
+    def acti(o, win, off):
+        emit("s", lambda: g.scalar.activation(o[0], win[0].indirect(off[0]), F_.Copy), [o], [win, off])
+
+    def mm(o, l, r, start, stop):
+        emit("p", lambda: g.tensor.matmul(o[0], l[0], r[0], start, stop), [o], [l, r])
+
+    def iota(nm, pat, base, cm):
+        o = view(nm)
+        emit("g", lambda: g.iota(o[0], pat, base, cm), [o], [])
+
+    def load(q, o, src, sem, total=16):
+        order(q, [o], [])
+        Q[q].dma_start(o[0], src).then_inc(T.sem[sem], 16)
+        note("dma", [o], [], (sem, total))
+
+    def send(dst, o, a, sem):
+        order("g", [], [a])
+        rid, pid = topo.addr(dst, core)
+        g.remote_dma(o[0], a[0], T.sem[sem], T.sem.snd, pid, rid, topo.mask(core, dst))
+        sent[0] += len(topo.engines(core, dst))
+
+    load("y", view("SI"), T.s0[:], "lz")
+    load("s", view("KA"), T.kap[:], "lk")
+    for k in range(16):
+        q, sem = (("y", "lpy"), ("s", "lps"))[k % 2]
+        load(q, view("PI", 16 * k, 16 * k + 16), T.pn[k::16, :], sem, 128)
+    load("y", view("AR", 0, 256), T.a0[:], "la")
+    load("s", view("AR", 256, 512), T.r0[:], "lr")
+    load("y", view("X", 0, 2048), T.x[:], "lx")
+
+    iota("ia", [[-1, 128]], 0, 1)
+    iota("ib", [[-16, 8], [0, 16]], 0, 1)
+    iota("ip", [[0, 16]], 0, 1)
+    iota("inn", [[1, 16]], 0, 0)
+    iota("il", [[1, 16]], 0, 16)
+    iota("irv", [[-16, 16]], 240, 0)
+    iota("idl", [[1, 8]], 1, 0)
+    iota("DUM", [[2, 16]], 2048, 0)
+    ts(view("Ib"), view("ia"), 0, A_.is_equal)
+    ts(view("If"), view("ia"), 0, A_.is_equal)
+    ts(view("bmi"), view("ib"), 4, A_.arith_shift_right)
+    ts(view("CI"), view("ip"), 15, A_.bitwise_and)
+    ts(view("li"), view("il"), 255, A_.bitwise_and)
+    ts(view("BM"), view("bmi"), 0, A_.is_equal)
+    ts(view("BMf"), view("bmi"), 0, A_.is_equal)
+    tt(view("SEL"), view("CI"), view("inn"), A_.is_equal)
+    cp(view("REP"), view("CI"))
+    cp(view("RK"), view("inn"))
+    ts(view("RVK"), view("inn"), -1, A_.mult, 15, A_.add)
+    ts(view("LT"), view("li"), 128, A_.add)
+    ms(view("ONE"), 1.0)
+    ms(view("F25"), 0.25)
+    ts(view("I32"), view("If"), 32.0, A_.mult)
+    ts(view("I16"), view("If"), 16.0, A_.mult)
+    ts(view("I1184"), view("If"), 1184.0, A_.mult)
+    for nm, c in (("NI", -1.0), ("N128", -128.0), ("I4k", 4096.0), ("N4k", -4096.0), ("NB", -262144.0), ("N2k", -2048.0), ("I64k", 65536.0)):
+        act(view(nm), view("Ib"), scale=c)
+    for k in range(16):
+        act(view("KI", 128 * k, 128 * k + 128), view("Ib"), scale=7.5 - k)
+    cp(view("kf"), view("KA"))
+    ts(view("rk"), view("SEL"), view("kf"), A_.mult)
+    mm(view("Q1", 0, 16), view("BMf"), view("rk"), True, True)
+    cp(view("KC"), view("Q1", 0, 16))
+    cpi(view("KTa"), view("KC"), view("RK"))
+    cpi(view("KTb"), view("KC"), view("RVK"))
+    ms(view("F376"), 376.0)
+    ms(view("Fm256"), -256.0)
+    ms(view("TH"), 67.0 * 512)
+    ms(view("LE"), 0.0)
+    ts(view("B8"), view("BM", 0, 128, 16), -65536.0, A_.mult)
+    for i in range(16):
+        cp(view("LE", 128 * i + i, 128 * i + 128, 16), view("B8"))
+    ms(view("Z0"), 0.0)
+    ms(view("Fm"), -1.0 / 4096)
+    ms(view("F16"), 16.0)
+    tt(view("ge"), view("CI", 0, 8), view("idl"), A_.is_ge)
+    ts(view("pb"), view("idl"), -1, A_.mult, 16, A_.add)
+    tt(view("rvi"), view("irv"), view("CI"), A_.add)
+    tt(view("pa"), view("ge"), view("idl"), A_.mult)
+    ts(view("ge"), view("ge"), -1, A_.mult, 1, A_.add)
+    cp(view("RVP"), view("rvi"))
+    tt(view("pa"), view("CI", 0, 8), view("pa"), A_.subtract)
+    tt(view("pb"), view("pb"), view("ge"), A_.mult)
+    tt(view("KD"), view("KTa", 0, 256, 16), view("KTb", 0, 256, 16), A_.subtract)
+    cp(view("PRE"), view("pa"))
+    tt(view("pb"), view("CI", 0, 8), view("pb"), A_.add)
+    for k in range(16):
+        ts(view("DG", 128 * k, 128 * k + 128), view("I16"), view("KD", k, k + 1), A_.mult)
+    cp(view("PRL"), view("pb"))
+    cp(view("MC", 0, 16), view("SI"))
+    ts(view("MC", 16, 32), view("inn"), 0, A_.mult, 1, A_.add)
+    ts(view("MC", 32, 48), view("inn"), 0, A_.mult, -7.5, A_.add)
+    cp(view("MP", 0, 256), view("PI"))
+    for d in (1, 2, 3):
+        send(T.cores[(rank + d) % n], view("AR", 512 * d, 512 * d + 512), view("AR", 0, 512), "ar%d" % d)
+
+    outs = {}
+
+    def store(q, out, a, sem):
+        order(q, [], [a])
+        Q[q].dma_start(out, a[0]).then_inc(T.sem[sem], 16)
+        outs[sem] = outs.get(sem, 0) + 16
+
+    def finish_names(U):
+        acti(view("Pv"), view("Pf"), view("RVP"))
+        mm(view("SK", 0, 256), view("F16"), view("ONE", 0, 256), True, False)
+        for k in range(16):
+            mm(view("SK", 16 * k, 16 * k + 16), view("N2k"), U, False, k == 15)
+        ts(view("y1"), U, -8.0, A_.mult, 8.0, A_.add)
+        cp(view("so"), view("hs"))
+        tt(view("po"), view("pq"), view("y1"), A_.add)
+        tt(view("yb"), view("Pf"), view("SK", 0, 256), A_.subtract)
+        tt(view("SK", 0, 256), view("Pv"), view("SK", 0, 256), A_.min)
+        tt(view("yo"), view("SK", 0, 256), view("yb"), A_.max)
+        for k in range(16):
+            store(("y", "s")[k % 2], T.yn[k::16, :], view("yo", 16 * k, 16 * k + 16), ("oy", "oz")[k % 2])
+        store("y", T.ys[:], view("so"), "oy")
+        store("s", T.yp[:], view("po"), "oz")
+
+    for t in range(HOPS):
+        last = t == HOPS - 1
+        s_, U, pc = (view("MC", 48 * t + 16 * x, 48 * t + 16 * x + 16) for x in range(3))
+        P = view("MP", 256 * t, 256 * t + 256)
+        if t:
+            ne = len(topo.engines(prv, core))
+            note("rem", [view("MC", 48 * t, 48 * t + 48)], [], ("mc%d" % t, ne))
+            note("rem", [P], [], ("mp%d" % t, ne))
+        d = t % n
+        if 1 <= t <= 3:
+            note("rem", [view("AR", 512 * d, 512 * d + 512)], [], ("ar%d" % d, len(topo.engines(T.cores[(rank - d) % n], core))))
+        mm(view("OB", 256, 512), view("F25"), view("ONE", 0, 256), True, False)
+        if t:
+            mm(view("SK", 256, 512), view("I16"), view("KTa"), True, False)
+            mm(view("SK", 256, 512), view("I16"), view("KTb"), False, False)
+        else:
+            mm(view("SK", 256, 512), view("I32"), view("KTa"), True, False)
+        mm(view("Q0", 0, 16), view("N128"), U, True, False)
+        mm(view("Q0", 0, 16), view("If"), view("LT"), False, True)
+        cp(view("AO"), view("Q0", 0, 16))
+        acti(view("AC"), view("AR", 512 * d, 512 * d + 512), view("AO"))
+        for k in range(16):
+            mm(view("OB", 256 + 16 * k, 272 + 16 * k), view("If"), s_, False, k == 15)
+        for k in range(16):
+            o = view("SK", 256 + 16 * k, 272 + 16 * k)
+            if t:
+                mm(o, view("DG", 128 * k, 128 * k + 128), U, False, False)
+            mm(o, view("I1184"), s_, False, k == 15)
+        for k in range(16):
+            mm(view("RG", 256 + 16 * k, 272 + 16 * k), view("KI", 128 * k, 128 * k + 128), U, True, True)
+        act(view("KU"), view("RG", 256, 512))
+        ts(view("sC"), s_, 32.0, A_.mult, 25952.0 * t, A_.add)
+        ts(view("U2"), U, 2.0, A_.mult)
+        for a in (0, 128):
+            b = a + 128
+            tt(view("Z", a, b), view("MP", 256 * t + a, 256 * t + b), view("OB", 256 + a, 256 + b), A_.mult)
+            tt(view("ZI", a, b), view("Z", a, b), view("SK", 256 + a, 256 + b), A_.add)
+            ts(view("HI", a, b), view("ZI", a, b), 5, A_.arith_shift_right, 2047, A_.bitwise_and)
+            cp(view("H16", a, b), view("HI", a, b))
+        mm(view("RG", 0, 256), view("Ib"), view("KU"), True, False)
+        for k in range(16):
+            mm(view("RG", 16 * k, 16 * k + 16), view("If"), pc, False, k == 15)
+
+        def bounds():
+            act(view("T1"), view("RG", 0, 256), F_.Relu)
+            mm(view("CC", 0, 256), view("F376"), view("ONE", 0, 256), True, False)
+            mm(view("CC", 0, 256), view("N2k"), view("KU"), False, False)
+            mm(view("CC", 0, 256), view("NB"), view("T1"), False, True)
+            mm(view("CC", 256, 512), view("Fm256"), view("ONE", 0, 256), True, False)
+            mm(view("CC", 256, 512), view("I64k"), view("KU"), False, False)
+            for k in range(16):
+                mm(view("CC", 256 + 16 * k, 272 + 16 * k), view("I64k"), pc, False, k == 15)
+
+        W_ = view("X", 0, 2048)
+
+        def grow(k):
+            acti(view("DR", 256 * k, 256 * k + 256), W_, view("H16", 16 * k, 16 * k + 16))
+
+        def psub(c):
+            q = "Q%d" % (c % 2)
+            mm(view(q, 0, 512), view("Ib"), view("DR", 1024 * c, 1024 * c + 512), True, False)
+            mm(view(q, 0, 256), view("NI"), view("AC"), False, False)
+            mm(view(q, 256, 512), view("NI"), view("AC"), False, True)
+
+        def vrows(*ks):
+            for k in ks:
+                tti(view("DR", 256 * k, 256 * k + 256), W_, view("H16", 16 * k, 16 * k + 16), view("AC"), A_.subtract)
+
+        def absps(c):
+            act(view("DA", 1024 * c, 1024 * c + 512), view("Q%d" % (c % 2), 0, 512), F_.Abs)
+
+        def absrows(k, k2):
+            act(view("DA", 256 * k, 256 * k2), view("DR", 256 * k, 256 * k2), F_.Abs)
+
+        def dsum(c):
+            o = view("E%d" % (c % 2), 0, 64)
+            mm(o, view("TH"), view("ONE", 0, 64), True, False)
+            for nm, src in ((("LP", "DR"), ("L2", "DA")) if c == RELU else (("LE", "DA"),)):
+                for i in range(16):
+                    mm(o, view(nm, 128 * i, 128 * i + 128), view(src, 1024 * c + i, 1024 * c + 1024, 16), False, i == 15 and nm != "LP")
+
+        def decide(c):
+            e = view("E%d" % (c % 2), 0, 64)
+            tt(e, e, view("FL", 64 * c, 64 * c + 64), A_.max)
+            if c == 0:
+                tt(view("M"), e, view("HK", 0, 64), A_.min)
+            else:
+                tt(e, e, view("HK", 64 * c, 64 * c + 64), A_.min)
+                tt(view("M"), e, view("M"), A_.max)
+
+        if t == 0:
+            ts(view("LP"), view("LE"), -1.0, A_.mult)
+            ts(view("L2"), view("LE"), 2.0, A_.mult)
+        grow(0)
+        grow(1)
+        psub(0)
+        vrows(2, 3)
+        grow(8)
+        bounds()
+        absps(0)
+        absrows(2, 4)
+        dsum(0)
+        vrows(4, 5, 6, 7)
+        ts(view("DA", 1024, 2048), view("DR", 1024, 2048), 0.0, A_.max)
+        grow(9)
+        psub(2)
+        dsum(1)
+        tt(view("HK"), view("HI"), view("CC", 0, 256), A_.add)
+        tt(view("FL"), view("HK"), view("CC", 256, 512), A_.add)
+        vrows(10, 11)
+        grow(12)
+        absps(2)
+        decide(0)
+        decide(1)
+        vrows(14)
+        grow(13)
+        psub(3)
+        absrows(10, 12)
+        dsum(2)
+        vrows(15)
+        absps(3)
+        absrows(14, 15)
+        absrows(15, 16)
+        dsum(3)
+        mm(view("RG", 256, 512), view("Ib"), view("KU"), True, False)
+        mm(view("OB", 0, 256), view("I4k"), view("T1"), True, False)
+        mm(view("CC", 0, 256), view("N4k"), view("T1"), True, False)
+        decide(2)
+        decide(3)
+        tt(view("M2"), view("M", 0, 32), view("M", 32, 64), A_.max)
+        tt(view("Wv"), view("M2", 0, 16), view("M2", 16, 32), A_.max)
+        w = view("Wv")
+        sn, Un, pn_ = (view("CO", 48 * t + 16 * x, 48 * t + 16 * x + 16) for x in range(3))
+        ts(view("kl"), w, 11, A_.arith_shift_right, 15, A_.bitwise_and)
+        ts(view("hs"), w, 2047, A_.bitwise_and)
+        ts(view("hit"), w, 32768, A_.is_ge, 4096, A_.mult)
+        ts(view("kc"), view("kl"), -7.5, A_.add)
+        for k in range(16):
+            mm(view("RG", 256 + 16 * k, 272 + 16 * k), view("If"), view("kc"), False, k == 15)
+        tt(view("tt"), s_, view("hs"), A_.mult)
+        tt(view("key"), view("hs"), view("hit"), A_.add)
+        ts(view("W2"), w, 2048, A_.add)
+        acti(view("KL"), view("key"), view("PRL"))
+        tt(view("tb"), view("tt"), view("sC"), A_.add)
+        ts(view("v2"), view("W2"), 10, A_.arith_shift_right, 62, A_.bitwise_and)
+        ts(view("bb"), view("tb"), 5, A_.arith_shift_right, 2047, A_.bitwise_and)
+        ts(view("hg"), view("v2"), 33, A_.is_gt, -0.5, A_.add)
+        cp(view("b16"), view("bb"))
+        tt(view("qq"), view("v2"), view("hg"), A_.mult)
+        cp(sn, view("hs"))
+        ts(view("pq"), view("qq"), 15, A_.bitwise_and)
+        tt(Un, view("U2"), view("hg"), A_.mult)
+        ts(pn_, view("pq"), -7.5, A_.add)
+        act(view("R2"), view("RG", 256, 512), F_.Relu, -1.0)
+        for k in range(16):
+            if k == 10:
+                mm(view("OB", 0, 256), view("I4k"), view("R2"), False, True)
+            mm(view("CC", 16 * k, 16 * k + 16), view("If"), view("b16"), False, False)
+        mm(view("CC", 0, 256), view("N4k"), view("R2"), False, True)
+        if not last:
+            send(nxt, view("MC", 48 * t + 48, 48 * t + 96), view("CO", 48 * t, 48 * t + 48), "mc%d" % (t + 1))
+        tti(view("eq"), view("key"), view("PRE"), view("KL"), A_.is_equal)
+        cp(view("hu"), view("hs"))
+        acti(view("old"), W_, view("hu"))
+        tt(view("tP"), P, view("OB", 0, 256), A_.min)
+        if not last:
+            tt(view("PO", 256 * t, 256 * t + 256), view("tP"), view("CC", 0, 256), A_.max)
+            send(nxt, view("MP", 256 * t + 256, 256 * t + 512), view("PO", 256 * t, 256 * t + 256), "mp%d" % (t + 1))
+        else:
+            tt(view("Pf"), view("tP"), view("CC", 0, 256), A_.max)
+        mm(view("E0", 0, 16), view("Z0"), view("ONE", 0, 16), True, False)
+        for dl in range(1, 9):
+            a = 16 * (dl - 1)
+            mm(view("E0", dl, 16), view("I4k"), view("eq", a + dl, a + 16), False, dl == 8)
+            if dl < 8:
+                mm(view("E0", 16 - dl, 16), view("I4k"), view("eq", a, a + dl), False, False)
+        mm(view("Q1", 0, 256), view("Ib"), view("old"), True, False)
+        mm(view("Q1", 0, 256), view("Ib"), view("AC"), False, True)
+        tt(view("G"), view("key"), view("E0", 0, 16), A_.max)
+        tt(view("Fv"), view("G"), view("DUM"), A_.min)
+        tti(view("FT"), view("Fv"), view("REP", 0, 8), view("BM"), A_.mult)
+        mm(view("Q0", 0, 16), view("FT"), view("SEL"), True, True)
+        ts(view("nv"), view("Q1", 0, 256), 0.5, A_.mult, -0.25, A_.add)
+        if last:
+            finish_names(Un)
+        cp(view("fo", 0, 32, 2), view("Q0", 0, 16))
+        if not last:
+            mm(view("E1", 0, 16), view("Fm"), view("hit"), True, True)
+            o, i_, m_ = view("jk"), view("E1", 0, 16), view("mc")
+            emit("s", lambda: g.scalar.activation(o[0], i_[0], F_.Copy, accum_out=m_[0]), [o, m_], [i_])
+        for i in range(15, -1, -1):
+            scat(view("X", 0, NX), view("fo", 2 * i, 2 * i + 1), view("nv", i, 256, 16))
+            if not last:
+                if i == 11:
+                    ts(view("mi"), view("mc"), 2048, A_.add)
+                if i == 7:
+                    ts(view("mj"), view("mi"), 15, A_.bitwise_and)
+                if i == 3:
+                    ts(view("mt"), view("mj"), 67, A_.add, 512, A_.mult)
+        if not last:
+            act(view("TH"), view("ONE", 0, 128), F_.Copy, view("mt"))
+
+    store("y", T.yx[:], view("X", 0, 2048), "oy")
+    for q in ("v", "s", "p", "g"):
+        need("g", (QS[q], cnt[q]))
+    for sem in outs:
+        need("g", (sem, outs[sem]))
+    for sem, val in (("lx", 16), ("la", 16), ("lr", 16), ("lk", 16), ("lz", 16), ("lpy", 128), ("lps", 128), ("snd", sent[0])):
+        need("g", (sem, val))

@@ -1,59 +1,55 @@
-from concourse.mybir import AluOpType, AxisListType, ActivationFunctionType
+from concourse.mybir import AluOpType, ActivationFunctionType
 
 A_ = AluOpType
 F_ = ActivationFunctionType
 HOPS = 7
-NX = 2080
-RELU = 1
+NX = 2064
+BIG = 2.0 ** 22
+ROUND16 = 1.5 * 2 ** 27
+EYES = {"NI": -1.0, "I16": 16.0, "I1184": 1184.0, "N128": -128.0, "N2": -2.0, "I2k": 2048.0, "Ikp": 135168.0, "Nkp": -135168.0,
+        "NB": -2.0 ** 23, "I32k": 32768.0, "N64k": -65536.0, "Ikm": 126976.0, "N32k": -32768.0, "I32": 32.0, "Ihit": 1.0 / 256,
+        "I4k": 4096.0, "N4k": -4096.0, "N2k": -2048.0}
 
 SCRATCH = {}
 PART = {}
-for _b, _d, _w, _ns in (("f32s", "float32", 16, ("so", "y1", "po", "jk", "ge", "pa", "pb", "G", "Fv", "hg", "tt", "sC", "U2", "KD")),
-                        ("i32s", "int32", 16, ("ip", "inn", "il", "irv", "idl", "CI", "li", "rvi", "kl", "hs", "W2", "v2", "tb", "qq", "bb", "pq"))):
-    SCRATCH[_b] = ("sbuf", [128, _w * len(_ns)], _d)
-    for _k, _n in enumerate(_ns):
-        PART[_n] = (_b, _w * _k, 8 if _n in ("ge", "pa", "pb", "idl") else _w)
 
 
-def _sb(n, w, d):
-    if n not in PART:
-        SCRATCH[n] = ("sbuf", [128, w], d)
+def _shared(buf, dtype, width, names):
+    SCRATCH[buf] = ("sbuf", [128, width * len(names)], dtype)
+    for k, n in enumerate(names):
+        PART[n] = (buf, width * k, width)
 
 
+_shared("eyes", "bfloat16", 128, ["Ib"] + list(EYES))
+_shared("cols", "float32", 4, ("p16", "q31", "c3", "p256", "dum", "kf", "mc", "m1", "m2", "m3"))
+_shared("i64", "int32", 64, ("w", "hs", "pi", "ub", "tb", "bb"))
+_shared("f64", "float32", 64, ("M", "M2", "M4", "tt", "fa"))
+_shared("u32", "uint16", 32, ("DUP1", "DUP2", "fo"))
+_shared("u16", "uint16", 16, ("UN1", "UN2", "RVP", "RK", "RVK", "AO", "hu", "REP"))
+_shared("i16", "int32", 16, ("inn", "ip", "q15", "q31i", "idl"))
 for _n, _w, _d in (
     ("X", NX, "bfloat16"), ("AR", 2048, "bfloat16"), ("DR", 4096, "bfloat16"), ("DA", 4096, "bfloat16"),
-    ("LE", 2048, "bfloat16"), ("LP", 2048, "bfloat16"), ("L2", 2048, "bfloat16"), ("KI", 2048, "bfloat16"), ("KU", 256, "bfloat16"), ("DG", 2048, "float16"),
-    ("MC", 48 * HOPS, "float16"), ("MP", 256 * HOPS, "float16"), ("CO", 48 * HOPS, "float16"), ("PO", 256 * HOPS, "float16"),
-    ("PI", 256, "int32"), ("SI", 16, "int32"), ("KA", 1, "int32"),
-    ("ia", 128, "int32"), ("ib", 128, "int32"), ("ip", 16, "int32"), ("inn", 16, "int32"), ("il", 16, "int32"),
-    ("idl", 8, "int32"), ("irv", 16, "int32"), ("DUM", 16, "int32"), ("bmi", 128, "int32"), ("CI", 16, "int32"),
-    ("li", 16, "int32"), ("ge", 8, "float32"), ("pa", 8, "float32"), ("pb", 8, "float32"), ("rvi", 16, "int32"),
-    ("Ib", 128, "bfloat16"), ("NI", 128, "bfloat16"), ("I4k", 128, "bfloat16"), ("N4k", 128, "bfloat16"),
-    ("NB", 128, "bfloat16"), ("N128", 128, "bfloat16"), ("N2k", 128, "bfloat16"), ("If", 128, "float16"),
-    ("I16", 128, "float16"), ("I32", 128, "float16"), ("I1184", 128, "float16"), ("BM", 128, "bfloat16"), ("BMf", 128, "float16"),
-    ("B8", 8, "bfloat16"), ("ONE", 512, "bfloat16"), ("Z0", 128, "bfloat16"), ("F25", 128, "bfloat16"), ("F376", 128, "bfloat16"),
-    ("Fm256", 128, "bfloat16"), ("Fm", 128, "bfloat16"), ("F16", 128, "bfloat16"),
-    ("REP", 16, "uint16"), ("RK", 16, "uint16"), ("RVK", 16, "uint16"), ("RVP", 16, "uint16"), ("PRE", 8, "uint16"), ("PRL", 8, "uint16"),
-    ("SEL", 16, "float16"), ("LT", 16, "float16"), ("kf", 1, "float32"), ("rk", 16, "float16"), ("KC", 16, "float32"),
-    ("KTa", 256, "float16"), ("KTb", 256, "float16"), ("KD", 16, "float32"),
-    ("TH", 128, "bfloat16"), ("AO", 16, "uint16"), ("AC", 256, "bfloat16"), ("T1", 256, "bfloat16"), ("I64k", 128, "bfloat16"),
-    ("Z", 256, "float32"), ("ZI", 256, "int32"), ("HI", 256, "int32"), ("H16", 256, "uint16"), ("HK", 256, "float32"), ("FL", 256, "float32"),
-    ("M", 64, "float32"), ("M2", 32, "float32"), ("Wv", 16, "int32"), ("kl", 16, "int32"), ("kc", 16, "float16"), ("hs", 16, "int32"),
-    ("W2", 16, "int32"), ("tt", 16, "float32"), ("v2", 16, "int32"), ("hg", 16, "float32"), ("tb", 16, "int32"), ("qq", 16, "int32"),
-    ("bb", 16, "int32"), ("b16", 16, "float16"), ("pq", 16, "int32"), ("sC", 16, "float32"), ("U2", 16, "float32"),
-    ("hu", 16, "uint16"), ("hit", 16, "bfloat16"), ("key", 16, "float32"), ("KL", 128, "float32"), ("eq", 128, "bfloat16"),
-    ("G", 16, "float32"), ("Fv", 16, "float32"), ("FT", 128, "float16"), ("fo", 32, "uint16"), ("old", 256, "bfloat16"),
-    ("nv", 256, "int32"), ("R2", 256, "bfloat16"), ("tP", 256, "float16"), ("jk", 16, "float32"), ("mc", 1, "float32"),
-    ("mi", 1, "int32"), ("mj", 1, "int32"), ("mt", 1, "float32"),
-    ("Pf", 256, "float32"), ("Pv", 256, "float32"), ("ya", 256, "float32"), ("yb", 256, "float32"), ("yo", 256, "float32"),
-    ("so", 16, "float32"), ("y1", 16, "float32"), ("po", 16, "float32"),
+    ("LE", 144, "bfloat16"), ("LP", 144, "bfloat16"), ("KI", 2048, "bfloat16"), ("DG", 2048, "float16"),
+    ("SH", 1024, "bfloat16"), ("RD", 1024, "bfloat16"), ("W8", 144, "bfloat16"), ("w8i", 144, "int32"),
+    ("MC", 192 * HOPS, "float16"), ("MP", 256 * HOPS, "float16"), ("CO", 192 * HOPS, "float16"), ("PO", 256 * HOPS, "float16"),
+    ("PI", 256, "int32"), ("SI", 256, "int32"), ("S16", 256, "float16"), ("KA", 1, "int32"), ("TA", 512, "float32"), ("TB", 512, "float32"),
+    ("ia", 128, "int32"), ("ib", 128, "int32"), ("jm", 128, "int32"), ("jb", 128, "int32"), ("J", 128, "bfloat16"), ("i2", 32, "int32"),
+    ("BM", 128, "bfloat16"), ("ONE", 256, "bfloat16"), ("F25", 128, "bfloat16"), ("Fm", 128, "bfloat16"), ("F16", 128, "bfloat16"),
+    ("CT", 256, "float16"), ("C511", 64, "float16"), ("C32k", 64, "bfloat16"), ("tg", 8, "float32"), ("te", 8, "float32"), ("tc", 8, "float32"),
+    ("LT", 16, "float16"), ("rk", 16, "float16"), ("KC", 16, "float32"), ("KTa", 256, "float16"), ("KTb", 256, "float16"), ("KD", 16, "float32"),
+    ("TH", 128, "bfloat16"), ("AC", 256, "bfloat16"), ("XK", 256, "bfloat16"), ("T1", 256, "bfloat16"), ("R2", 256, "bfloat16"),
+    ("Z", 256, "float32"), ("ZI", 256, "int32"), ("HI", 256, "int32"), ("H16", 256, "uint16"), ("HK", 256, "float32"), ("PR", 256, "float16"),
+    ("hp", 16, "float16"), ("hit", 64, "bfloat16"), ("hk", 64, "float16"), ("b16", 64, "float16"), ("eq", 128, "bfloat16"),
+    ("old", 256, "bfloat16"), ("n1", 256, "bfloat16"), ("nv", 256, "bfloat16"), ("tP", 256, "float16"), ("jk", 16, "float32"), ("fb", 16, "float32"),
+    ("Pf", 256, "float32"), ("Pv", 256, "float32"), ("yb", 256, "float32"), ("yo", 256, "float32"), ("yl", 256, "float32"),
+    ("y1", 16, "float32"), ("sp", 32, "float16"), ("so", 512, "float32"),
 ):
-    _sb(_n, _w, _d)
-PS = ("E0", "E1", "Q0", "Q1", "SK", "CC", "RG", "OB")
+    SCRATCH[_n] = ("sbuf", [128, _w], _d)
+PS = ("E0", "E1", "Q0", "Q1", "ZB", "CB", "RG", "DB")
 for _n in PS:
     SCRATCH[_n] = ("psum", [128, 512], "float32")
 
-SEMAPHORES = (["qv", "qs", "qp", "qg", "snd", "lx", "la", "lr", "lk", "lz", "lpy", "lps", "oy", "oz"]
+SEMAPHORES = (["qv", "qs", "qp", "qg", "snd", "lx", "la", "lr", "lk", "lz", "lp", "oy", "oz"]
               + ["mc%d" % t for t in range(1, HOPS)] + ["mp%d" % t for t in range(1, HOPS)] + ["ar%d" % d for d in (1, 2, 3)])
 
 
@@ -70,13 +66,16 @@ def rank_program(g, core, T, topo):
     log = {}
     sent = [0]
 
-    def view(name, a=0, b=None, st=1):
+    def view(name, a=0, b=None, st=1, parts=128):
         if name in PART:
             name, o, w = PART[name]
             a, b = o + a, o + (w if b is None else b)
         b = SCRATCH[name][1][1] if b is None else b
-        ap = T[name][:, a:b] if st == 1 else T[name][:, a:b:st]
+        ap = T[name][0:parts, a:b] if st == 1 else T[name][0:parts, a:b:st]
         return (ap, name, a, b)
+
+    def col(name):
+        return view(name, 0, 1)
 
     def need(q, ev):
         if seen[q].get(ev[0], 0) < ev[1]:
@@ -90,7 +89,7 @@ def rank_program(g, core, T, topo):
                 ps = nm in PS
                 for (q2, a2, b2, w2), ev in log.get(nm, {}).items():
                     hitx = a < b2 and a2 < b
-                    dep = (hitx and w2 and not (wr and ps)) or (q2 != q and ((hitx and (wr or w2)) or ps))
+                    dep = (hitx and w2 and not (wr and ps and q == "p")) or (q2 != q and ((hitx and (wr or w2)) or ps))
                     if dep and todo.get(ev[0], 0) < ev[1]:
                         todo[ev[0]] = ev[1]
         for k in sorted(todo):
@@ -118,13 +117,13 @@ def rank_program(g, core, T, topo):
         emit("v", lambda: g.vector.tensor_tensor(o[0], win[0].indirect(off[0]), b[0], op), [o], [win, off, b])
 
     def ts(o, a, s1, op0, s2=None, op1=None):
-        col = isinstance(s1, tuple)
-        sc = s1[0] if col else s1
+        cs = [s for s in (s1, s2) if isinstance(s, tuple)]
+        x1, x2 = (s[0] if isinstance(s, tuple) else s for s in (s1, s2))
         if op1 is None:
-            f = lambda: g.vector.tensor_scalar(o[0], a[0], sc, None, op0)
+            f = lambda: g.vector.tensor_scalar(o[0], a[0], x1, None, op0)
         else:
-            f = lambda: g.vector.tensor_scalar(o[0], a[0], sc, s2, op0, op1)
-        emit("v", f, [o], [a] + ([s1] if col else []))
+            f = lambda: g.vector.tensor_scalar(o[0], a[0], x1, x2, op0, op1)
+        emit("v", f, [o], [a] + cs)
 
     def cp(o, a):
         emit("v", lambda: g.vector.tensor_copy(o[0], a[0]), [o], [a])
@@ -135,110 +134,43 @@ def rank_program(g, core, T, topo):
     def scat(win, off, a):
         emit("v", lambda: g.vector.tensor_copy(win[0].indirect(off[0]), a[0]), [win], [off, a])
 
+    def turn32(o, a):
+        emit("v", lambda: g.vector.transpose(o[0], a[0]), [o], [a])
+
     def ms(o, c):
         emit("v", lambda: g.vector.memset(o[0], c), [o], [])
 
-    def act(o, a, f=F_.Copy, scale=1.0):
-        if isinstance(scale, tuple):
-            emit("s", lambda: g.scalar.activation(o[0], a[0], f, scale=scale[0]), [o], [a, scale])
+    def act(o, a, f=F_.Copy, scale=1.0, bias=0.0, acc=None):
+        cs = [s for s in (scale, bias) if isinstance(s, tuple)]
+        sc, bi = (s[0] if isinstance(s, tuple) else s for s in (scale, bias))
+        if acc is None:
+            emit("s", lambda: g.scalar.activation(o[0], a[0], f, bias=bi, scale=sc), [o], [a] + cs)
         else:
-            emit("s", lambda: g.scalar.activation(o[0], a[0], f, scale=scale), [o], [a])
+            emit("s", lambda: g.scalar.activation(o[0], a[0], f, bias=bi, scale=sc, accum_out=acc[0]), [o, acc], [a] + cs)
 
     def acti(o, win, off):
         emit("s", lambda: g.scalar.activation(o[0], win[0].indirect(off[0]), F_.Copy), [o], [win, off])
 
-    def mm(o, l, r, start, stop):
+    def mm(o, l, r, start=False, stop=False):
         emit("p", lambda: g.tensor.matmul(o[0], l[0], r[0], start, stop), [o], [l, r])
 
-    def iota(nm, pat, base, cm):
-        o = view(nm)
+    def spread(bank, a, l, r, start=False, stop=False, blocks=4):
+        for k in range(blocks):
+            mm(view(bank, a + 64 * k, a + 64 * k + 64), view(l), r, start and k == 0, stop and k == blocks - 1)
+
+    def iota(o, pat, base, cm):
         emit("g", lambda: g.iota(o[0], pat, base, cm), [o], [])
 
-    def load(q, o, src, sem, total=16):
+    def load(q, o, src, sem):
         order(q, [o], [])
         Q[q].dma_start(o[0], src).then_inc(T.sem[sem], 16)
-        note("dma", [o], [], (sem, total))
+        note("dma", [o], [], (sem, 16))
 
     def send(dst, o, a, sem):
         order("g", [], [a])
         rid, pid = topo.addr(dst, core)
         g.remote_dma(o[0], a[0], T.sem[sem], T.sem.snd, pid, rid, topo.mask(core, dst))
         sent[0] += len(topo.engines(core, dst))
-
-    load("y", view("SI"), T.s0[:], "lz")
-    load("s", view("KA"), T.kap[:], "lk")
-    for k in range(16):
-        q, sem = (("y", "lpy"), ("s", "lps"))[k % 2]
-        load(q, view("PI", 16 * k, 16 * k + 16), T.pn[k::16, :], sem, 128)
-    load("y", view("AR", 0, 256), T.a0[:], "la")
-    load("s", view("AR", 256, 512), T.r0[:], "lr")
-    load("y", view("X", 0, 2048), T.x[:], "lx")
-
-    iota("ia", [[-1, 128]], 0, 1)
-    iota("ib", [[-16, 8], [0, 16]], 0, 1)
-    iota("ip", [[0, 16]], 0, 1)
-    iota("inn", [[1, 16]], 0, 0)
-    iota("il", [[1, 16]], 0, 16)
-    iota("irv", [[-16, 16]], 240, 0)
-    iota("idl", [[1, 8]], 1, 0)
-    iota("DUM", [[2, 16]], 2048, 0)
-    ts(view("Ib"), view("ia"), 0, A_.is_equal)
-    ts(view("If"), view("ia"), 0, A_.is_equal)
-    ts(view("bmi"), view("ib"), 4, A_.arith_shift_right)
-    ts(view("CI"), view("ip"), 15, A_.bitwise_and)
-    ts(view("li"), view("il"), 255, A_.bitwise_and)
-    ts(view("BM"), view("bmi"), 0, A_.is_equal)
-    ts(view("BMf"), view("bmi"), 0, A_.is_equal)
-    tt(view("SEL"), view("CI"), view("inn"), A_.is_equal)
-    cp(view("REP"), view("CI"))
-    cp(view("RK"), view("inn"))
-    ts(view("RVK"), view("inn"), -1, A_.mult, 15, A_.add)
-    ts(view("LT"), view("li"), 128, A_.add)
-    ms(view("ONE"), 1.0)
-    ms(view("F25"), 0.25)
-    ts(view("I32"), view("If"), 32.0, A_.mult)
-    ts(view("I16"), view("If"), 16.0, A_.mult)
-    ts(view("I1184"), view("If"), 1184.0, A_.mult)
-    for nm, c in (("NI", -1.0), ("N128", -128.0), ("I4k", 4096.0), ("N4k", -4096.0), ("NB", -262144.0), ("N2k", -2048.0), ("I64k", 65536.0)):
-        act(view(nm), view("Ib"), scale=c)
-    for k in range(16):
-        act(view("KI", 128 * k, 128 * k + 128), view("Ib"), scale=7.5 - k)
-    cp(view("kf"), view("KA"))
-    ts(view("rk"), view("SEL"), view("kf"), A_.mult)
-    mm(view("Q1", 0, 16), view("BMf"), view("rk"), True, True)
-    cp(view("KC"), view("Q1", 0, 16))
-    cpi(view("KTa"), view("KC"), view("RK"))
-    cpi(view("KTb"), view("KC"), view("RVK"))
-    ms(view("F376"), 376.0)
-    ms(view("Fm256"), -256.0)
-    ms(view("TH"), 67.0 * 512)
-    ms(view("LE"), 0.0)
-    ts(view("B8"), view("BM", 0, 128, 16), -65536.0, A_.mult)
-    for i in range(16):
-        cp(view("LE", 128 * i + i, 128 * i + 128, 16), view("B8"))
-    ms(view("Z0"), 0.0)
-    ms(view("Fm"), -1.0 / 4096)
-    ms(view("F16"), 16.0)
-    tt(view("ge"), view("CI", 0, 8), view("idl"), A_.is_ge)
-    ts(view("pb"), view("idl"), -1, A_.mult, 16, A_.add)
-    tt(view("rvi"), view("irv"), view("CI"), A_.add)
-    tt(view("pa"), view("ge"), view("idl"), A_.mult)
-    ts(view("ge"), view("ge"), -1, A_.mult, 1, A_.add)
-    cp(view("RVP"), view("rvi"))
-    tt(view("pa"), view("CI", 0, 8), view("pa"), A_.subtract)
-    tt(view("pb"), view("pb"), view("ge"), A_.mult)
-    tt(view("KD"), view("KTa", 0, 256, 16), view("KTb", 0, 256, 16), A_.subtract)
-    cp(view("PRE"), view("pa"))
-    tt(view("pb"), view("CI", 0, 8), view("pb"), A_.add)
-    for k in range(16):
-        ts(view("DG", 128 * k, 128 * k + 128), view("I16"), view("KD", k, k + 1), A_.mult)
-    cp(view("PRL"), view("pb"))
-    cp(view("MC", 0, 16), view("SI"))
-    ts(view("MC", 16, 32), view("inn"), 0, A_.mult, 1, A_.add)
-    ts(view("MC", 32, 48), view("inn"), 0, A_.mult, -7.5, A_.add)
-    cp(view("MP", 0, 256), view("PI"))
-    for d in (1, 2, 3):
-        send(T.cores[(rank + d) % n], view("AR", 512 * d, 512 * d + 512), view("AR", 0, 512), "ar%d" % d)
 
     outs = {}
 
@@ -247,228 +179,396 @@ def rank_program(g, core, T, topo):
         Q[q].dma_start(out, a[0]).then_inc(T.sem[sem], 16)
         outs[sem] = outs.get(sem, 0) + 16
 
-    def finish_names(U):
-        acti(view("Pv"), view("Pf"), view("RVP"))
-        mm(view("SK", 0, 256), view("F16"), view("ONE", 0, 256), True, False)
-        for k in range(16):
-            mm(view("SK", 16 * k, 16 * k + 16), view("N2k"), U, False, k == 15)
-        ts(view("y1"), U, -8.0, A_.mult, 8.0, A_.add)
-        cp(view("so"), view("hs"))
-        tt(view("po"), view("pq"), view("y1"), A_.add)
-        tt(view("yb"), view("Pf"), view("SK", 0, 256), A_.subtract)
-        tt(view("SK", 0, 256), view("Pv"), view("SK", 0, 256), A_.min)
-        tt(view("yo"), view("SK", 0, 256), view("yb"), A_.max)
-        for k in range(16):
-            store(("y", "s")[k % 2], T.yn[k::16, :], view("yo", 16 * k, 16 * k + 16), ("oy", "oz")[k % 2])
-        store("y", T.ys[:], view("so"), "oy")
-        store("s", T.yp[:], view("po"), "oz")
+    def mat(name, k):
+        return view(name, 128 * k, 128 * k + 128)
 
-    for t in range(HOPS):
-        last = t == HOPS - 1
-        s_, U, pc = (view("MC", 48 * t + 16 * x, 48 * t + 16 * x + 16) for x in range(3))
-        P = view("MP", 256 * t, 256 * t + 256)
+    def state(buf, t):
+        return [view(buf, 192 * t + 64 * x, 192 * t + 64 * x + 64) for x in range(3)]
+
+    def first16(v):
+        return view(v[1], v[2], v[2] + 16)
+
+    SITES = view("X", 0, 2048)
+
+    load("y", view("PI"), T.pn[:], "lp")
+    load("s", view("SI", parts=8), T.s0[:], "lz")
+    load("s", view("KA"), T.kap[:], "lk")
+    load("y", view("X", 0, 2048), T.x[:], "lx")
+    load("s", view("AR", 0, 256), T.a0[:], "la")
+    load("s", view("AR", 256, 512), T.r0[:], "lr")
+
+    iota(view("ip"), [[0, 16]], 0, 1)
+    iota(view("i2"), [[1, 16], [0, 2]], 0, 0)
+    iota(view("inn"), [[1, 16]], 0, 0)
+    iota(view("ia"), [[1, 128]], 0, -1)
+    iota(view("w8i", parts=8), [[1, 144]], -15, -16)
+    iota(view("ib"), [[-16, 8], [0, 16]], 0, 1)
+    iota(view("idl", 0, 8), [[1, 8]], 1, 0)
+    ms(view("ONE"), 1.0)
+    ms(view("F25"), 0.25)
+    ts(view("q15"), view("ip"), 15, A_.bitwise_and)
+    ts(view("q31i"), view("ip"), 31, A_.bitwise_and)
+    ms(view("LE"), 0.0)
+    ms(view("LP"), 0.0)
+    cp(col("p16"), col("q15"))
+    cp(col("q31"), col("q31i"))
+    ms(view("CT", 0, 240), 1537.0)
+    ms(view("CT", 240, 256), 1505.0)
+    ts(view("DUP1"), view("i2"), 16, A_.mult, col("p16"), A_.add)
+    ts(col("c3"), col("p16"), 31, A_.mult, col("q31"), A_.add)
+    ts(view("Ib"), view("ia"), 0, A_.is_equal)
+    cp(view("RK"), view("inn"))
+    ts(view("UN1"), view("inn"), col("c3"), A_.add)
+    cpi(view("TA"), view("PI"), view("DUP1"))
+    for nm in EYES:
+        act(view(nm), view("Ib"), scale=EYES[nm])
+    cp(col("kf"), view("KA"))
+    cp(view("S16", parts=8), view("SI", parts=8))
+    turn32(view("TB"), view("TA"))
+    ts(view("W8", parts=8), view("w8i", parts=8), 0, A_.is_equal)
+    ts(view("jb"), view("ib"), -16, A_.bitwise_and)
+    ts(view("rk"), view("inn"), col("p16"), A_.is_equal, col("kf"), A_.mult)
+    cpi(view("MP", 0, 256), view("TB"), view("UN1"))
+    for i in range(16):
+        mm(view("E0", 0, 16), view("W8", 15 - i, 143 - i, parts=8), view("S16", i, 256, 16, parts=8), i == 0, i == 15)
+    ts(view("BM"), view("jb"), 0, A_.is_equal)
+    ts(view("LT"), view("inn"), 16, A_.mult, col("p16"), A_.add)
+    s0_, U0, p0 = state("MC", 0)
+    for k in range(4):
+        cp(view("MC", 16 * k, 16 * k + 16), view("E0", 0, 16))
+    mm(view("Q1", 0, 16), view("BM"), view("rk"), True, True)
+    ms(U0, 1.0)
+    ms(p0, -7.5)
+    ts(view("LT"), view("LT"), 128, A_.add)
+    cp(view("KC"), view("Q1", 0, 16))
+    ts(view("LE", 15, 143, 16), view("BM", 0, 128, 16), -BIG, A_.mult)
+    ts(view("LP", 15, 143, 16), view("BM", 0, 128, 16), BIG, A_.mult)
+    cpi(view("KTa"), view("KC"), view("RK"))
+    for k in range(16):
+        act(mat("KI", k), view("Ib"), scale=7.5 - k)
+    ms(view("TH"), 67.0)
+    ms(view("C32k"), 32768.0)
+    ms(view("C511"), 511.0)
+
+    def late_constants():
+        ts(view("jm"), view("ia"), 15, A_.bitwise_and)
+        ts(view("tg"), view("idl", 0, 8), col("p16"), A_.is_gt)
+        ts(view("te"), view("idl", 0, 8), -1, A_.mult, 16, A_.add)
+        tt(view("J"), view("jm"), view("jb"), A_.add)
+        cp(view("REP"), view("q15"))
+        tt(view("tc"), view("tg"), view("te"), A_.mult)
+        ts(col("dum"), col("p16"), 2048, A_.add)
+        ms(view("Fm"), -1.0 / 4096)
+        for d in range(1, 9):
+            ts(mat("SH", d - 1), view("J"), d, A_.is_equal)
+        for d in range(1, 9):
+            ts(mat("RD", d - 1), view("J"), view("tc", d - 1, d), A_.is_equal, 4096, A_.mult)
+
+    def key_constants():
+        steps = [lambda: ts(view("RVK"), view("inn"), -1, A_.mult, 15, A_.add),
+                 lambda: cpi(view("KTb"), view("KC"), view("RVK")),
+                 lambda: tt(view("KD"), view("KTa", 0, 256, 16), view("KTb", 0, 256, 16), A_.subtract)]
+        for k in range(16):
+            steps.append(lambda k=k: ts(mat("DG", k), view("I16"), view("KD", k, k + 1), A_.mult))
+        return steps
+
+    def end_constants():
+        return [lambda: ts(col("p256"), col("p16"), 16, A_.mult),
+                lambda: ts(view("UN2"), view("inn"), 32, A_.mult, col("q31"), A_.add),
+                lambda: ts(view("RVP"), view("RVK"), 16, A_.mult, col("p16"), A_.add),
+                lambda: ts(view("DUP2"), view("i2"), col("p256"), A_.add),
+                lambda: ms(view("F16"), 16.0)]
+
+    def arrive(t):
+        s_, U, pc = state("MC", t)
         if t:
             ne = len(topo.engines(prv, core))
-            note("rem", [view("MC", 48 * t, 48 * t + 48)], [], ("mc%d" % t, ne))
-            note("rem", [P], [], ("mp%d" % t, ne))
+            note("rem", [view("MC", 192 * t, 192 * t + 192)], [], ("mc%d" % t, ne))
+            note("rem", [view("MP", 256 * t, 256 * t + 256)], [], ("mp%d" % t, ne))
         d = t % n
         if 1 <= t <= 3:
             note("rem", [view("AR", 512 * d, 512 * d + 512)], [], ("ar%d" % d, len(topo.engines(T.cores[(rank - d) % n], core))))
-        mm(view("OB", 256, 512), view("F25"), view("ONE", 0, 256), True, False)
+        mm(view("ZB", 0, 256), view("F25"), view("ONE"), True)
+        mm(view("ZB", 256, 512), view("I16"), view("KTa"))
+        mm(view("ZB", 256, 512), view("I16"), view("KTb" if t else "KTa"))
+        mm(view("E1", 128, 144), view("Ib"), view("LT"), True)
+        mm(view("E1", 128, 144), view("N128"), first16(U), False, True)
+        spread("ZB", 0, "Ib", s_)
         if t:
-            mm(view("SK", 256, 512), view("I16"), view("KTa"), True, False)
-            mm(view("SK", 256, 512), view("I16"), view("KTb"), False, False)
-        else:
-            mm(view("SK", 256, 512), view("I32"), view("KTa"), True, False)
-        mm(view("Q0", 0, 16), view("N128"), U, True, False)
-        mm(view("Q0", 0, 16), view("If"), view("LT"), False, True)
-        cp(view("AO"), view("Q0", 0, 16))
-        acti(view("AC"), view("AR", 512 * d, 512 * d + 512), view("AO"))
-        for k in range(16):
-            mm(view("OB", 256 + 16 * k, 272 + 16 * k), view("If"), s_, False, k == 15)
-        for k in range(16):
-            o = view("SK", 256 + 16 * k, 272 + 16 * k)
-            if t:
-                mm(o, view("DG", 128 * k, 128 * k + 128), U, False, False)
-            mm(o, view("I1184"), s_, False, k == 15)
-        for k in range(16):
-            mm(view("RG", 256 + 16 * k, 272 + 16 * k), view("KI", 128 * k, 128 * k + 128), U, True, True)
-        act(view("KU"), view("RG", 256, 512))
-        ts(view("sC"), s_, 32.0, A_.mult, 25952.0 * t, A_.add)
-        ts(view("U2"), U, 2.0, A_.mult)
-        for a in (0, 128):
-            b = a + 128
-            tt(view("Z", a, b), view("MP", 256 * t + a, 256 * t + b), view("OB", 256 + a, 256 + b), A_.mult)
-            tt(view("ZI", a, b), view("Z", a, b), view("SK", 256 + a, 256 + b), A_.add)
-            ts(view("HI", a, b), view("ZI", a, b), 5, A_.arith_shift_right, 2047, A_.bitwise_and)
-            cp(view("H16", a, b), view("HI", a, b))
-        mm(view("RG", 0, 256), view("Ib"), view("KU"), True, False)
-        for k in range(16):
-            mm(view("RG", 16 * k, 16 * k + 16), view("If"), pc, False, k == 15)
-
-        def bounds():
-            act(view("T1"), view("RG", 0, 256), F_.Relu)
-            mm(view("CC", 0, 256), view("F376"), view("ONE", 0, 256), True, False)
-            mm(view("CC", 0, 256), view("N2k"), view("KU"), False, False)
-            mm(view("CC", 0, 256), view("NB"), view("T1"), False, True)
-            mm(view("CC", 256, 512), view("Fm256"), view("ONE", 0, 256), True, False)
-            mm(view("CC", 256, 512), view("I64k"), view("KU"), False, False)
             for k in range(16):
-                mm(view("CC", 256 + 16 * k, 272 + 16 * k), view("I64k"), pc, False, k == 15)
+                mm(view("ZB", 256 + 16 * k, 272 + 16 * k), mat("DG", k), first16(U))
+        spread("ZB", 256, "I1184", s_, stop=True)
+        for k in range(16):
+            mm(view("RG", 16 * k, 16 * k + 16), mat("KI", k), first16(U), k == 0)
+        spread("RG", 0, "Ib", pc, stop=True)
 
-        W_ = view("X", 0, 2048)
+    def records(t):
+        d = t % n
+        cp(view("AO"), view("E1", 128, 144))
+        acti(view("AC"), view("AR", 512 * d, 512 * d + 512), view("AO"))
 
-        def grow(k):
-            acti(view("DR", 256 * k, 256 * k + 256), W_, view("H16", 16 * k, 16 * k + 16))
+    def rows_against_p(t):
+        s_, U, pc = state("MC", t)
+        act(view("XK"), view("RG", 0, 256))
+        act(view("T1"), view("RG", 0, 256), F_.Relu)
+        mm(view("RG", 256, 512), view("Ib"), view("XK"), True)
+        mm(view("RG", 256, 512), view("N2"), view("T1"), False, True)
+        act(view("RG", 256, 512), view("RG", 256, 512), F_.Relu, bias=1.0)
+        mm(view("CB", 0, 256), view("I2k"), view("CT"), True)
+        mm(view("CB", 0, 256), view("F25"), view("ONE"))
+        spread("CB", 0, "Ikp", pc)
+        spread("CB", 0, "I32k", U)
+        mm(view("CB", 240, 256), view("N64k"), first16(U))
+        mm(view("CB", 0, 256), view("Nkp"), view("XK"))
+        mm(view("CB", 0, 256), view("NB"), view("T1"), False, True)
 
-        def psub(c):
-            q = "Q%d" % (c % 2)
-            mm(view(q, 0, 512), view("Ib"), view("DR", 1024 * c, 1024 * c + 512), True, False)
-            mm(view(q, 0, 256), view("NI"), view("AC"), False, False)
-            mm(view(q, 256, 512), view("NI"), view("AC"), False, True)
+    def site_steps(t, a, b):
+        return [lambda: tt(view("Z", a, b), view("MP", 256 * t + a, 256 * t + b), view("ZB", a, b), A_.mult),
+                lambda: tt(view("ZI", a, b), view("Z", a, b), view("ZB", 256 + a, 256 + b), A_.add),
+                lambda: ts(view("HI", a, b), view("ZI", a, b), 5, A_.arith_shift_right, 2047, A_.bitwise_and),
+                lambda: cp(view("H16", a, b), view("HI", a, b))]
 
-        def vrows(*ks):
-            for k in ks:
-                tti(view("DR", 256 * k, 256 * k + 256), W_, view("H16", 16 * k, 16 * k + 16), view("AC"), A_.subtract)
+    def weave(*lists):
+        return [l[k] for k in range(max(len(l) for l in lists)) for l in lists if k < len(l)]
 
-        def absps(c):
-            act(view("DA", 1024 * c, 1024 * c + 512), view("Q%d" % (c % 2), 0, 512), F_.Abs)
+    def grow(k):
+        acti(view("DR", 256 * k, 256 * k + 256), SITES, view("H16", 16 * k, 16 * k + 16))
 
-        def absrows(k, k2):
-            act(view("DA", 256 * k, 256 * k2), view("DR", 256 * k, 256 * k2), F_.Abs)
+    def psub(k, q):
+        mm(view(q, 0, 512), view("Ib"), view("DR", 256 * k, 256 * k + 512), True)
+        mm(view(q, 0, 256), view("NI"), view("AC"))
+        mm(view(q, 256, 512), view("NI"), view("AC"), False, True)
 
-        def dsum(c):
-            o = view("E%d" % (c % 2), 0, 64)
-            mm(o, view("TH"), view("ONE", 0, 64), True, False)
-            for nm, src in ((("LP", "DR"), ("L2", "DA")) if c == RELU else (("LE", "DA"),)):
-                for i in range(16):
-                    mm(o, view(nm, 128 * i, 128 * i + 128), view(src, 1024 * c + i, 1024 * c + 1024, 16), False, i == 15 and nm != "LP")
+    def absps(k, q):
+        act(view("DA", 256 * k, 256 * k + 512), view(q), F_.Abs)
 
-        def decide(c):
-            e = view("E%d" % (c % 2), 0, 64)
-            tt(e, e, view("FL", 64 * c, 64 * c + 64), A_.max)
-            if c == 0:
-                tt(view("M"), e, view("HK", 0, 64), A_.min)
-            else:
-                tt(e, e, view("HK", 64 * c, 64 * c + 64), A_.min)
-                tt(view("M"), e, view("M"), A_.max)
+    def vrows(*ks):
+        for k in ks:
+            tti(view("DR", 256 * k, 256 * k + 256), SITES, view("H16", 16 * k, 16 * k + 16), view("AC"), A_.subtract)
 
-        if t == 0:
-            ts(view("LP"), view("LE"), -1.0, A_.mult)
-            ts(view("L2"), view("LE"), 2.0, A_.mult)
+    def absrows(k, k2):
+        act(view("DA", 256 * k, 256 * k2), view("DR", 256 * k, 256 * k2), F_.Abs)
+
+    def relurows(k, k2):
+        ts(view("DA", 256 * k, 256 * k2), view("DR", 256 * k, 256 * k2), 0.0, A_.max, 2.0, A_.mult)
+
+    def dopen(c, k=0, k2=0):
+        e = "E%d" % (c % 2)
+        mm(view(e, 0, 64), view("TH"), view("C32k"), True)
+        if k2 > k:
+            for i in range(16):
+                mm(view(e, 16 * (k % 4), 16 * (k % 4 + k2 - k)), view("LP", 15 - i, 143 - i), view("DR", 256 * k + i, 256 * k2, 16))
+
+    def dsum(c):
+        for i in range(16):
+            mm(view("E%d" % (c % 2), 0, 64), view("LE", 15 - i, 143 - i), view("DA", 1024 * c + i, 1024 * c + 1024, 16), False, i == 15)
+
+    def dmin(c, first=False):
+        e = view("E%d" % (c % 2), 0, 64)
+        tt(view("M") if first else e, e, view("HK", 64 * c, 64 * c + 64), A_.min)
+
+    def dmax(c, first=False):
+        tt(view("M"), view("CB", 256, 320) if first else view("E%d" % (c % 2), 0, 64), view("M"), A_.max)
+
+    def fold(nm):
+        tt(view("fa", 0, 32), view(nm, 0, 32), view(nm, 32, 64), A_.max)
+        tt(view("fb"), view("fa", 0, 16), view("fa", 16, 32), A_.max)
+
+    def row_p(t):
+        s_, U, pc = state("MC", t)
+        for k in range(16):
+            mm(view("CB", 320, 336), view("Ib"), view("PR", 16 * k, 16 * k + 16), k == 0)
+        o = view("CB", 256, 320)
+        mm(o, view("I2k"), view("C511"))
+        mm(o, view("F25"), view("ONE", 0, 64))
+        mm(o, view("Ikm"), pc)
+        mm(o, view("N32k"), U)
+        for k in range(4):
+            mm(o, view("Ib"), view("PR", 64 * k, 64 * k + 64), False, k == 3)
+
+    def open_groups(t):
+        s_, U, pc = state("MC", t)
+        for d in range(8):
+            o = view("DB", 16 * d, 16 * d + 16)
+            mm(o, mat("SH", d), view("hp"), d == 0)
+            mm(o, view("NI"), view("hp"))
+        mm(view("RG", 0, 256), view("NI"), view("XK"), True)
+        mm(view("RG", 0, 256), view("I32"), view("T1"))
+        spread("RG", 0, "Ib", pc)
+
+    def finish_steps(t):
+        sn, Un, pn_ = state("CO", t)
+
+        def backwards():
+            acti(view("Pv"), view("Pf"), view("RVP"))
+            mm(view("ZB", 256, 512), view("F16"), view("ONE"), True)
+            spread("ZB", 256, "N2k", Un, stop=True)
+            tt(view("yb"), view("Pf"), view("ZB", 256, 512), A_.subtract)
+
+        def pick():
+            tt(view("yo"), view("ZB", 256, 512), view("yb"), A_.max)
+            acti(view("TA"), view("yo"), view("DUP2"))
+
+        def small():
+            tt(view("sp", 16, 32), first16(pn_), view("y1"), A_.add)
+            for i in range(16):
+                mm(view("CB", i, 512, 16, parts=8), view("Ib", i, 128, 16), view("sp"), i == 0, i == 15)
+            act(view("so", parts=8), view("CB", parts=8))
+            store("y", T.ys[:], view("so", 0, 256, parts=8), "oy")
+            store("y", T.yp[:], view("so", 256, 512, parts=8), "oy")
+
+        def names():
+            turn32(view("TB"), view("TA"))
+            acti(view("yl"), view("TB"), view("UN2"))
+            store("s", T.yn[:], view("yl"), "oz")
+
+        return [backwards, lambda: ts(view("y1"), first16(Un), -8.0, A_.mult, 15.5, A_.add),
+                lambda: tt(view("ZB", 256, 512), view("Pv"), view("ZB", 256, 512), A_.min),
+                lambda: cp(view("sp", 0, 16), first16(sn)), pick, small, None, None, None, names]
+
+    arrive(0)
+    records(0)
+    rows_against_p(0)
+    for f in weave(site_steps(0, 0, 128), site_steps(0, 128, 256)):
+        f()
+
+    for t in range(HOPS):
+        last = t == HOPS - 1
+        s_, U, pc = state("MC", t)
+        sn, Un, pn_ = state("CO", t)
+        P = view("MP", 256 * t, 256 * t + 256)
         grow(0)
         grow(1)
-        psub(0)
         vrows(2, 3)
+        if t < n - 1:
+            d = t + 1
+            order("g", [], [view("DR", 512, 768)])
+            send(T.cores[(rank + d) % n], view("AR", 512 * d, 512 * d + 512), view("AR", 0, 512), "ar%d" % d)
+        psub(0, "Q0")
+        tt(view("PR"), view("HI"), view("RG", 256, 512), A_.mult)
+        tt(view("HK"), view("HI"), view("CB", 0, 256), A_.add)
         grow(8)
-        bounds()
-        absps(0)
-        absrows(2, 4)
-        dsum(0)
-        vrows(4, 5, 6, 7)
-        ts(view("DA", 1024, 2048), view("DR", 1024, 2048), 0.0, A_.max)
         grow(9)
-        psub(2)
+        row_p(t)
+        vrows(4, 5)
+        absps(0, "Q0")
+        psub(8, "Q1")
+        absrows(2, 4)
+        cp(view("hp"), view("CB", 320, 336))
+        cp(view("hu"), view("CB", 320, 336))
+        vrows(6, 7)
+        dopen(0)
+        dsum(0)
+        dopen(1, 4, 8)
+        relurows(4, 8)
+        if t == 0:
+            late_constants()
+        grow(10)
+        grow(11)
+        vrows(12)
+        dmin(0, True)
         dsum(1)
-        tt(view("HK"), view("HI"), view("CC", 0, 256), A_.add)
-        tt(view("FL"), view("HK"), view("CC", 256, 512), A_.add)
-        vrows(10, 11)
-        grow(12)
-        absps(2)
-        decide(0)
-        decide(1)
+        absps(8, "Q1")
+        psub(10, "Q0")
+        vrows(13)
+        dmax(0, True)
+        open_groups(t)
         vrows(14)
-        grow(13)
-        psub(3)
-        absrows(10, 12)
-        dsum(2)
+        dmin(1)
+        absps(10, "Q0")
+        dopen(2)
+        relurows(12, 14)
+        dmax(1)
         vrows(15)
-        absps(3)
+        dsum(2)
+        dopen(3, 12, 14)
         absrows(14, 15)
         absrows(15, 16)
+        acti(view("old"), SITES, view("hu"))
         dsum(3)
-        mm(view("RG", 256, 512), view("Ib"), view("KU"), True, False)
-        mm(view("OB", 0, 256), view("I4k"), view("T1"), True, False)
-        mm(view("CC", 0, 256), view("N4k"), view("T1"), True, False)
-        decide(2)
-        decide(3)
-        tt(view("M2"), view("M", 0, 32), view("M", 32, 64), A_.max)
-        tt(view("Wv"), view("M2", 0, 16), view("M2", 16, 32), A_.max)
-        w = view("Wv")
-        sn, Un, pn_ = (view("CO", 48 * t + 16 * x, 48 * t + 16 * x + 16) for x in range(3))
-        ts(view("kl"), w, 11, A_.arith_shift_right, 15, A_.bitwise_and)
-        ts(view("hs"), w, 2047, A_.bitwise_and)
-        ts(view("hit"), w, 32768, A_.is_ge, 4096, A_.mult)
-        ts(view("kc"), view("kl"), -7.5, A_.add)
-        for k in range(16):
-            mm(view("RG", 256 + 16 * k, 272 + 16 * k), view("If"), view("kc"), False, k == 15)
-        tt(view("tt"), s_, view("hs"), A_.mult)
-        tt(view("key"), view("hs"), view("hit"), A_.add)
-        ts(view("W2"), w, 2048, A_.add)
-        acti(view("KL"), view("key"), view("PRL"))
-        tt(view("tb"), view("tt"), view("sC"), A_.add)
-        ts(view("v2"), view("W2"), 10, A_.arith_shift_right, 62, A_.bitwise_and)
+        dmin(2)
+        dmax(2)
+        mm(view("E0", 256, 512), view("Ib"), view("AC"), True)
+        mm(view("E0", 256, 512), view("Ib"), view("old"), False, True)
+        act(view("n1"), view("E0", 256, 512), F_.Identity, 0.5, 127.75)
+        fold("M")
+        cpi(view("M4"), view("fb"), view("REP", 0, 4))
+        tt(view("M2"), view("E1", 0, 64), view("HK", 192, 256), A_.min)
+        fold("M2")
+        tti(view("w"), view("fb"), view("REP", 0, 4), view("M4"), A_.max)
+        w = view("w")
+        ts(view("hit"), w, 2 ** 21, A_.is_ge, 4096, A_.mult)
+        ts(view("hs"), w, 4095, A_.bitwise_and)
+        ts(view("hk"), w, 2.0 ** -17, A_.mult, 1023.5076, A_.add)
+        for d in range(8):
+            mm(view("DB", 16 * d, 16 * d + 16), mat("SH", d), view("hit", 0, 16))
+        spread("DB", 0, "Ib", view("hit"), stop=True, blocks=2)
+        spread("RG", 0, "Ihit", view("hit"))
+        spread("RG", 0, "NI", view("hk"), stop=True)
+        mm(view("Q1", 0, 16), view("Ib"), view("hp"), True)
+        mm(view("Q1", 0, 16), view("Ib"), view("hit", 0, 16))
+        ts(view("ub"), w, 16, A_.arith_shift_right, 1, A_.bitwise_and)
+        ts(view("pi"), w, 12, A_.arith_shift_right, 15, A_.bitwise_and)
+        tt(view("tt" if t else "tb"), s_, view("hs"), A_.mult)
+        ts(sn, view("hs"), -32, A_.add)
+        ts(Un, view("ub"), 2, A_.mult, -1, A_.add)
+        act(view("R2"), view("RG", 0, 256), F_.Relu, bias=1031.5)
+        act(view("nv"), view("n1"), F_.Identity, bias=-128.0)
+        ts(view("eq"), view("DB", 0, 128), 0, A_.is_equal)
+        if t:
+            ts(view("tb"), view("tt"), 25952 * t, A_.add)
+        ts(pn_, view("pi"), -7.5, A_.add)
+        if not last:
+            send(nxt, view("MC", 192 * t + 192, 192 * t + 384), view("CO", 192 * t, 192 * t + 192), "mc%d" % (t + 1))
+        for d in range(8):
+            mm(view("Q1", 0, 16), mat("RD", d), view("eq", 16 * d, 16 * d + 16), False, d == 7)
+        mm(view("Q0", 0, 256), view("I4k"), view("R2"), True, True)
+        mm(view("ZB", 0, 256), view("N4k"), view("R2"), True)
         ts(view("bb"), view("tb"), 5, A_.arith_shift_right, 2047, A_.bitwise_and)
-        ts(view("hg"), view("v2"), 33, A_.is_gt, -0.5, A_.add)
+        ts(view("fo", 0, 32, 2), view("Q1", 0, 16), col("dum"), A_.min)
         cp(view("b16"), view("bb"))
-        tt(view("qq"), view("v2"), view("hg"), A_.mult)
-        cp(sn, view("hs"))
-        ts(view("pq"), view("qq"), 15, A_.bitwise_and)
-        tt(Un, view("U2"), view("hg"), A_.mult)
-        ts(pn_, view("pq"), -7.5, A_.add)
-        act(view("R2"), view("RG", 256, 512), F_.Relu, -1.0)
-        for k in range(16):
-            if k == 10:
-                mm(view("OB", 0, 256), view("I4k"), view("R2"), False, True)
-            mm(view("CC", 16 * k, 16 * k + 16), view("If"), view("b16"), False, False)
-        mm(view("CC", 0, 256), view("N4k"), view("R2"), False, True)
-        if not last:
-            send(nxt, view("MC", 48 * t + 48, 48 * t + 96), view("CO", 48 * t, 48 * t + 48), "mc%d" % (t + 1))
-        tti(view("eq"), view("key"), view("PRE"), view("KL"), A_.is_equal)
-        cp(view("hu"), view("hs"))
-        acti(view("old"), W_, view("hu"))
-        tt(view("tP"), P, view("OB", 0, 256), A_.min)
-        if not last:
-            tt(view("PO", 256 * t, 256 * t + 256), view("tP"), view("CC", 0, 256), A_.max)
-            send(nxt, view("MP", 256 * t + 256, 256 * t + 512), view("PO", 256 * t, 256 * t + 256), "mp%d" % (t + 1))
-        else:
-            tt(view("Pf"), view("tP"), view("CC", 0, 256), A_.max)
-        mm(view("E0", 0, 16), view("Z0"), view("ONE", 0, 16), True, False)
-        for dl in range(1, 9):
-            a = 16 * (dl - 1)
-            mm(view("E0", dl, 16), view("I4k"), view("eq", a + dl, a + 16), False, dl == 8)
-            if dl < 8:
-                mm(view("E0", 16 - dl, 16), view("I4k"), view("eq", a, a + dl), False, False)
-        mm(view("Q1", 0, 256), view("Ib"), view("old"), True, False)
-        mm(view("Q1", 0, 256), view("Ib"), view("AC"), False, True)
-        tt(view("G"), view("key"), view("E0", 0, 16), A_.max)
-        tt(view("Fv"), view("G"), view("DUM"), A_.min)
-        tti(view("FT"), view("Fv"), view("REP", 0, 8), view("BM"), A_.mult)
-        mm(view("Q0", 0, 16), view("FT"), view("SEL"), True, True)
-        ts(view("nv"), view("Q1", 0, 256), 0.5, A_.mult, -0.25, A_.add)
-        if last:
-            finish_names(Un)
-        cp(view("fo", 0, 32, 2), view("Q0", 0, 16))
-        if not last:
-            mm(view("E1", 0, 16), view("Fm"), view("hit"), True, True)
-            o, i_, m_ = view("jk"), view("E1", 0, 16), view("mc")
-            emit("s", lambda: g.scalar.activation(o[0], i_[0], F_.Copy, accum_out=m_[0]), [o, m_], [i_])
-        for i in range(15, -1, -1):
-            scat(view("X", 0, NX), view("fo", 2 * i, 2 * i + 1), view("nv", i, 256, 16))
-            if not last:
-                if i == 11:
-                    ts(view("mi"), view("mc"), 2048, A_.add)
-                if i == 7:
-                    ts(view("mj"), view("mi"), 15, A_.bitwise_and)
-                if i == 3:
-                    ts(view("mt"), view("mj"), 67, A_.add, 512, A_.mult)
-        if not last:
-            act(view("TH"), view("ONE", 0, 128), F_.Copy, view("mt"))
+        spread("ZB", 0, "Ib", view("b16"), stop=True)
+        tt(view("tP"), P, view("Q0", 0, 256), A_.min)
 
-    store("y", T.yx[:], view("X", 0, 2048), "oy")
+        def names():
+            if last:
+                tt(view("Pf"), view("tP"), view("ZB", 0, 256), A_.max)
+            else:
+                tt(view("PO", 256 * t, 256 * t + 256), view("tP"), view("ZB", 0, 256), A_.max)
+                send(nxt, view("MP", 256 * t + 256, 256 * t + 512), view("PO", 256 * t, 256 * t + 256), "mp%d" % (t + 1))
+
+        def limit():
+            mm(view("E1", 64, 80), view("Fm"), view("hit", 0, 16), True, True)
+            act(view("jk"), view("E1", 64, 80), F_.Identity, bias=2040.5 / 16, acc=col("mc"))
+            act(col("m1"), col("mc"), F_.Identity, bias=ROUND16)
+            act(col("m2"), col("m1"), F_.Identity, -1.0, ROUND16)
+            act(col("m3"), col("m2"), F_.Identity, bias=74.5)
+            act(view("TH"), view("ONE", 0, 128), F_.Identity, col("mc"), col("m3"))
+
+        fill = {0: [names]}
+        if last:
+            for k, f in enumerate(finish_steps(t)):
+                fill[k + 1] = [f] if f else []
+        else:
+            fill[0].append(limit)
+            extra = key_constants() if t == 0 else end_constants() if t == 1 else []
+            for k, f in enumerate(extra):
+                fill.setdefault(1 + k // 4, []).append(f)
+            fill.setdefault(5, []).append(lambda: arrive(t + 1))
+            fill[7] = [lambda: records(t + 1), lambda: rows_against_p(t + 1)]
+            for k, f in enumerate(weave(site_steps(t + 1, 0, 128), site_steps(t + 1, 128, 256))):
+                fill.setdefault(min(10 + k, 15), []).append(f)
+        for k in range(16):
+            j = 15 - k
+            scat(view("X"), view("fo", 2 * j, 2 * j + 1), view("nv", 16 * j, 16 * j + 16))
+            for f in fill.get(k, []):
+                f()
+
+    store("y", T.yx[:], SITES, "oy")
     for q in ("v", "s", "p", "g"):
         need("g", (QS[q], cnt[q]))
     for sem in outs:
         need("g", (sem, outs[sem]))
-    for sem, val in (("lx", 16), ("la", 16), ("lr", 16), ("lk", 16), ("lz", 16), ("lpy", 128), ("lps", 128), ("snd", sent[0])):
-        need("g", (sem, val))
+    for sem in ("lx", "la", "lr", "lk", "lz", "lp"):
+        need("g", (sem, 16))
+    need("g", ("snd", sent[0]))

@@ -3,12 +3,19 @@ from concourse.mybir import AluOpType, ActivationFunctionType
 A_ = AluOpType
 F_ = ActivationFunctionType
 HOPS = 7
-NX = 2064
+NX = 2080
 BIG = 2.0 ** 22
 ROUND16 = 1.5 * 2 ** 27
-EYES = {"NI": -1.0, "I16": 16.0, "I1184": 1184.0, "N128": -128.0, "N2": -2.0, "I2k": 2048.0, "Ikp": 135168.0, "Nkp": -135168.0,
-        "NB": -2.0 ** 23, "I32k": 32768.0, "N64k": -65536.0, "Ikm": 126976.0, "N32k": -32768.0, "I32": 32.0, "Ihit": 1.0 / 256,
+CHUNKS = ("RRRR", "SSSS", "SSAA", "RRAA")
+STEPS = "g0 g4 g1 g5 g2 g6 b0 g3 b4 g7 b2 d0 h0 ga g8 gb b6 d1 g9 gc p0 m0 ba gd x0 m1 b8 d2 ge x1 bc gf ae m2 af d3 x2 w3"
+CYCLE, GATHER, SCATTER, COLUMN, WAKE, HOPLAT, LINK, DMALAT, DMABW = 1.04e-3, 1.3e-3, 3.15e-3, 0.48e-3, 0.19, 1.2, 100e3, 2.0, 200e3
+PASSES = 4
+ORDER = []
+PIECES = ((256, 448, "ms"), (0, 128, "ma"), (128, 256, "mb"))
+EYES = {"NI": -1.0, "I16": 16.0, "I1184": 1184.0, "N128": -128.0, "I2k": 2048.0, "Ikp": 135168.0, "N1k": -1024.0,
+        "I32k": 32768.0, "N64k": -65536.0, "Ikm": 126976.0, "N32k": -32768.0, "I32": 32.0, "N32": -32.0, "I31": 31.0, "N31": -31.0, "N16": -16.0,
         "I4k": 4096.0, "N4k": -4096.0, "N2k": -2048.0}
+SIZE = {"float32": 4, "int32": 4, "bfloat16": 2, "float16": 2, "uint16": 2}
 
 SCRATCH = {}
 PART = {}
@@ -21,26 +28,29 @@ def _shared(buf, dtype, width, names):
 
 
 _shared("eyes", "bfloat16", 128, ["Ib"] + list(EYES))
-_shared("cols", "float32", 4, ("p16", "q31", "c3", "p256", "dum", "kf", "mc", "m1", "m2", "m3"))
-_shared("i64", "int32", 64, ("w", "hs", "pi", "ub", "tb", "bb"))
-_shared("f64", "float32", 64, ("M", "M2", "M4", "tt", "fa"))
+_shared("cols", "float32", 4, ("p16", "q31", "c3", "p256", "dum", "dun", "p8", "ph", "kf", "mc", "m1", "m2", "m3"))
+_shared("i64", "int32", 64, ("hs", "pi", "ub", "sh", "bq"))
+_shared("f64", "float32", 64, ("M", "M2", "M4", "fa", "sf"))
 _shared("u32", "uint16", 32, ("DUP1", "DUP2", "fo"))
-_shared("u16", "uint16", 16, ("UN1", "UN2", "RVP", "RK", "RVK", "AO", "hu", "REP"))
-_shared("i16", "int32", 16, ("inn", "ip", "q15", "q31i", "idl"))
+_shared("u16", "uint16", 16, ("UN1", "UN2", "RVP", "RK", "RVK", "AO", "hu", "REP", "EV", "OD"))
+_shared("i16", "int32", 16, ("inn", "ip", "q15", "q31i", "q7", "idl"))
 for _n, _w, _d in (
     ("X", NX, "bfloat16"), ("AR", 2048, "bfloat16"), ("DR", 4096, "bfloat16"), ("DA", 4096, "bfloat16"),
     ("LE", 144, "bfloat16"), ("LP", 144, "bfloat16"), ("KI", 2048, "bfloat16"), ("DG", 2048, "float16"),
     ("SH", 1024, "bfloat16"), ("RD", 1024, "bfloat16"), ("W8", 144, "bfloat16"), ("w8i", 144, "int32"),
-    ("MC", 192 * HOPS, "float16"), ("MP", 256 * HOPS, "float16"), ("CO", 192 * HOPS, "float16"), ("PO", 256 * HOPS, "float16"),
+    ("ST", 448 * HOPS, "float16"), ("CO", 448 * HOPS, "float16"), ("W", 64, "int32"),
     ("PI", 256, "int32"), ("SI", 256, "int32"), ("S16", 256, "float16"), ("KA", 1, "int32"), ("TA", 512, "float32"), ("TB", 512, "float32"),
     ("ia", 128, "int32"), ("ib", 128, "int32"), ("jm", 128, "int32"), ("jb", 128, "int32"), ("J", 128, "bfloat16"), ("i2", 32, "int32"),
     ("BM", 128, "bfloat16"), ("ONE", 256, "bfloat16"), ("F25", 128, "bfloat16"), ("Fm", 128, "bfloat16"), ("F16", 128, "bfloat16"),
     ("CT", 256, "float16"), ("C511", 64, "float16"), ("C32k", 64, "bfloat16"), ("tg", 8, "float32"), ("te", 8, "float32"), ("tc", 8, "float32"),
     ("LT", 16, "float16"), ("rk", 16, "float16"), ("KC", 16, "float32"), ("KTa", 256, "float16"), ("KTb", 256, "float16"), ("KD", 16, "float32"),
-    ("TH", 128, "bfloat16"), ("AC", 256, "bfloat16"), ("XK", 256, "bfloat16"), ("T1", 256, "bfloat16"), ("R2", 256, "bfloat16"),
+    ("TH", 128, "bfloat16"), ("AC", 256, "bfloat16"), ("A1", 256, "bfloat16"), ("T2", 256, "bfloat16"), ("I1057", 128, "float16"), ("R2", 256, "bfloat16"),
     ("Z", 256, "float32"), ("ZI", 256, "int32"), ("HI", 256, "int32"), ("H16", 256, "uint16"), ("HK", 256, "float32"), ("PR", 256, "float16"),
-    ("hp", 16, "float16"), ("hit", 64, "bfloat16"), ("hk", 64, "float16"), ("b16", 64, "float16"), ("eq", 128, "bfloat16"),
-    ("old", 256, "bfloat16"), ("n1", 256, "bfloat16"), ("nv", 256, "bfloat16"), ("tP", 256, "float16"), ("jk", 16, "float32"), ("fb", 16, "float32"),
+    ("hp", 16, "float16"), ("hit", 64, "bfloat16"), ("hn", 64, "bfloat16"), ("hk", 64, "float16"), ("b16", 64, "float16"), ("bw", 64, "bfloat16"),
+    ("eq", 128, "bfloat16"), ("old", 256, "bfloat16"), ("n1", 256, "bfloat16"), ("nv", 256, "bfloat16"), ("tP", 256, "float32"),
+    ("hf", 16, "float32"), ("HE", 128, "float32"), ("HO", 128, "float16"), ("ex", 128, "bfloat16"), ("SEL", 128, "bfloat16"),
+    ("i8", 128, "int32"), ("FRG", 128, "bfloat16"), ("FQ0", 128, "bfloat16"),
+    ("jk", 16, "float32"), ("fb", 16, "float32"), ("fc", 16, "float32"),
     ("Pf", 256, "float32"), ("Pv", 256, "float32"), ("yb", 256, "float32"), ("yo", 256, "float32"), ("yl", 256, "float32"),
     ("y1", 16, "float32"), ("sp", 32, "float16"), ("so", 512, "float32"),
 ):
@@ -50,7 +60,94 @@ for _n in PS:
     SCRATCH[_n] = ("psum", [128, 512], "float32")
 
 SEMAPHORES = (["qv", "qs", "qp", "qg", "snd", "lx", "la", "lr", "lk", "lz", "lp", "oy", "oz"]
-              + ["mc%d" % t for t in range(1, HOPS)] + ["mp%d" % t for t in range(1, HOPS)] + ["ar%d" % d for d in (1, 2, 3)])
+              + [m + str(t) for m in ("ma", "mb", "ms") for t in range(HOPS - 1)] + ["ar%d" % d for d in (1, 2, 3)])
+
+
+def plan(calls):
+    n = len(calls)
+    pre = [dict() for _ in calls]
+    log, bank, sender = {}, {}, {}
+    for k, c in enumerate(calls):
+        def after(j, wait=True):
+            gap = calls[j]["done"] + WAKE if wait else 0.0
+            pre[k][j] = max(pre[k].get(j, 0.0), gap)
+        if c["kind"] == "gather":
+            if c["q"] in sender:
+                pre[k][sender[c["q"]]] = calls[sender[c["q"]]]["hold"]
+            sender[c["q"]] = k
+        if c["kind"] == "send":
+            sender[c["sem"]] = k
+        if c["kind"] == "land":
+            pre[k][sender[c["sem"]]] = calls[sender[c["sem"]]]["done"]
+        for vs, wr in ((c["ins"], False), (c["outs"], True)):
+            for _, nm, a, b in vs:
+                for a2, b2, w2, j in log.get(nm, []):
+                    if j != k and a < b2 and a2 < b and (wr or w2):
+                        after(j, not calls[j]["q"] == c["q"] == "p")
+                if nm in PS:
+                    old, cur = bank.get(nm, ([], []))
+                    if cur and calls[cur[0]]["q"] != c["q"]:
+                        old, cur = cur, []
+                    for j in old:
+                        after(j)
+                    if c["q"] == "p" and cur and cur[-1] != k:
+                        after(cur[-1], False)
+                    bank[nm] = (old, cur + [k])
+        for vs, wr in ((c["ins"], False), (c["outs"], True)):
+            for _, nm, a, b in vs:
+                keep = [e for e in log.get(nm, []) if not (wr and a <= e[0] and e[1] <= b)]
+                log[nm] = keep + [(a, b, wr, k)]
+    hold, queue = [c["hold"] for c in calls], [c["q"] for c in calls]
+    tail = [c["done"] - c["hold"] for c in calls]
+    ahead, back = [[] for _ in calls], [[] for _ in calls]
+    for k in range(n):
+        for j, gap in pre[k].items():
+            ahead[j].append((k, gap))
+            back[k].append((j, gap + hold[k] - hold[j]))
+
+    def run(post, first, rest):
+        left, start, free, out = [0] * n, list(first), {}, []
+        for k in range(n):
+            for j, _ in post[k]:
+                left[j] += 1
+        ready = {q: [k for k in range(n) if queue[k] == q and not left[k]] for q in set(queue)}
+        head = {}
+
+        def at(k):
+            return max(start[k], free.get(queue[k], 0.0))
+        while len(out) < n:
+            for q in ready:
+                if q not in head and ready[q]:
+                    head[q] = min((at(k), -rest[k], k) for k in ready[q])
+            a = min(head.values())[2]
+            for b in ready[queue[a]]:
+                if rest[b] > rest[a] and at(b) < at(a) + hold[a]:
+                    if max(at(b) + rest[b], at(b) + hold[b] + rest[a]) < max(at(a) + rest[a], at(a) + hold[a] + rest[b]):
+                        a = b
+            ready[queue[a]].remove(a)
+            del head[queue[a]]
+            start[a] = at(a)
+            free[queue[a]] = start[a] + hold[a]
+            out.append(a)
+            for j, gap in post[a]:
+                start[j] = max(start[j], start[a] + gap)
+                left[j] -= 1
+                if not left[j]:
+                    ready[queue[j]].append(j)
+                    head.pop(queue[j], None)
+        return out, [start[k] + hold[k] for k in range(n)]
+
+    rest = [0.0] * n
+    for k in range(n - 1, -1, -1):
+        rest[k] = max([calls[k]["done"]] + [max(gap, hold[k]) + rest[j] for j, gap in ahead[k]])
+    best = None
+    for _ in range(PASSES):
+        out, end = run(ahead, [0.0] * n, rest)
+        span = max(end[k] + tail[k] for k in range(n))
+        if best is None or span < best[0]:
+            best = (span, out)
+        rest = run(back, tail, end)[1]
+    return best[1]
 
 
 def rank_program(g, core, T, topo):
@@ -61,10 +158,7 @@ def rank_program(g, core, T, topo):
     nxt, prv = T.cores[(rank + 1) % n], T.cores[(rank - 1) % n]
     Q = {"v": g.vector, "s": g.scalar, "p": g.tensor, "g": g, "y": g.sync}
     QS = {"v": "qv", "s": "qs", "p": "qp", "g": "qg"}
-    cnt = {q: 0 for q in Q}
-    seen = {q: {} for q in Q}
-    log = {}
-    sent = [0]
+    calls = []
 
     def view(name, a=0, b=None, st=1, parts=128):
         if name in PART:
@@ -76,6 +170,455 @@ def rank_program(g, core, T, topo):
 
     def col(name):
         return view(name, 0, 1)
+
+    def width(v):
+        return v[0].shape[1]
+
+    def nbytes(v):
+        return v[0].shape[0] * width(v) * SIZE[SCRATCH[v[1]][2]]
+
+    def call(q, fn, outs, ins, hold, done=None, kind="compute", sem=None, count=0):
+        calls.append(dict(q=q, fn=fn, outs=outs, ins=ins, hold=hold, done=hold if done is None else done, kind=kind, sem=sem, count=count))
+
+    def vcost(o, a):
+        half = SIZE[SCRATCH[a[1]][2]] == 2 and SIZE[SCRATCH[o[1]][2]] == 2
+        return CYCLE * max(64, width(a) * (0.5 if half else 1))
+
+    def tt(o, a, b, op):
+        call("v", lambda: g.vector.tensor_tensor(o[0], a[0], b[0], op), [o], [a, b],
+             CYCLE * max(64, width(a) * (1 if a[1] in PS or b[1] in PS else 2)))
+
+    def tti(o, win, off, b, op):
+        call("v", lambda: g.vector.tensor_tensor(o[0], win[0].indirect(off[0]), b[0], op), [o], [win, off, b], 0.05 + GATHER * width(o))
+
+    def ts(o, a, s1, op0, s2=None, op1=None):
+        cs = [s for s in (s1, s2) if isinstance(s, tuple)]
+        x1, x2 = (s[0] if isinstance(s, tuple) else s for s in (s1, s2))
+        if op1 is None:
+            f = lambda: g.vector.tensor_scalar(o[0], a[0], x1, None, op0)
+        else:
+            f = lambda: g.vector.tensor_scalar(o[0], a[0], x1, x2, op0, op1)
+        call("v", f, [o], [a] + cs, vcost(o, a))
+
+    def cp(o, a):
+        call("v", lambda: g.vector.tensor_copy(o[0], a[0]), [o], [a], vcost(o, a))
+
+    def cpi(o, win, off):
+        call("v", lambda: g.vector.tensor_copy(o[0], win[0].indirect(off[0])), [o], [win, off], 0.05 + GATHER * width(o))
+
+    def scat(win, off, a):
+        call("v", lambda: g.vector.tensor_copy(win[0].indirect(off[0]), a[0]), [win], [off, a], 0.05 + SCATTER * width(a))
+
+    def turn32(o, a):
+        call("v", lambda: g.vector.transpose(o[0], a[0]), [o], [a], vcost(o, a))
+
+    def ms(o, c):
+        call("v", lambda: g.vector.memset(o[0], c), [o], [], vcost(o, o))
+
+    def act(o, a, f=F_.Copy, scale=1.0, bias=0.0, acc=None):
+        cs = [s for s in (scale, bias) if isinstance(s, tuple)]
+        sc, bi = (s[0] if isinstance(s, tuple) else s for s in (scale, bias))
+        if acc is None:
+            call("s", lambda: g.scalar.activation(o[0], a[0], f, bias=bi, scale=sc), [o], [a] + cs, 0.06 + CYCLE * width(a))
+        else:
+            call("s", lambda: g.scalar.activation(o[0], a[0], f, bias=bi, scale=sc, accum_out=acc[0]), [o, acc], [a] + cs,
+                 0.2 + CYCLE * width(a))
+
+    def acti(o, win, off):
+        call("s", lambda: g.scalar.activation(o[0], win[0].indirect(off[0]), F_.Copy), [o], [win, off], 0.065 + GATHER * width(o))
+
+    def mm(o, l, r, start=False, stop=False):
+        call("p", lambda: g.tensor.matmul(o[0], l[0], r[0], start, stop), [o], [l, r], COLUMN * max(min(64, width(l)), width(r)))
+
+    def spread(bank, a, l, r, start=False, stop=False):
+        for k in range(4):
+            mm(view(bank, a + 64 * k, a + 64 * k + 64), view(l), r, start and k == 0, stop and k == 3)
+
+    def iota(o, pat, base, cm):
+        call("g", lambda: g.iota(o[0], pat, base, cm, allow_small_or_imprecise_dtypes=True), [o], [], 0.13 + 2 * CYCLE * width(o))
+
+    def load(q, o, src, sem):
+        call(q, lambda: Q[q].dma_start(o[0], src), [o], [], 0.05, DMALAT + nbytes(o) / DMABW, "dma", sem, 16)
+
+    def store(q, out, a, sem):
+        call(q, lambda: Q[q].dma_start(out, a[0]), [], [a], 0.05, DMALAT + nbytes(a) / DMABW, "dma", sem, 16)
+
+    def send(d, o, a, sem, also=()):
+        dst, src = T.cores[(rank + d) % n], T.cores[(rank - d) % n]
+        rid, pid = topo.addr(dst, core)
+        call("g", lambda: g.remote_dma(o[0], a[0], T.sem[sem], T.sem.snd, pid, rid, topo.mask(core, dst)), [], [a] + list(also),
+             0.4, 0.4 + HOPLAT + nbytes(a) / LINK, "send", sem, len(topo.engines(core, dst)))
+        call("rem", None, [o], [], 0.0, 0.0, "land", sem, len(topo.engines(src, core)))
+
+    def in_turn():
+        calls[-1]["kind"] = "gather"
+
+    def mat(name, k):
+        return view(name, 128 * k, 128 * k + 128)
+
+    def state(t, buf="ST"):
+        return [view(buf, 448 * t, 448 * t + 256)] + [view(buf, 448 * t + 256 + 64 * x, 448 * t + 320 + 64 * x) for x in range(3)]
+
+    def record(t):
+        return view("AC") if t else view("AR", 0, 256)
+
+    def part(v, a, b):
+        return view(v[1], v[2] + a, v[2] + b)
+
+    SITES = view("X", 0, 2048)
+    HALVES = ((0, 128), (128, 256))
+
+    load("y", view("PI"), T.pn[:], "lp")
+    load("s", view("SI", parts=8), T.s0[:], "lz")
+    load("s", view("KA"), T.kap[:], "lk")
+    load("s", view("AR", 0, 256), T.a0[:], "la")
+    load("y", SITES, T.x[:], "lx")
+    load("s", view("AR", 256, 512), T.r0[:], "lr")
+
+    iota(view("ip"), [[0, 16]], 0, 1)
+    iota(view("i2"), [[1, 16], [0, 2]], 0, 0)
+    iota(view("inn"), [[1, 16]], 0, 0)
+    iota(view("ia"), [[1, 128]], 0, -1)
+    iota(view("w8i", parts=8), [[1, 144]], -15, -16)
+    iota(view("ib"), [[-16, 8], [0, 16]], 0, 1)
+    iota(view("idl", 0, 8), [[1, 8]], 1, 0)
+    for nm, c in (("ONE", 1.0), ("F25", 0.25), ("LE", 0.0), ("LP", 0.0), ("TH", 67.0), ("C32k", 32768.0), ("C511", 511.0),
+                  ("Fm", -1.0 / 4096), ("F16", 16.0)):
+        ms(view(nm), c)
+    for nm, lo, hi in (("FRG", 65536.0, 480.0), ("FQ0", -65536.0, -448.0)):
+        ms(view(nm), hi)
+        ms(view(nm, parts=64), lo)
+    ms(view("CT", 0, 240), 1537.0)
+    ms(view("CT", 240, 256), 1505.0)
+    ts(view("q15"), view("ip"), 15, A_.bitwise_and)
+    ts(view("q31i"), view("ip"), 31, A_.bitwise_and)
+    cp(col("p16"), col("q15"))
+    cp(col("q31"), col("q31i"))
+    ts(col("c3"), col("p16"), 31, A_.mult, col("q31"), A_.add)
+    ts(col("p256"), col("p16"), 16, A_.mult)
+    ts(col("dum"), col("p16"), 2048, A_.add)
+    ts(col("dun"), col("p16"), 2064, A_.add)
+    ts(view("q7"), view("ip"), 7, A_.bitwise_and)
+    ts(view("EV"), view("q7"), 2, A_.mult)
+    ts(view("OD"), view("q7"), 2, A_.mult, 1, A_.add)
+    iota(view("i8"), [[1, 16], [0, 8]], 0, 0)
+    ts(view("SEL"), view("i8"), col("p16"), A_.is_equal)
+    ts(view("DUP1"), view("i2"), 16, A_.mult, col("p16"), A_.add)
+    ts(view("UN1"), view("inn"), col("c3"), A_.add)
+    ts(view("DUP2"), view("i2"), col("p256"), A_.add)
+    ts(view("UN2"), view("inn"), 32, A_.mult, col("q31"), A_.add)
+    cp(view("RK"), view("inn"))
+    ts(view("RVK"), view("inn"), -1, A_.mult, 15, A_.add)
+    ts(view("RVP"), view("RVK"), 16, A_.mult, col("p16"), A_.add)
+    cp(view("REP"), view("q15"))
+    ts(view("LT"), view("inn"), 16, A_.mult, col("p16"), A_.add)
+    ts(view("LT"), view("LT"), 128, A_.add)
+    ts(view("Ib"), view("ia"), 0, A_.is_equal)
+    for nm in EYES:
+        act(view(nm), view("Ib"), scale=EYES[nm])
+    ts(view("I1057"), view("Ib"), 1057, A_.mult)
+    for k in range(16):
+        act(mat("KI", k), view("Ib"), scale=7.5 - k)
+    ts(view("W8", parts=8), view("w8i", parts=8), 0, A_.is_equal)
+    ts(view("jb"), view("ib"), -16, A_.bitwise_and)
+    ts(view("BM"), view("jb"), 0, A_.is_equal)
+    ts(view("LE", 15, 143, 16), view("BM", 0, 128, 16), -BIG, A_.mult)
+    ts(view("LP", 15, 143, 16), view("BM", 0, 128, 16), BIG, A_.mult)
+    ts(view("jm"), view("ia"), 15, A_.bitwise_and)
+    tt(view("J"), view("jm"), view("jb"), A_.add)
+    ts(view("tg"), view("idl", 0, 8), col("p16"), A_.is_gt)
+    ts(view("te"), view("idl", 0, 8), -1, A_.mult, 16, A_.add)
+    tt(view("tc"), view("tg"), view("te"), A_.mult)
+    for d in range(1, 9):
+        ts(mat("SH", d - 1), view("J"), d, A_.is_equal)
+        ts(mat("RD", d - 1), view("J"), view("tc", d - 1, d), A_.is_equal, 4096, A_.mult)
+    cp(col("kf"), view("KA"))
+    ts(view("rk"), view("inn"), col("p16"), A_.is_equal, col("kf"), A_.mult)
+    mm(view("Q1", 0, 16), view("BM"), view("rk"), True, True)
+    cp(view("KC"), view("Q1", 0, 16))
+    cpi(view("KTa"), view("KC"), view("RK"))
+    cpi(view("KTb"), view("KC"), view("RVK"))
+    tt(view("KD"), view("KTa", 0, 256, 16), view("KTb", 0, 256, 16), A_.subtract)
+    for k in range(16):
+        ts(mat("DG", k), view("I16"), view("KD", k, k + 1), A_.mult)
+    P0, s0_, U0, p0 = state(0)
+    cpi(view("TA"), view("PI"), view("DUP1"))
+    turn32(view("TB"), view("TA"))
+    cpi(P0, view("TB"), view("UN1"))
+    cp(view("S16", parts=8), view("SI", parts=8))
+    for i in range(16):
+        mm(view("E0", 0, 16), view("W8", 15 - i, 143 - i, parts=8), view("S16", i, 256, 16, parts=8), i == 0, i == 15)
+    for k in range(4):
+        cp(part(s0_, 16 * k, 16 * k + 16), view("E0", 0, 16))
+    ms(U0, 1.0)
+    ms(p0, -7.5)
+
+    def sites(t):
+        P, s_, U, pc = state(t)
+        U1 = part(U, 0, 16)
+        d = t % n
+        if t:
+            mm(view("E1", 128, 144), view("Ib"), view("LT"), True)
+            mm(view("E1", 128, 144), view("N128"), U1, False, True)
+            cp(view("AO"), view("E1", 128, 144))
+            acti(record(t), view("AR", 512 * d, 512 * d + 512), view("AO"))
+            in_turn()
+        mm(view("ZB", 0, 256), view("F25"), view("ONE"), True)
+        mm(view("ZB", 256, 512), view("I16"), view("KTa"))
+        mm(view("ZB", 256, 512), view("I16"), view("KTb" if t else "KTa"))
+        spread("ZB", 0, "Ib", s_)
+        spread("ZB", 256, "I1184", s_, stop=not t)
+        if t:
+            for k in range(16):
+                mm(view("ZB", 256 + 16 * k, 272 + 16 * k), mat("DG", k), U1, False, k == 15)
+        for a, b in HALVES:
+            tt(view("Z", a, b), part(P, a, b), view("ZB", a, b), A_.mult)
+            tt(view("ZI", a, b), view("Z", a, b), view("ZB", 256 + a, 256 + b), A_.add)
+            ts(view("HI", a, b), view("ZI", a, b), 5, A_.arith_shift_right, 2047, A_.bitwise_and)
+            cp(view("H16", a, b), view("HI", a, b))
+        if t:
+            for k in range(16):
+                mm(view("Q1", 256 + 16 * k, 272 + 16 * k), mat("KI", k), U1, k == 0)
+            spread("Q1", 256, "Ib", pc, stop=True)
+            act(view("A1"), view("Q1", 256, 512), F_.Abs, 4096.0)
+            in_turn()
+            act(view("T2"), view("Q1", 256, 512), F_.Relu, -4096.0)
+            in_turn()
+        else:
+            iota(view("A1"), [[4096, 16], [0, 16]], 0, 0)
+            act(view("T2"), view("A1"))
+        act(view("RG", 256, 512), view("A1"), F_.Relu, -1.0, 1.0)
+        in_turn()
+        mm(view("CB", 0, 256), view("I2k"), view("CT"), True)
+        mm(view("CB", 0, 256), view("F25"), view("ONE"))
+        spread("CB", 0, "Ikp", pc)
+        spread("CB", 0, "I32k", U)
+        mm(view("CB", 240, 256), view("N64k"), U1)
+        mm(view("CB", 0, 256), view("N1k"), view("A1"))
+        mm(view("CB", 0, 256), view("I1057"), view("T2"), False, True)
+
+    def row_p(t):
+        P, s_, U, pc = state(t)
+        tt(view("PR"), view("HI"), view("RG", 256, 512), A_.mult)
+        in_turn()
+        tt(view("HK"), view("HI"), view("CB", 0, 256), A_.add)
+        in_turn()
+        for k in range(16):
+            mm(view("CB", 320, 336), view("Ib"), view("PR", 16 * k, 16 * k + 16), k == 0)
+        o = view("CB", 256, 320)
+        mm(o, view("I2k"), view("C511"))
+        mm(o, view("F25"), view("ONE", 0, 64))
+        mm(o, view("Ikm"), pc)
+        mm(o, view("N32k"), U)
+        for k in range(4):
+            mm(o, view("Ib"), view("PR", 64 * k, 64 * k + 64), False, k == 3)
+
+    def pairs_open():
+        cp(view("hp"), view("CB", 320, 336))
+        in_turn()
+        cp(view("hu"), view("CB", 320, 336))
+        in_turn()
+        for d in range(8):
+            o = view("DB", 16 * d, 16 * d + 16)
+            mm(o, mat("SH", d), view("hp"), d == 0)
+            mm(o, view("NI"), view("hp"))
+
+    def columns_open():
+        cp(view("hf"), view("CB", 320, 336))
+        acti(view("HE"), view("hf"), view("EV", 0, 8))
+        tti(view("HO"), view("hf"), view("OD", 0, 8), view("SEL"), A_.mult)
+        mm(view("CB", 384, 512), view("BM"), view("HO"), True)
+
+    def fold(o, nm, rows):
+        if rows == 4:
+            a = 32 * (nm == "M")
+            tt(view("fa", a, a + 32), view(nm, 0, 32), view(nm, 32, 64), A_.max)
+            tt(o, view("fa", a, a + 16), view("fa", a + 16, a + 32), A_.max)
+        else:
+            tt(o, view(nm, 0, 16), view(nm, 16, 32), A_.max)
+
+    def distances(t):
+        kind, pairs = "".join(CHUNKS), [0]
+
+        def span(buf, k, m=1):
+            return view(buf, 256 * k, 256 * (k + m))
+
+        def gather(k):
+            off = view("H16", 16 * k, 16 * k + 16)
+            if kind[k] == "S":
+                acti(span("DR", k), SITES, off)
+            else:
+                tti(span("DR", k), SITES, off, record(t), A_.subtract)
+            in_turn()
+
+        def size(k, m):
+            if kind[k] == "S":
+                q = "Q%d" % (pairs[0] % 2)
+                pairs[0] += 1
+                mm(view(q, 0, 256 * m), view("Ib"), span("DR", k, m), True)
+                for x in range(m):
+                    mm(view(q, 256 * x, 256 * x + 256), view("NI"), record(t), False, x == m - 1)
+                act(span("DA", k, m), view(q, 0, 256 * m), F_.Abs)
+            elif kind[k] == "A":
+                act(span("DA", k, m), span("DR", k, m), F_.Abs)
+            else:
+                ts(span("DA", k, m), span("DR", k, m), 0.0, A_.max, 2.0, A_.mult)
+            in_turn()
+
+        def decide(c):
+            kinds, k0 = CHUNKS[c], len("".join(CHUNKS[:c]))
+            rows = len(kinds)
+            bank = "E%d" % (c % 2)
+            e = view(bank, 0, 16 * rows)
+            mm(e, view("TH"), view("C32k", 0, 16 * rows), True)
+            if "R" in kinds:
+                a, b = kinds.index("R"), kinds.rindex("R") + 1
+                for i in range(16):
+                    mm(view(bank, 16 * a, 16 * b), view("LP", 15 - i, 143 - i), view("DR", 256 * (k0 + a) + i, 256 * (k0 + b), 16))
+            for i in range(16):
+                mm(e, view("LE", 15 - i, 143 - i), view("DA", 256 * k0 + i, 256 * (k0 + rows), 16), False, i == 15)
+
+        def choose(c, step):
+            k0, rows = len("".join(CHUNKS[:c])), len(CHUNKS[c])
+            e, hk = view("E%d" % (c % 2), 0, 16 * rows), view("HK", 16 * k0, 16 * (k0 + rows))
+            if step == "m":
+                tt(e if c else view("M"), e, hk, A_.min)
+                in_turn()
+            elif step == "x":
+                tt(view("M", 0, 16 * rows), e if c else view("CB", 256, 320), view("M", 0, 16 * rows), A_.max)
+                in_turn()
+            else:
+                fold(view("fb"), "M", 4)
+                cpi(view("M4"), view("fb"), view("REP", 0, 4))
+                if rows == 1:
+                    tt(view("fc"), e, hk, A_.min)
+                else:
+                    tt(view("M2", 0, 16 * rows), e, hk, A_.min)
+                    fold(view("fc"), "M2", rows)
+                tti(view("W"), view("fc"), view("REP", 0, 4), view("M4"), A_.max)
+
+        for step in STEPS.split():
+            k = int(step[1], 16)
+            if step[0] == "g":
+                gather(k)
+            elif step[0] == "d":
+                decide(k)
+            elif step[0] in "mxw":
+                choose(k, step[0])
+            elif step[0] == "h":
+                row_p(t)
+            elif step[0] == "p":
+                pairs_open()
+            else:
+                size(k, " abc".index(step[0]))
+
+    def writes(t):
+        acti(view("old"), SITES, view("hu"))
+        mm(view("E1", 256, 512), view("Ib"), record(t), True)
+        mm(view("E1", 256, 512), view("Ib"), view("old"), False, True)
+        act(view("n1"), view("E1", 256, 512), F_.Identity, 0.5, 127.75)
+        act(view("nv"), view("n1"), F_.Identity, bias=-128.0)
+        ts(view("hit"), view("W"), 2 ** 21, A_.is_ge, 4096, A_.mult)
+        columns_open()
+        for k in range(4):
+            mm(view("CB", 384 + 32 * k, 416 + 32 * k), view("Ib"), view("hit", 0, 64, 2), False, k == 3)
+        tt(view("ex"), view("CB", 384, 512), view("HE"), A_.is_equal)
+        for d in range(8):
+            mm(view("DB", 16 * d, 16 * d + 16), mat("SH", d), view("hit", 0, 16))
+        mm(view("DB", 0, 64), view("Ib"), view("hit"))
+        mm(view("DB", 64, 128), view("Ib"), view("hit"), False, True)
+        mm(view("Q1", 0, 16), view("Ib"), view("hp"), True)
+        mm(view("Q1", 0, 16), view("Ib"), view("hit", 0, 16))
+        ts(view("eq"), view("DB", 0, 128), 0, A_.is_equal)
+        for i in range(16):
+            mm(view("Q1", 1, 16, 2), view("LP", 15 - i, 143 - i), view("ex", 8 * i, 8 * i + 8))
+        for d in range(8):
+            mm(view("Q1", 0, 16), mat("RD", d), view("eq", 16 * d, 16 * d + 16), False, d == 7)
+        ts(view("fo", 0, 16, 2), view("Q1", 0, 16, 2), col("dum"), A_.min)
+        odd = (view("fo", 1, 16, 2)[0], "fp", 0, 16)
+        ts(odd, view("Q1", 1, 16, 2), col("dun"), A_.min)
+        for j in range(14, -1, -2):
+            scat(view("X"), view("fo", j, j + 2), view("nv", 16 * j, 16 * j + 32))
+            calls[-1]["ins"].append(odd)
+
+    def limit():
+        mm(view("E1", 64, 80), view("Fm"), view("hit", 0, 16), True, True)
+        act(view("jk"), view("E1", 64, 80), F_.Identity, bias=2040.5 / 16, acc=col("mc"))
+        act(col("m1"), col("mc"), F_.Identity, bias=ROUND16)
+        act(col("m2"), col("m1"), F_.Identity, -1.0, ROUND16)
+        act(col("m3"), col("m2"), F_.Identity, bias=74.5)
+        act(view("TH"), view("ONE", 0, 128), F_.Identity, col("mc"), col("m3"))
+
+    def become(t, names):
+        P, s_, U, pc = state(t)
+        _, sn, Un, pn_ = state(t, "CO")
+        w = view("W")
+        for bank, sign in (("RG", "IN"), ("Q0", "NI")):
+            mm(view(bank, 0, 256), view("F" + bank), view("ONE"), True)
+            spread(bank, 0, sign[0] + "4k", pc)
+            mm(view(bank, 0, 256), view(sign[0] + "32"), view("A1"))
+            mm(view(bank, 0, 256), view(sign[1] + "31"), view("T2"))
+        ts(view("hs"), w, 4095, A_.bitwise_and)
+        ts(view("hk"), w, 2.0 ** -17, A_.mult, 1023.5076, A_.add)
+        ts(view("ub"), w, 16, A_.arith_shift_right, 1, A_.bitwise_and)
+        ts(view("pi"), w, 12, A_.arith_shift_right, 15, A_.bitwise_and)
+        tt(view("sh" if t == 0 else "sf"), s_, view("hs"), A_.mult)
+        if t:
+            ts(view("sh"), view("sf"), 25952 * t, A_.add)
+        ts(sn, view("hs"), -32, A_.add)
+        ts(Un, view("ub"), 2, A_.mult, -1, A_.add)
+        ts(pn_, view("pi"), -7.5, A_.add)
+        ts(view("bq"), view("sh"), 5, A_.arith_shift_right, 2047, A_.bitwise_and)
+        for bank, sign in (("RG", "IN"), ("Q0", "NI")):
+            spread(bank, 0, sign[1] + "4k", view("hk"))
+            spread(bank, 0, sign[0] + "16", view("hit"), stop=True)
+        for a, b in HALVES:
+            tt(view("RG", a, b), part(P, a, b), view("RG", a, b), A_.min)
+            for x in range(a, b, 64):
+                tt(view("tP", x, x + 64), view("bq"), view("Q0", x, x + 64), A_.min)
+            tt(part(names, a, b), view("tP", a, b), view("RG", a, b), A_.max)
+
+    def finish():
+        _, sn, Un, pn_ = state(HOPS - 1, "CO")
+        acti(view("Pv"), view("Pf"), view("RVP"))
+        mm(view("ZB", 256, 512), view("F16"), view("ONE"), True)
+        spread("ZB", 256, "N2k", Un, stop=True)
+        tt(view("yb"), view("Pf"), view("ZB", 256, 512), A_.subtract)
+        tt(view("ZB", 256, 512), view("Pv"), view("ZB", 256, 512), A_.min)
+        tt(view("yo"), view("ZB", 256, 512), view("yb"), A_.max)
+        acti(view("TA"), view("yo"), view("DUP2"))
+        turn32(view("TB"), view("TA"))
+        acti(view("yl"), view("TB"), view("UN2"))
+        store("s", T.yn[:], view("yl"), "oz")
+        ts(view("y1"), part(Un, 0, 16), -8.0, A_.mult, 15.5, A_.add)
+        cp(view("sp", 0, 16), part(sn, 0, 16))
+        tt(view("sp", 16, 32), part(pn_, 0, 16), view("y1"), A_.add)
+        for i in range(16):
+            mm(view("CB", i, 512, 16, parts=8), view("Ib", i, 128, 16), view("sp"), i == 0, i == 15)
+        act(view("so", parts=8), view("CB", parts=8))
+        store("y", T.ys[:], view("so", 0, 256, parts=8), "oy")
+        store("y", T.yp[:], view("so", 256, 512, parts=8), "oy")
+        store("y", T.yx[:], SITES, "oy")
+
+    sites(0)
+    for t in range(HOPS):
+        if t < n - 1:
+            send(t + 1, view("AR", 512 * t + 512, 512 * t + 1024), view("AR", 0, 512), "ar%d" % (t + 1), [view("H16", 0, 64)])
+        distances(t)
+        writes(t)
+        if t < HOPS - 1:
+            limit()
+            become(t, state(t, "CO")[0])
+            for a, b, sem in PIECES:
+                send(1, view("ST", 448 * t + 448 + a, 448 * t + 448 + b), view("CO", 448 * t + a, 448 * t + b), sem + str(t))
+            sites(t + 1)
+        else:
+            become(t, view("Pf"))
+            finish()
+
+    cnt = {q: 0 for q in QS}
+    seen = {q: {} for q in Q}
+    log, total = {}, {"snd": 0}
 
     def need(q, ev):
         if seen[q].get(ev[0], 0) < ev[1]:
@@ -89,7 +632,7 @@ def rank_program(g, core, T, topo):
                 ps = nm in PS
                 for (q2, a2, b2, w2), ev in log.get(nm, {}).items():
                     hitx = a < b2 and a2 < b
-                    dep = (hitx and w2 and not (wr and ps and q == "p")) or (q2 != q and ((hitx and (wr or w2)) or ps))
+                    dep = (hitx and (wr or w2) and not q == q2 == "p") or (q2 != q and ps)
                     if dep and todo.get(ev[0], 0) < ev[1]:
                         todo[ev[0]] = ev[1]
         for k in sorted(todo):
@@ -104,471 +647,26 @@ def rank_program(g, core, T, topo):
                         del d[k]
                 d[(q, a, b, wr)] = ev
 
-    def emit(q, fn, outs, ins):
-        order(q, outs, ins)
-        cnt[q] += 1
-        fn().then_inc(T.sem[QS[q]], 1)
-        note(q, outs, ins, (QS[q], cnt[q]))
-
-    def tt(o, a, b, op):
-        emit("v", lambda: g.vector.tensor_tensor(o[0], a[0], b[0], op), [o], [a, b])
-
-    def tti(o, win, off, b, op):
-        emit("v", lambda: g.vector.tensor_tensor(o[0], win[0].indirect(off[0]), b[0], op), [o], [win, off, b])
-
-    def ts(o, a, s1, op0, s2=None, op1=None):
-        cs = [s for s in (s1, s2) if isinstance(s, tuple)]
-        x1, x2 = (s[0] if isinstance(s, tuple) else s for s in (s1, s2))
-        if op1 is None:
-            f = lambda: g.vector.tensor_scalar(o[0], a[0], x1, None, op0)
+    if not ORDER:
+        ORDER.extend(plan(calls))
+    for c in [calls[k] for k in ORDER]:
+        q = c["q"]
+        if c["kind"] == "land":
+            note(q, c["outs"], [], (c["sem"], c["count"]))
+            continue
+        order(q, c["outs"], c["ins"])
+        if c["kind"] == "send":
+            c["fn"]()
+            total["snd"] += c["count"]
+        elif c["kind"] == "dma":
+            c["fn"]().then_inc(T.sem[c["sem"]], 16)
+            total[c["sem"]] = total.get(c["sem"], 0) + 16
+            note("dma", c["outs"], [], (c["sem"], 16))
         else:
-            f = lambda: g.vector.tensor_scalar(o[0], a[0], x1, x2, op0, op1)
-        emit("v", f, [o], [a] + cs)
-
-    def cp(o, a):
-        emit("v", lambda: g.vector.tensor_copy(o[0], a[0]), [o], [a])
-
-    def cpi(o, win, off):
-        emit("v", lambda: g.vector.tensor_copy(o[0], win[0].indirect(off[0])), [o], [win, off])
-
-    def scat(win, off, a):
-        emit("v", lambda: g.vector.tensor_copy(win[0].indirect(off[0]), a[0]), [win], [off, a])
-
-    def turn32(o, a):
-        emit("v", lambda: g.vector.transpose(o[0], a[0]), [o], [a])
-
-    def ms(o, c):
-        emit("v", lambda: g.vector.memset(o[0], c), [o], [])
-
-    def act(o, a, f=F_.Copy, scale=1.0, bias=0.0, acc=None):
-        cs = [s for s in (scale, bias) if isinstance(s, tuple)]
-        sc, bi = (s[0] if isinstance(s, tuple) else s for s in (scale, bias))
-        if acc is None:
-            emit("s", lambda: g.scalar.activation(o[0], a[0], f, bias=bi, scale=sc), [o], [a] + cs)
-        else:
-            emit("s", lambda: g.scalar.activation(o[0], a[0], f, bias=bi, scale=sc, accum_out=acc[0]), [o, acc], [a] + cs)
-
-    def acti(o, win, off):
-        emit("s", lambda: g.scalar.activation(o[0], win[0].indirect(off[0]), F_.Copy), [o], [win, off])
-
-    def mm(o, l, r, start=False, stop=False):
-        emit("p", lambda: g.tensor.matmul(o[0], l[0], r[0], start, stop), [o], [l, r])
-
-    def spread(bank, a, l, r, start=False, stop=False, blocks=4):
-        for k in range(blocks):
-            mm(view(bank, a + 64 * k, a + 64 * k + 64), view(l), r, start and k == 0, stop and k == blocks - 1)
-
-    def iota(o, pat, base, cm):
-        emit("g", lambda: g.iota(o[0], pat, base, cm), [o], [])
-
-    def load(q, o, src, sem):
-        order(q, [o], [])
-        Q[q].dma_start(o[0], src).then_inc(T.sem[sem], 16)
-        note("dma", [o], [], (sem, 16))
-
-    def send(dst, o, a, sem):
-        order("g", [], [a])
-        rid, pid = topo.addr(dst, core)
-        g.remote_dma(o[0], a[0], T.sem[sem], T.sem.snd, pid, rid, topo.mask(core, dst))
-        sent[0] += len(topo.engines(core, dst))
-
-    outs = {}
-
-    def store(q, out, a, sem):
-        order(q, [], [a])
-        Q[q].dma_start(out, a[0]).then_inc(T.sem[sem], 16)
-        outs[sem] = outs.get(sem, 0) + 16
-
-    def mat(name, k):
-        return view(name, 128 * k, 128 * k + 128)
-
-    def state(buf, t):
-        return [view(buf, 192 * t + 64 * x, 192 * t + 64 * x + 64) for x in range(3)]
-
-    def first16(v):
-        return view(v[1], v[2], v[2] + 16)
-
-    SITES = view("X", 0, 2048)
-
-    load("y", view("PI"), T.pn[:], "lp")
-    load("s", view("SI", parts=8), T.s0[:], "lz")
-    load("s", view("KA"), T.kap[:], "lk")
-    load("y", view("X", 0, 2048), T.x[:], "lx")
-    load("s", view("AR", 0, 256), T.a0[:], "la")
-    load("s", view("AR", 256, 512), T.r0[:], "lr")
-
-    iota(view("ip"), [[0, 16]], 0, 1)
-    iota(view("i2"), [[1, 16], [0, 2]], 0, 0)
-    iota(view("inn"), [[1, 16]], 0, 0)
-    iota(view("ia"), [[1, 128]], 0, -1)
-    iota(view("w8i", parts=8), [[1, 144]], -15, -16)
-    iota(view("ib"), [[-16, 8], [0, 16]], 0, 1)
-    iota(view("idl", 0, 8), [[1, 8]], 1, 0)
-    ms(view("ONE"), 1.0)
-    ms(view("F25"), 0.25)
-    ts(view("q15"), view("ip"), 15, A_.bitwise_and)
-    ts(view("q31i"), view("ip"), 31, A_.bitwise_and)
-    ms(view("LE"), 0.0)
-    ms(view("LP"), 0.0)
-    cp(col("p16"), col("q15"))
-    cp(col("q31"), col("q31i"))
-    ms(view("CT", 0, 240), 1537.0)
-    ms(view("CT", 240, 256), 1505.0)
-    ts(view("DUP1"), view("i2"), 16, A_.mult, col("p16"), A_.add)
-    ts(col("c3"), col("p16"), 31, A_.mult, col("q31"), A_.add)
-    ts(view("Ib"), view("ia"), 0, A_.is_equal)
-    cp(view("RK"), view("inn"))
-    ts(view("UN1"), view("inn"), col("c3"), A_.add)
-    cpi(view("TA"), view("PI"), view("DUP1"))
-    for nm in EYES:
-        act(view(nm), view("Ib"), scale=EYES[nm])
-    cp(col("kf"), view("KA"))
-    cp(view("S16", parts=8), view("SI", parts=8))
-    turn32(view("TB"), view("TA"))
-    ts(view("W8", parts=8), view("w8i", parts=8), 0, A_.is_equal)
-    ts(view("jb"), view("ib"), -16, A_.bitwise_and)
-    ts(view("rk"), view("inn"), col("p16"), A_.is_equal, col("kf"), A_.mult)
-    cpi(view("MP", 0, 256), view("TB"), view("UN1"))
-    for i in range(16):
-        mm(view("E0", 0, 16), view("W8", 15 - i, 143 - i, parts=8), view("S16", i, 256, 16, parts=8), i == 0, i == 15)
-    ts(view("BM"), view("jb"), 0, A_.is_equal)
-    ts(view("LT"), view("inn"), 16, A_.mult, col("p16"), A_.add)
-    s0_, U0, p0 = state("MC", 0)
-    for k in range(4):
-        cp(view("MC", 16 * k, 16 * k + 16), view("E0", 0, 16))
-    mm(view("Q1", 0, 16), view("BM"), view("rk"), True, True)
-    ms(U0, 1.0)
-    ms(p0, -7.5)
-    ts(view("LT"), view("LT"), 128, A_.add)
-    cp(view("KC"), view("Q1", 0, 16))
-    ts(view("LE", 15, 143, 16), view("BM", 0, 128, 16), -BIG, A_.mult)
-    ts(view("LP", 15, 143, 16), view("BM", 0, 128, 16), BIG, A_.mult)
-    cpi(view("KTa"), view("KC"), view("RK"))
-    for k in range(16):
-        act(mat("KI", k), view("Ib"), scale=7.5 - k)
-    ms(view("TH"), 67.0)
-    ms(view("C32k"), 32768.0)
-    ms(view("C511"), 511.0)
-
-    def late_constants():
-        ts(view("jm"), view("ia"), 15, A_.bitwise_and)
-        ts(view("tg"), view("idl", 0, 8), col("p16"), A_.is_gt)
-        ts(view("te"), view("idl", 0, 8), -1, A_.mult, 16, A_.add)
-        tt(view("J"), view("jm"), view("jb"), A_.add)
-        cp(view("REP"), view("q15"))
-        tt(view("tc"), view("tg"), view("te"), A_.mult)
-        ts(col("dum"), col("p16"), 2048, A_.add)
-        ms(view("Fm"), -1.0 / 4096)
-        for d in range(1, 9):
-            ts(mat("SH", d - 1), view("J"), d, A_.is_equal)
-        for d in range(1, 9):
-            ts(mat("RD", d - 1), view("J"), view("tc", d - 1, d), A_.is_equal, 4096, A_.mult)
-
-    def key_constants():
-        steps = [lambda: ts(view("RVK"), view("inn"), -1, A_.mult, 15, A_.add),
-                 lambda: cpi(view("KTb"), view("KC"), view("RVK")),
-                 lambda: tt(view("KD"), view("KTa", 0, 256, 16), view("KTb", 0, 256, 16), A_.subtract)]
-        for k in range(16):
-            steps.append(lambda k=k: ts(mat("DG", k), view("I16"), view("KD", k, k + 1), A_.mult))
-        return steps
-
-    def end_constants():
-        return [lambda: ts(col("p256"), col("p16"), 16, A_.mult),
-                lambda: ts(view("UN2"), view("inn"), 32, A_.mult, col("q31"), A_.add),
-                lambda: ts(view("RVP"), view("RVK"), 16, A_.mult, col("p16"), A_.add),
-                lambda: ts(view("DUP2"), view("i2"), col("p256"), A_.add),
-                lambda: ms(view("F16"), 16.0)]
-
-    def arrive(t):
-        s_, U, pc = state("MC", t)
-        if t:
-            ne = len(topo.engines(prv, core))
-            note("rem", [view("MC", 192 * t, 192 * t + 192)], [], ("mc%d" % t, ne))
-            note("rem", [view("MP", 256 * t, 256 * t + 256)], [], ("mp%d" % t, ne))
-        d = t % n
-        if 1 <= t <= 3:
-            note("rem", [view("AR", 512 * d, 512 * d + 512)], [], ("ar%d" % d, len(topo.engines(T.cores[(rank - d) % n], core))))
-        mm(view("ZB", 0, 256), view("F25"), view("ONE"), True)
-        mm(view("ZB", 256, 512), view("I16"), view("KTa"))
-        mm(view("ZB", 256, 512), view("I16"), view("KTb" if t else "KTa"))
-        mm(view("E1", 128, 144), view("Ib"), view("LT"), True)
-        mm(view("E1", 128, 144), view("N128"), first16(U), False, True)
-        spread("ZB", 0, "Ib", s_)
-        if t:
-            for k in range(16):
-                mm(view("ZB", 256 + 16 * k, 272 + 16 * k), mat("DG", k), first16(U))
-        spread("ZB", 256, "I1184", s_, stop=True)
-        for k in range(16):
-            mm(view("RG", 16 * k, 16 * k + 16), mat("KI", k), first16(U), k == 0)
-        spread("RG", 0, "Ib", pc, stop=True)
-
-    def records(t):
-        d = t % n
-        cp(view("AO"), view("E1", 128, 144))
-        acti(view("AC"), view("AR", 512 * d, 512 * d + 512), view("AO"))
-
-    def rows_against_p(t):
-        s_, U, pc = state("MC", t)
-        act(view("XK"), view("RG", 0, 256))
-        act(view("T1"), view("RG", 0, 256), F_.Relu)
-        mm(view("RG", 256, 512), view("Ib"), view("XK"), True)
-        mm(view("RG", 256, 512), view("N2"), view("T1"), False, True)
-        act(view("RG", 256, 512), view("RG", 256, 512), F_.Relu, bias=1.0)
-        mm(view("CB", 0, 256), view("I2k"), view("CT"), True)
-        mm(view("CB", 0, 256), view("F25"), view("ONE"))
-        spread("CB", 0, "Ikp", pc)
-        spread("CB", 0, "I32k", U)
-        mm(view("CB", 240, 256), view("N64k"), first16(U))
-        mm(view("CB", 0, 256), view("Nkp"), view("XK"))
-        mm(view("CB", 0, 256), view("NB"), view("T1"), False, True)
-
-    def site_steps(t, a, b):
-        return [lambda: tt(view("Z", a, b), view("MP", 256 * t + a, 256 * t + b), view("ZB", a, b), A_.mult),
-                lambda: tt(view("ZI", a, b), view("Z", a, b), view("ZB", 256 + a, 256 + b), A_.add),
-                lambda: ts(view("HI", a, b), view("ZI", a, b), 5, A_.arith_shift_right, 2047, A_.bitwise_and),
-                lambda: cp(view("H16", a, b), view("HI", a, b))]
-
-    def weave(*lists):
-        return [l[k] for k in range(max(len(l) for l in lists)) for l in lists if k < len(l)]
-
-    def grow(k):
-        acti(view("DR", 256 * k, 256 * k + 256), SITES, view("H16", 16 * k, 16 * k + 16))
-
-    def psub(k, q):
-        mm(view(q, 0, 512), view("Ib"), view("DR", 256 * k, 256 * k + 512), True)
-        mm(view(q, 0, 256), view("NI"), view("AC"))
-        mm(view(q, 256, 512), view("NI"), view("AC"), False, True)
-
-    def absps(k, q):
-        act(view("DA", 256 * k, 256 * k + 512), view(q), F_.Abs)
-
-    def vrows(*ks):
-        for k in ks:
-            tti(view("DR", 256 * k, 256 * k + 256), SITES, view("H16", 16 * k, 16 * k + 16), view("AC"), A_.subtract)
-
-    def absrows(k, k2):
-        act(view("DA", 256 * k, 256 * k2), view("DR", 256 * k, 256 * k2), F_.Abs)
-
-    def relurows(k, k2):
-        ts(view("DA", 256 * k, 256 * k2), view("DR", 256 * k, 256 * k2), 0.0, A_.max, 2.0, A_.mult)
-
-    def dopen(c, k=0, k2=0):
-        e = "E%d" % (c % 2)
-        mm(view(e, 0, 64), view("TH"), view("C32k"), True)
-        if k2 > k:
-            for i in range(16):
-                mm(view(e, 16 * (k % 4), 16 * (k % 4 + k2 - k)), view("LP", 15 - i, 143 - i), view("DR", 256 * k + i, 256 * k2, 16))
-
-    def dsum(c):
-        for i in range(16):
-            mm(view("E%d" % (c % 2), 0, 64), view("LE", 15 - i, 143 - i), view("DA", 1024 * c + i, 1024 * c + 1024, 16), False, i == 15)
-
-    def dmin(c, first=False):
-        e = view("E%d" % (c % 2), 0, 64)
-        tt(view("M") if first else e, e, view("HK", 64 * c, 64 * c + 64), A_.min)
-
-    def dmax(c, first=False):
-        tt(view("M"), view("CB", 256, 320) if first else view("E%d" % (c % 2), 0, 64), view("M"), A_.max)
-
-    def fold(nm):
-        tt(view("fa", 0, 32), view(nm, 0, 32), view(nm, 32, 64), A_.max)
-        tt(view("fb"), view("fa", 0, 16), view("fa", 16, 32), A_.max)
-
-    def row_p(t):
-        s_, U, pc = state("MC", t)
-        for k in range(16):
-            mm(view("CB", 320, 336), view("Ib"), view("PR", 16 * k, 16 * k + 16), k == 0)
-        o = view("CB", 256, 320)
-        mm(o, view("I2k"), view("C511"))
-        mm(o, view("F25"), view("ONE", 0, 64))
-        mm(o, view("Ikm"), pc)
-        mm(o, view("N32k"), U)
-        for k in range(4):
-            mm(o, view("Ib"), view("PR", 64 * k, 64 * k + 64), False, k == 3)
-
-    def open_groups(t):
-        s_, U, pc = state("MC", t)
-        for d in range(8):
-            o = view("DB", 16 * d, 16 * d + 16)
-            mm(o, mat("SH", d), view("hp"), d == 0)
-            mm(o, view("NI"), view("hp"))
-        mm(view("RG", 0, 256), view("NI"), view("XK"), True)
-        mm(view("RG", 0, 256), view("I32"), view("T1"))
-        spread("RG", 0, "Ib", pc)
-
-    def finish_steps(t):
-        sn, Un, pn_ = state("CO", t)
-
-        def backwards():
-            acti(view("Pv"), view("Pf"), view("RVP"))
-            mm(view("ZB", 256, 512), view("F16"), view("ONE"), True)
-            spread("ZB", 256, "N2k", Un, stop=True)
-            tt(view("yb"), view("Pf"), view("ZB", 256, 512), A_.subtract)
-
-        def pick():
-            tt(view("yo"), view("ZB", 256, 512), view("yb"), A_.max)
-            acti(view("TA"), view("yo"), view("DUP2"))
-
-        def small():
-            tt(view("sp", 16, 32), first16(pn_), view("y1"), A_.add)
-            for i in range(16):
-                mm(view("CB", i, 512, 16, parts=8), view("Ib", i, 128, 16), view("sp"), i == 0, i == 15)
-            act(view("so", parts=8), view("CB", parts=8))
-            store("y", T.ys[:], view("so", 0, 256, parts=8), "oy")
-            store("y", T.yp[:], view("so", 256, 512, parts=8), "oy")
-
-        def names():
-            turn32(view("TB"), view("TA"))
-            acti(view("yl"), view("TB"), view("UN2"))
-            store("s", T.yn[:], view("yl"), "oz")
-
-        return [backwards, lambda: ts(view("y1"), first16(Un), -8.0, A_.mult, 15.5, A_.add),
-                lambda: tt(view("ZB", 256, 512), view("Pv"), view("ZB", 256, 512), A_.min),
-                lambda: cp(view("sp", 0, 16), first16(sn)), pick, small, None, None, None, names]
-
-    arrive(0)
-    records(0)
-    rows_against_p(0)
-    for f in weave(site_steps(0, 0, 128), site_steps(0, 128, 256)):
-        f()
-
-    for t in range(HOPS):
-        last = t == HOPS - 1
-        s_, U, pc = state("MC", t)
-        sn, Un, pn_ = state("CO", t)
-        P = view("MP", 256 * t, 256 * t + 256)
-        grow(0)
-        grow(1)
-        vrows(2, 3)
-        if t < n - 1:
-            d = t + 1
-            order("g", [], [view("DR", 512, 768)])
-            send(T.cores[(rank + d) % n], view("AR", 512 * d, 512 * d + 512), view("AR", 0, 512), "ar%d" % d)
-        psub(0, "Q0")
-        tt(view("PR"), view("HI"), view("RG", 256, 512), A_.mult)
-        tt(view("HK"), view("HI"), view("CB", 0, 256), A_.add)
-        grow(8)
-        grow(9)
-        row_p(t)
-        vrows(4, 5)
-        absps(0, "Q0")
-        psub(8, "Q1")
-        absrows(2, 4)
-        cp(view("hp"), view("CB", 320, 336))
-        cp(view("hu"), view("CB", 320, 336))
-        vrows(6, 7)
-        dopen(0)
-        dsum(0)
-        dopen(1, 4, 8)
-        relurows(4, 8)
-        if t == 0:
-            late_constants()
-        grow(10)
-        grow(11)
-        vrows(12)
-        dmin(0, True)
-        dsum(1)
-        absps(8, "Q1")
-        psub(10, "Q0")
-        vrows(13)
-        dmax(0, True)
-        open_groups(t)
-        vrows(14)
-        dmin(1)
-        absps(10, "Q0")
-        dopen(2)
-        relurows(12, 14)
-        dmax(1)
-        vrows(15)
-        dsum(2)
-        dopen(3, 12, 14)
-        absrows(14, 15)
-        absrows(15, 16)
-        acti(view("old"), SITES, view("hu"))
-        dsum(3)
-        dmin(2)
-        dmax(2)
-        mm(view("E0", 256, 512), view("Ib"), view("AC"), True)
-        mm(view("E0", 256, 512), view("Ib"), view("old"), False, True)
-        act(view("n1"), view("E0", 256, 512), F_.Identity, 0.5, 127.75)
-        fold("M")
-        cpi(view("M4"), view("fb"), view("REP", 0, 4))
-        tt(view("M2"), view("E1", 0, 64), view("HK", 192, 256), A_.min)
-        fold("M2")
-        tti(view("w"), view("fb"), view("REP", 0, 4), view("M4"), A_.max)
-        w = view("w")
-        ts(view("hit"), w, 2 ** 21, A_.is_ge, 4096, A_.mult)
-        ts(view("hs"), w, 4095, A_.bitwise_and)
-        ts(view("hk"), w, 2.0 ** -17, A_.mult, 1023.5076, A_.add)
-        for d in range(8):
-            mm(view("DB", 16 * d, 16 * d + 16), mat("SH", d), view("hit", 0, 16))
-        spread("DB", 0, "Ib", view("hit"), stop=True, blocks=2)
-        spread("RG", 0, "Ihit", view("hit"))
-        spread("RG", 0, "NI", view("hk"), stop=True)
-        mm(view("Q1", 0, 16), view("Ib"), view("hp"), True)
-        mm(view("Q1", 0, 16), view("Ib"), view("hit", 0, 16))
-        ts(view("ub"), w, 16, A_.arith_shift_right, 1, A_.bitwise_and)
-        ts(view("pi"), w, 12, A_.arith_shift_right, 15, A_.bitwise_and)
-        tt(view("tt" if t else "tb"), s_, view("hs"), A_.mult)
-        ts(sn, view("hs"), -32, A_.add)
-        ts(Un, view("ub"), 2, A_.mult, -1, A_.add)
-        act(view("R2"), view("RG", 0, 256), F_.Relu, bias=1031.5)
-        act(view("nv"), view("n1"), F_.Identity, bias=-128.0)
-        ts(view("eq"), view("DB", 0, 128), 0, A_.is_equal)
-        if t:
-            ts(view("tb"), view("tt"), 25952 * t, A_.add)
-        ts(pn_, view("pi"), -7.5, A_.add)
-        if not last:
-            send(nxt, view("MC", 192 * t + 192, 192 * t + 384), view("CO", 192 * t, 192 * t + 192), "mc%d" % (t + 1))
-        for d in range(8):
-            mm(view("Q1", 0, 16), mat("RD", d), view("eq", 16 * d, 16 * d + 16), False, d == 7)
-        mm(view("Q0", 0, 256), view("I4k"), view("R2"), True, True)
-        mm(view("ZB", 0, 256), view("N4k"), view("R2"), True)
-        ts(view("bb"), view("tb"), 5, A_.arith_shift_right, 2047, A_.bitwise_and)
-        ts(view("fo", 0, 32, 2), view("Q1", 0, 16), col("dum"), A_.min)
-        cp(view("b16"), view("bb"))
-        spread("ZB", 0, "Ib", view("b16"), stop=True)
-        tt(view("tP"), P, view("Q0", 0, 256), A_.min)
-
-        def names():
-            if last:
-                tt(view("Pf"), view("tP"), view("ZB", 0, 256), A_.max)
-            else:
-                tt(view("PO", 256 * t, 256 * t + 256), view("tP"), view("ZB", 0, 256), A_.max)
-                send(nxt, view("MP", 256 * t + 256, 256 * t + 512), view("PO", 256 * t, 256 * t + 256), "mp%d" % (t + 1))
-
-        def limit():
-            mm(view("E1", 64, 80), view("Fm"), view("hit", 0, 16), True, True)
-            act(view("jk"), view("E1", 64, 80), F_.Identity, bias=2040.5 / 16, acc=col("mc"))
-            act(col("m1"), col("mc"), F_.Identity, bias=ROUND16)
-            act(col("m2"), col("m1"), F_.Identity, -1.0, ROUND16)
-            act(col("m3"), col("m2"), F_.Identity, bias=74.5)
-            act(view("TH"), view("ONE", 0, 128), F_.Identity, col("mc"), col("m3"))
-
-        fill = {0: [names]}
-        if last:
-            for k, f in enumerate(finish_steps(t)):
-                fill[k + 1] = [f] if f else []
-        else:
-            fill[0].append(limit)
-            extra = key_constants() if t == 0 else end_constants() if t == 1 else []
-            for k, f in enumerate(extra):
-                fill.setdefault(1 + k // 4, []).append(f)
-            fill.setdefault(5, []).append(lambda: arrive(t + 1))
-            fill[7] = [lambda: records(t + 1), lambda: rows_against_p(t + 1)]
-            for k, f in enumerate(weave(site_steps(t + 1, 0, 128), site_steps(t + 1, 128, 256))):
-                fill.setdefault(min(10 + k, 15), []).append(f)
-        for k in range(16):
-            j = 15 - k
-            scat(view("X"), view("fo", 2 * j, 2 * j + 1), view("nv", 16 * j, 16 * j + 16))
-            for f in fill.get(k, []):
-                f()
-
-    store("y", T.yx[:], SITES, "oy")
-    for q in ("v", "s", "p", "g"):
+            cnt[q] += 1
+            c["fn"]().then_inc(T.sem[QS[q]], 1)
+            note(q, c["outs"], c["ins"], (QS[q], cnt[q]))
+    for q in QS:
         need("g", (QS[q], cnt[q]))
-    for sem in outs:
-        need("g", (sem, outs[sem]))
-    for sem in ("lx", "la", "lr", "lk", "lz", "lp"):
-        need("g", (sem, 16))
-    need("g", ("snd", sent[0]))
+    for sem in total:
+        need("g", (sem, total[sem]))

@@ -7,14 +7,15 @@ NX = 2080
 BIG = 2.0 ** 22
 ROUND16 = 1.5 * 2 ** 27
 CHUNKS = ("RRRR", "SSSS", "SSAA", "RRAA")
-STEPS = "g0 g4 g1 g5 g2 g6 b0 g3 b4 g7 b2 d0 h0 ga g8 gb b6 d1 g9 gc p0 m0 ba gd x0 m1 b8 d2 ge x1 bc gf ae m2 af d3 x2 w3"
+STEPS = "g4 z0 z1 g5 g6 g0 z2 g1 g7 b4 g2 g3 b0 b6 z3 g8 h0 b2 ga g9 gb gc ba d0 m0 d1 p0 ge b8 gd gf ae m1 x0 af d2 bc x1 m2 d3 x2 w3"
 CYCLE, GATHER, SCATTER, COLUMN, WAKE, HOPLAT, LINK, DMALAT, DMABW = 1.04e-3, 1.3e-3, 3.15e-3, 0.48e-3, 0.19, 1.2, 100e3, 2.0, 200e3
 PASSES = 4
+BANKS = ("E0", "E1", "ZB", "E0")
 ORDER = []
 PIECES = ((256, 448, "ms"), (0, 128, "ma"), (128, 256, "mb"))
-EYES = {"NI": -1.0, "I16": 16.0, "I1184": 1184.0, "N128": -128.0, "I2k": 2048.0, "Ikp": 135168.0, "N1k": -1024.0,
-        "I32k": 32768.0, "N64k": -65536.0, "Ikm": 126976.0, "N32k": -32768.0, "I32": 32.0, "N32": -32.0, "I31": 31.0, "N31": -31.0, "N16": -16.0,
-        "I4k": 4096.0, "N4k": -4096.0, "N2k": -2048.0}
+EYES = {"NI": -1.0, "I16": 16.0, "I1184": 1184.0, "N128": -128.0, "I2k": 2048.0, "N2k": -2048.0, "N1k": -1024.0,
+        "I32k": 32768.0, "N32k": -32768.0, "N64k": -65536.0, "I4k": 4096.0, "N4k": -4096.0, "I1984": 1984.0, "N1984": -1984.0,
+        "I256k": 2.0 ** 18, "N256k": -2.0 ** 18}
 SIZE = {"float32": 4, "int32": 4, "bfloat16": 2, "float16": 2, "uint16": 2}
 
 SCRATCH = {}
@@ -42,9 +43,9 @@ for _n, _w, _d in (
     ("PI", 256, "int32"), ("SI", 256, "int32"), ("S16", 256, "float16"), ("KA", 1, "int32"), ("TA", 512, "float32"), ("TB", 512, "float32"),
     ("ia", 128, "int32"), ("ib", 128, "int32"), ("jm", 128, "int32"), ("jb", 128, "int32"), ("J", 128, "bfloat16"), ("i2", 32, "int32"),
     ("BM", 128, "bfloat16"), ("ONE", 256, "bfloat16"), ("F25", 128, "bfloat16"), ("Fm", 128, "bfloat16"), ("F16", 128, "bfloat16"),
-    ("CT", 256, "float16"), ("C511", 64, "float16"), ("C32k", 64, "bfloat16"), ("tg", 8, "float32"), ("te", 8, "float32"), ("tc", 8, "float32"),
+    ("Fhit", 128, "bfloat16"), ("Fmiss", 128, "bfloat16"), ("C32k", 64, "bfloat16"), ("tg", 8, "float32"), ("te", 8, "float32"), ("tc", 8, "float32"),
     ("LT", 16, "float16"), ("rk", 16, "float16"), ("KC", 16, "float32"), ("KTa", 256, "float16"), ("KTb", 256, "float16"), ("KD", 16, "float32"),
-    ("TH", 128, "bfloat16"), ("AC", 256, "bfloat16"), ("A1", 256, "bfloat16"), ("T2", 256, "bfloat16"), ("I1057", 128, "float16"), ("R2", 256, "bfloat16"),
+    ("TH", 128, "bfloat16"), ("AC", 256, "bfloat16"), ("A1", 256, "bfloat16"), ("T2", 256, "bfloat16"), ("I1057", 128, "float16"), ("oh", 256, "bfloat16"),
     ("Z", 256, "float32"), ("ZI", 256, "int32"), ("HI", 256, "int32"), ("H16", 256, "uint16"), ("HK", 256, "float32"), ("PR", 256, "float16"),
     ("hp", 16, "float16"), ("hit", 64, "bfloat16"), ("hn", 64, "bfloat16"), ("hk", 64, "float16"), ("b16", 64, "float16"), ("bw", 64, "bfloat16"),
     ("eq", 128, "bfloat16"), ("old", 256, "bfloat16"), ("n1", 256, "bfloat16"), ("nv", 256, "bfloat16"), ("tP", 256, "float32"),
@@ -282,14 +283,12 @@ def rank_program(g, core, T, topo):
     iota(view("w8i", parts=8), [[1, 144]], -15, -16)
     iota(view("ib"), [[-16, 8], [0, 16]], 0, 1)
     iota(view("idl", 0, 8), [[1, 8]], 1, 0)
-    for nm, c in (("ONE", 1.0), ("F25", 0.25), ("LE", 0.0), ("LP", 0.0), ("TH", 67.0), ("C32k", 32768.0), ("C511", 511.0),
-                  ("Fm", -1.0 / 4096), ("F16", 16.0)):
+    for nm, c in (("ONE", 1.0), ("F25", 0.25), ("LE", 0.0), ("LP", 0.0), ("TH", 67.0), ("C32k", 32768.0),
+                  ("Fm", -1.0 / 4096), ("F16", 16.0), ("FRG", 2048.0), ("FQ0", -2032.0)):
         ms(view(nm), c)
-    for nm, lo, hi in (("FRG", 65536.0, 480.0), ("FQ0", -65536.0, -448.0)):
-        ms(view(nm), hi)
-        ms(view(nm, parts=64), lo)
-    ms(view("CT", 0, 240), 1537.0)
-    ms(view("CT", 240, 256), 1505.0)
+    for nm, c in (("Fhit", 3072.0), ("Fmiss", 960.0)):
+        ms(view(nm), 32.5)
+        ms(view(nm, parts=64), c)
     ts(view("q15"), view("ip"), 15, A_.bitwise_and)
     ts(view("q31i"), view("ip"), 31, A_.bitwise_and)
     cp(col("p16"), col("q15"))
@@ -353,6 +352,17 @@ def rank_program(g, core, T, topo):
     ms(U0, 1.0)
     ms(p0, -7.5)
 
+    def site_numbers(t, half, step):
+        a, b = HALVES[half]
+        if step == 0:
+            tt(view("Z", a, b), part(state(t)[0], a, b), view("ZB", a, b), A_.mult)
+        elif step == 1:
+            tt(view("ZI", a, b), view("Z", a, b), view("ZB", 256 + a, 256 + b), A_.add)
+        elif step == 2:
+            ts(view("HI", a, b), view("ZI", a, b), 5, A_.arith_shift_right, 2047, A_.bitwise_and)
+        else:
+            cp(view("H16", a, b), view("HI", a, b))
+
     def sites(t):
         P, s_, U, pc = state(t)
         U1 = part(U, 0, 16)
@@ -371,11 +381,8 @@ def rank_program(g, core, T, topo):
         if t:
             for k in range(16):
                 mm(view("ZB", 256 + 16 * k, 272 + 16 * k), mat("DG", k), U1, False, k == 15)
-        for a, b in HALVES:
-            tt(view("Z", a, b), part(P, a, b), view("ZB", a, b), A_.mult)
-            tt(view("ZI", a, b), view("Z", a, b), view("ZB", 256 + a, 256 + b), A_.add)
-            ts(view("HI", a, b), view("ZI", a, b), 5, A_.arith_shift_right, 2047, A_.bitwise_and)
-            cp(view("H16", a, b), view("HI", a, b))
+        for step in range(4):
+            site_numbers(t, 0, step)
         if t:
             for k in range(16):
                 mm(view("Q1", 256 + 16 * k, 272 + 16 * k), mat("KI", k), U1, k == 0)
@@ -389,9 +396,9 @@ def rank_program(g, core, T, topo):
             act(view("T2"), view("A1"))
         act(view("RG", 256, 512), view("A1"), F_.Relu, -1.0, 1.0)
         in_turn()
-        mm(view("CB", 0, 256), view("I2k"), view("CT"), True)
-        mm(view("CB", 0, 256), view("F25"), view("ONE"))
-        spread("CB", 0, "Ikp", pc)
+        mm(view("CB", 0, 256), view("Fhit"), view("ONE"), True)
+        mm(view("CB", 240, 256), view("N64k"), view("ONE", 0, 16))
+        spread("CB", 0, "I4k", pc)
         spread("CB", 0, "I32k", U)
         mm(view("CB", 240, 256), view("N64k"), U1)
         mm(view("CB", 0, 256), view("N1k"), view("A1"))
@@ -404,27 +411,26 @@ def rank_program(g, core, T, topo):
         tt(view("HK"), view("HI"), view("CB", 0, 256), A_.add)
         in_turn()
         for k in range(16):
-            mm(view("CB", 320, 336), view("Ib"), view("PR", 16 * k, 16 * k + 16), k == 0)
-        o = view("CB", 256, 320)
-        mm(o, view("I2k"), view("C511"))
-        mm(o, view("F25"), view("ONE", 0, 64))
-        mm(o, view("Ikm"), pc)
-        mm(o, view("N32k"), U)
-        for k in range(4):
-            mm(o, view("Ib"), view("PR", 64 * k, 64 * k + 64), False, k == 3)
+            mm(view("CB", 320, 336), view("Ib"), view("PR", 16 * k, 16 * k + 16), k == 0, k == 15)
 
-    def pairs_open():
+    def pairs_open(t):
+        P, s_, U, pc = state(t)
         cp(view("hp"), view("CB", 320, 336))
         in_turn()
         cp(view("hu"), view("CB", 320, 336))
         in_turn()
+        act(view("hf"), view("CB", 320, 336))
+        o = view("CB", 256, 272)
+        mm(o, view("Fmiss"), view("ONE", 0, 16), True)
+        mm(o, view("N4k"), part(pc, 0, 16))
+        mm(o, view("N32k"), part(U, 0, 16))
+        mm(o, view("Ib"), view("hp"), False, True)
         for d in range(8):
             o = view("DB", 16 * d, 16 * d + 16)
             mm(o, mat("SH", d), view("hp"), d == 0)
             mm(o, view("NI"), view("hp"))
 
     def columns_open():
-        cp(view("hf"), view("CB", 320, 336))
         acti(view("HE"), view("hf"), view("EV", 0, 8))
         tti(view("HO"), view("hf"), view("OD", 0, 8), view("SEL"), A_.mult)
         mm(view("CB", 384, 512), view("BM"), view("HO"), True)
@@ -468,7 +474,7 @@ def rank_program(g, core, T, topo):
         def decide(c):
             kinds, k0 = CHUNKS[c], len("".join(CHUNKS[:c]))
             rows = len(kinds)
-            bank = "E%d" % (c % 2)
+            bank = BANKS[c]
             e = view(bank, 0, 16 * rows)
             mm(e, view("TH"), view("C32k", 0, 16 * rows), True)
             if "R" in kinds:
@@ -480,12 +486,13 @@ def rank_program(g, core, T, topo):
 
         def choose(c, step):
             k0, rows = len("".join(CHUNKS[:c])), len(CHUNKS[c])
-            e, hk = view("E%d" % (c % 2), 0, 16 * rows), view("HK", 16 * k0, 16 * (k0 + rows))
+            e, hk = view(BANKS[c], 0, 16 * rows), view("HK", 16 * k0, 16 * (k0 + rows))
             if step == "m":
                 tt(e if c else view("M"), e, hk, A_.min)
                 in_turn()
             elif step == "x":
-                tt(view("M", 0, 16 * rows), e if c else view("CB", 256, 320), view("M", 0, 16 * rows), A_.max)
+                m = view("M", 0, 16 * rows if c else 16)
+                tt(m, e if c else view("CB", 256, 272), m, A_.max)
                 in_turn()
             else:
                 fold(view("fb"), "M", 4)
@@ -505,10 +512,13 @@ def rank_program(g, core, T, topo):
                 decide(k)
             elif step[0] in "mxw":
                 choose(k, step[0])
+            elif step[0] == "z":
+                site_numbers(t, 1, k)
+                in_turn()
             elif step[0] == "h":
                 row_p(t)
             elif step[0] == "p":
-                pairs_open()
+                pairs_open(t)
             else:
                 size(k, " abc".index(step[0]))
 
@@ -518,7 +528,7 @@ def rank_program(g, core, T, topo):
         mm(view("E1", 256, 512), view("Ib"), view("old"), False, True)
         act(view("n1"), view("E1", 256, 512), F_.Identity, 0.5, 127.75)
         act(view("nv"), view("n1"), F_.Identity, bias=-128.0)
-        ts(view("hit"), view("W"), 2 ** 21, A_.is_ge, 4096, A_.mult)
+        ts(view("hit"), view("W"), 2 ** 17, A_.is_ge, 4096, A_.mult)
         columns_open()
         for k in range(4):
             mm(view("CB", 384 + 32 * k, 416 + 32 * k), view("Ib"), view("hit", 0, 64, 2), False, k == 3)
@@ -555,11 +565,10 @@ def rank_program(g, core, T, topo):
         w = view("W")
         for bank, sign in (("RG", "IN"), ("Q0", "NI")):
             mm(view(bank, 0, 256), view("F" + bank), view("ONE"), True)
-            spread(bank, 0, sign[0] + "4k", pc)
-            mm(view(bank, 0, 256), view(sign[0] + "32"), view("A1"))
-            mm(view(bank, 0, 256), view(sign[1] + "31"), view("T2"))
+            mm(view(bank, 0, 256), view(sign[0] + "2k"), view("A1"))
+            mm(view(bank, 0, 256), view(sign[1] + "1984"), view("T2"))
         ts(view("hs"), w, 4095, A_.bitwise_and)
-        ts(view("hk"), w, 2.0 ** -17, A_.mult, 1023.5076, A_.add)
+        ts(view("hk"), w, 2.0 ** -17, A_.mult, 1.0, A_.max)
         ts(view("ub"), w, 16, A_.arith_shift_right, 1, A_.bitwise_and)
         ts(view("pi"), w, 12, A_.arith_shift_right, 15, A_.bitwise_and)
         tt(view("sh" if t == 0 else "sf"), s_, view("hs"), A_.mult)
@@ -570,8 +579,7 @@ def rank_program(g, core, T, topo):
         ts(pn_, view("pi"), -7.5, A_.add)
         ts(view("bq"), view("sh"), 5, A_.arith_shift_right, 2047, A_.bitwise_and)
         for bank, sign in (("RG", "IN"), ("Q0", "NI")):
-            spread(bank, 0, sign[1] + "4k", view("hk"))
-            spread(bank, 0, sign[0] + "16", view("hit"), stop=True)
+            spread(bank, 0, sign[1] + "256k", view("hk"), stop=True)
         for a, b in HALVES:
             tt(view("RG", a, b), part(P, a, b), view("RG", a, b), A_.min)
             for x in range(a, b, 64):

@@ -1,3 +1,5 @@
+import math
+from concourse.bass import DstId, RemoteDMATransfer
 from concourse.mybir import AluOpType, ActivationFunctionType
 
 A_ = AluOpType
@@ -6,16 +8,27 @@ HOPS = 7
 NX = 2080
 BIG = 2.0 ** 22
 ROUND16 = 1.5 * 2 ** 27
-CHUNKS = ("RRRR", "SSSS", "SSAA", "RRAA")
-STEPS = "g4 z0 z1 g5 g6 g0 z2 g1 g7 b4 g2 g3 b0 b6 z3 g8 h0 b2 ga g9 gb gc ba d0 m0 d1 p0 ge b8 gd gf ae m1 x0 af d2 bc x1 m2 d3 x2 w3"
+CHUNKS = ("RRRRR", "SSSS", "SSAA", "AAA")
+STEPS = "h0 g0 g1 b0 g2 g3 b2 g4 a4 d0 p0 m0 f0 g5 g6 b5 g7 g8 b7 d1 m1 x1 g9 ga b9 gb gc bb d2 m2 x2 gd ad ge ae gf af d3 f1 f2 w3"
 CYCLE, GATHER, SCATTER, COLUMN, WAKE, HOPLAT, LINK, DMALAT, DMABW = 1.04e-3, 1.3e-3, 3.15e-3, 0.48e-3, 0.19, 1.2, 100e3, 2.0, 200e3
 PASSES = 4
 BANKS = ("E0", "E1", "ZB", "E0")
-ORDER = []
-PIECES = ((256, 448, "ms"), (0, 128, "ma"), (128, 256, "mb"))
-EYES = {"NI": -1.0, "I16": 16.0, "I1184": 1184.0, "N128": -128.0, "I2k": 2048.0, "N2k": -2048.0, "N1k": -1024.0,
-        "I32k": 32768.0, "N32k": -32768.0, "N64k": -65536.0, "I4k": 4096.0, "N4k": -4096.0, "I1984": 1984.0, "N1984": -1984.0,
-        "I256k": 2.0 ** 18, "N256k": -2.0 ** 18}
+ORDER, SPAN = [], []
+TURNS = ("hs ex sf sh bq eq Pa t1 t0 Pb t3 t2 fo fp low hr x7 s x6 x5 x4 x3 AO y0 u0 x2 y1 z0 x1 y2 u1 z1 x0 y3 u2 z2 g4 z3 HK u3 PR "
+         "g2 g0 g3 gc g1 hu hp a4 b0 gb b2 gf gd ge m0 m1 f0 m2 x1m HO x2m f1 w0 f2 w1 w2 "
+         "G4 mis U jk F l1 l2 l3 R1 SA AC TH SB g5 g6 ga g8 g7 b5 g9 b7 hf b9 bb Mm af ad ae old n1 HE "
+         "ms ma mb "
+         "Pa. eq. Pb. ex. fo. jk. keysZB 32. pay. SA. sUZB s. keysE1 sUE1 payF. A5. HK. A7. D2. PR. D1. X5. hp. mask. X7. A9. X9. D0. Mm. "
+         "E1. E0. E2. pairs. D3. E3. n1. HE. maskb. hq.")
+LAST = ("ex hs sf eq sh low bq hr fp fo s Pb x7 Pa x6 t3 t0 t2 x5 t1 Nb x4 Na y1 x3 bb ba x2 mb ma x1 ob oa x0 sq sp Tb Ta "
+        "G4 F U Vb Va Db Da so Un eq. ex. fo. Pb. Pa. U. sp.")
+PIECES = ((0, 128, "ma"), (128, 256, "mb"))
+EYES = {"I1184": 1184.0, "I4k": 4096.0, "N64k": -2.0 ** 16, "I260k": 2.0 ** 18 + 4096, "I16": 16.0, "N4k": -4096.0, "NI": -1.0,
+        "N128": -128.0, "N32k": -32768.0, "I34k": 34816.0, "Ih": 0.5, "Nh": -0.5}
+MASKS = ("RG", "Q0")
+FOLD = True
+FO = GO = 192
+RO = GO // 2 + 8
 SIZE = {"float32": 4, "int32": 4, "bfloat16": 2, "float16": 2, "uint16": 2}
 
 SCRATCH = {}
@@ -29,29 +42,28 @@ def _shared(buf, dtype, width, names):
 
 
 _shared("eyes", "bfloat16", 128, ["Ib"] + list(EYES))
-_shared("cols", "float32", 4, ("p16", "q31", "c3", "p256", "dum", "dun", "p8", "ph", "kf", "mc", "m1", "m2", "m3"))
-_shared("i64", "int32", 64, ("hs", "pi", "ub", "sh", "bq"))
-_shared("f64", "float32", 64, ("M", "M2", "M4", "fa", "sf"))
+_shared("cols", "float32", 4, ("p16", "q31", "c3", "p256", "dum", "dun", "pa", "pb", "p128", "p112", "kf", "mc", "m1", "m2", "m3"))
+_shared("i64", "int32", 64, ("hs", "low", "hr", "sh", "bq"))
+_shared("f64", "float32", 64, ("M2", "fa", "sf"))
 _shared("u32", "uint16", 32, ("DUP1", "DUP2", "fo"))
-_shared("u16", "uint16", 16, ("UN1", "UN2", "RVP", "RK", "RVK", "AO", "hu", "REP", "EV", "OD"))
-_shared("i16", "int32", 16, ("inn", "ip", "q15", "q31i", "q7", "idl"))
+_shared("u16", "uint16", 16, ("UN1", "UN2", "RVP", "AO", "hu", "REP", "EV", "OD"))
+_shared("i16", "int32", 16, ("inn", "ip", "q15", "q31i", "q7"))
+_shared("f8", "float32", 8, ("td", "te", "tg", "tc"))
+_shared("b128", "bfloat16", 128, ("BM", "BM16", "D", "LOW", "J", "i8", "SEL", "F25", "F32", "Fhit", "Fmiss", "TH", "eq", "ex"))
 for _n, _w, _d in (
     ("X", NX, "bfloat16"), ("AR", 2048, "bfloat16"), ("DR", 4096, "bfloat16"), ("DA", 4096, "bfloat16"),
     ("LE", 144, "bfloat16"), ("LP", 144, "bfloat16"), ("KI", 2048, "bfloat16"), ("DG", 2048, "float16"),
-    ("SH", 1024, "bfloat16"), ("RD", 1024, "bfloat16"), ("W8", 144, "bfloat16"), ("w8i", 144, "int32"),
-    ("ST", 448 * HOPS, "float16"), ("CO", 448 * HOPS, "float16"), ("W", 64, "int32"),
+    ("SH", 1024, "bfloat16"), ("RD", 1024, "bfloat16"), ("W8", 144, "bfloat16"),
+    ("ST", 320 * (HOPS + 1), "float16"), ("CO", 256 * HOPS, "float16"), ("CP", 256 * HOPS, "float16"), ("W", 16 * HOPS, "int32"),
+    ("WL", 16 * HOPS, "int32"), ("M", 96, "float32"),
     ("PI", 256, "int32"), ("SI", 256, "int32"), ("S16", 256, "float16"), ("KA", 1, "int32"), ("TA", 512, "float32"), ("TB", 512, "float32"),
-    ("ia", 128, "int32"), ("ib", 128, "int32"), ("jm", 128, "int32"), ("jb", 128, "int32"), ("J", 128, "bfloat16"), ("i2", 32, "int32"),
-    ("BM", 128, "bfloat16"), ("ONE", 256, "bfloat16"), ("F25", 128, "bfloat16"), ("Fm", 128, "bfloat16"), ("F16", 128, "bfloat16"),
-    ("Fhit", 128, "bfloat16"), ("Fmiss", 128, "bfloat16"), ("C32k", 64, "bfloat16"), ("tg", 8, "float32"), ("te", 8, "float32"), ("tc", 8, "float32"),
-    ("LT", 16, "float16"), ("rk", 16, "float16"), ("KC", 16, "float32"), ("KTa", 256, "float16"), ("KTb", 256, "float16"), ("KD", 16, "float32"),
-    ("TH", 128, "bfloat16"), ("AC", 256, "bfloat16"), ("A1", 256, "bfloat16"), ("T2", 256, "bfloat16"), ("I1057", 128, "float16"), ("oh", 256, "bfloat16"),
+    ("i2", 32, "int32"), ("ONE", 256, "bfloat16"), ("C32k", 96, "bfloat16"),
+    ("LT", 16, "float16"), ("rk", 16, "float16"), ("s1", 16, "float32"), ("KTa", 256, "float16"), ("KTb", 256, "float16"), ("KD", 16, "float32"),
+    ("AC", 256, "bfloat16"), ("R1", 256, "bfloat16"), ("SA", 256, "bfloat16"), ("SB", 256, "bfloat16"),
     ("Z", 256, "float32"), ("ZI", 256, "int32"), ("HI", 256, "int32"), ("H16", 256, "uint16"), ("HK", 256, "float32"), ("PR", 256, "float16"),
-    ("hp", 16, "float16"), ("hit", 64, "bfloat16"), ("hn", 64, "bfloat16"), ("hk", 64, "float16"), ("b16", 64, "float16"), ("bw", 64, "bfloat16"),
-    ("eq", 128, "bfloat16"), ("old", 256, "bfloat16"), ("n1", 256, "bfloat16"), ("nv", 256, "bfloat16"), ("tP", 256, "float32"),
-    ("hf", 16, "float32"), ("HE", 128, "float32"), ("HO", 128, "float16"), ("ex", 128, "bfloat16"), ("SEL", 128, "bfloat16"),
-    ("i8", 128, "int32"), ("FRG", 128, "bfloat16"), ("FQ0", 128, "bfloat16"),
-    ("jk", 16, "float32"), ("fb", 16, "float32"), ("fc", 16, "float32"),
+    ("hp", 16, "float16"), ("G4", 64, "bfloat16"), ("mis", 16, "bfloat16"), ("C128", 32, "bfloat16"), ("UF", 128 * (HOPS + 1), "bfloat16"),
+    ("old", 256, "bfloat16"), ("n1", 256, "bfloat16"), ("tP", 256, "float32"),
+    ("hf", 16, "float32"), ("HE", 128, "float32"), ("HO", 128, "float16"), ("jk", 16, "float32"),
     ("Pf", 256, "float32"), ("Pv", 256, "float32"), ("yb", 256, "float32"), ("yo", 256, "float32"), ("yl", 256, "float32"),
     ("y1", 16, "float32"), ("sp", 32, "float16"), ("so", 512, "float32"),
 ):
@@ -64,18 +76,13 @@ SEMAPHORES = (["qv", "qs", "qp", "qg", "snd", "lx", "la", "lr", "lk", "lz", "lp"
               + [m + str(t) for m in ("ma", "mb", "ms") for t in range(HOPS - 1)] + ["ar%d" % d for d in (1, 2, 3)])
 
 
-def plan(calls):
-    n = len(calls)
+def needs(calls):
     pre = [dict() for _ in calls]
     log, bank, sender = {}, {}, {}
     for k, c in enumerate(calls):
         def after(j, wait=True):
             gap = calls[j]["done"] + WAKE if wait else 0.0
             pre[k][j] = max(pre[k].get(j, 0.0), gap)
-        if c["kind"] == "gather":
-            if c["q"] in sender:
-                pre[k][sender[c["q"]]] = calls[sender[c["q"]]]["hold"]
-            sender[c["q"]] = k
         if c["kind"] == "send":
             sender[c["sem"]] = k
         if c["kind"] == "land":
@@ -98,6 +105,16 @@ def plan(calls):
             for _, nm, a, b in vs:
                 keep = [e for e in log.get(nm, []) if not (wr and a <= e[0] and e[1] <= b)]
                 log[nm] = keep + [(a, b, wr, k)]
+    return pre
+
+
+def plan(calls, pre):
+    n = len(calls)
+    place = {nm: x for x, nm in enumerate(["first"] + TURNS.split() + [x + "!" for x in LAST.split()])}
+    for q in "vsgp":
+        named = sorted((c["name"][0], place[c["name"][1]], k) for k, c in enumerate(calls) if c["q"] == q and c["name"] and c["name"][1] in place)
+        for (_, _, j), (_, _, k) in zip(named, named[1:]):
+            pre[k][j] = max(pre[k].get(j, 0.0), calls[j]["hold"])
     hold, queue = [c["hold"] for c in calls], [c["q"] for c in calls]
     tail = [c["done"] - c["hold"] for c in calls]
     ahead, back = [[] for _ in calls], [[] for _ in calls]
@@ -138,9 +155,15 @@ def plan(calls):
                     head.pop(queue[j], None)
         return out, [start[k] + hold[k] for k in range(n)]
 
-    rest = [0.0] * n
-    for k in range(n - 1, -1, -1):
+    rest, left = [0.0] * n, [len(a) for a in ahead]
+    todo = [k for k in range(n) if not left[k]]
+    for k in todo:
         rest[k] = max([calls[k]["done"]] + [max(gap, hold[k]) + rest[j] for j, gap in ahead[k]])
+        for j, _ in back[k]:
+            left[j] -= 1
+            if not left[j]:
+                todo.append(j)
+    assert len(todo) == n
     best = None
     for _ in range(PASSES):
         out, end = run(ahead, [0.0] * n, rest)
@@ -148,6 +171,7 @@ def plan(calls):
         if best is None or span < best[0]:
             best = (span, out)
         rest = run(back, tail, end)[1]
+    SPAN[:] = [best[0]]
     return best[1]
 
 
@@ -159,14 +183,14 @@ def rank_program(g, core, T, topo):
     nxt, prv = T.cores[(rank + 1) % n], T.cores[(rank - 1) % n]
     Q = {"v": g.vector, "s": g.scalar, "p": g.tensor, "g": g, "y": g.sync}
     QS = {"v": "qv", "s": "qs", "p": "qp", "g": "qg"}
-    calls = []
+    calls, names, block, turn = [], [], [None], [0]
 
-    def view(name, a=0, b=None, st=1, parts=128):
+    def view(name, a=0, b=None, st=1, parts=128, p0=0):
         if name in PART:
             name, o, w = PART[name]
             a, b = o + a, o + (w if b is None else b)
         b = SCRATCH[name][1][1] if b is None else b
-        ap = T[name][0:parts, a:b] if st == 1 else T[name][0:parts, a:b:st]
+        ap = T[name][p0:p0 + parts, a:b] if st == 1 else T[name][p0:p0 + parts, a:b:st]
         return (ap, name, a, b)
 
     def col(name):
@@ -179,7 +203,20 @@ def rank_program(g, core, T, topo):
         return v[0].shape[0] * width(v) * SIZE[SCRATCH[v[1]][2]]
 
     def call(q, fn, outs, ins, hold, done=None, kind="compute", sem=None, count=0):
-        calls.append(dict(q=q, fn=fn, outs=outs, ins=ins, hold=hold, done=hold if done is None else done, kind=kind, sem=sem, count=count))
+        name = (turn[0], names.pop(0)) if names and q in "vsg" else (turn[0], block[0]) if q == "p" else None
+        if turn[0] < 0:
+            name = (-1, "first")
+        if turn[0] == HOPS and name:
+            name = (HOPS, "%s!" % name[1])
+        calls.append(dict(q=q, fn=fn, outs=outs, ins=ins, hold=hold, done=hold if done is None else done, kind=kind, sem=sem, count=count,
+                          name=name))
+
+    def named(text):
+        assert not names
+        names.extend(text.split())
+
+    def tensor(name):
+        block[0] = name
 
     def vcost(o, a):
         half = SIZE[SCRATCH[a[1]][2]] == 2 and SIZE[SCRATCH[o[1]][2]] == 2
@@ -207,8 +244,23 @@ def rank_program(g, core, T, topo):
     def cpi(o, win, off):
         call("v", lambda: g.vector.tensor_copy(o[0], win[0].indirect(off[0])), [o], [win, off], 0.05 + GATHER * width(o))
 
-    def scat(win, off, a):
-        call("v", lambda: g.vector.tensor_copy(win[0].indirect(off[0]), a[0]), [win], [off, a], 0.05 + SCATTER * width(a))
+    def tsi(o, win, off, s1, op0, s2=None, op1=None):
+        more = () if op1 is None else (op1,)
+        call("v", lambda: g.vector.tensor_scalar(o[0], win[0].indirect(off[0]), s1, s2, op0, *more), [o], [win, off], 0.05 + GATHER * width(o))
+
+    def scat(win, off, a, b):
+        call("v", lambda: g.vector.tensor_tensor(win[0].indirect(off[0]), a[0], b[0], A_.add), [win], [off, a, b], 0.05 + SCATTER * width(a))
+
+    def pieces(total):
+        left, out = total / 32, []
+        for k in range(4):
+            unit = 2.0 ** (math.frexp(left)[1] - 8)
+            out.append(round(left / unit) * unit)
+            left -= out[-1]
+        return out
+
+    def select(o, a, pattern, op, fill, base=0, step=1):
+        call("g", lambda: g.affine_select(o[0], a[0], pattern, op, fill, base, step), [o], [a], 0.17 + 2 * CYCLE * width(o))
 
     def turn32(o, a):
         call("v", lambda: g.vector.transpose(o[0], a[0]), [o], [a], vcost(o, a))
@@ -225,8 +277,8 @@ def rank_program(g, core, T, topo):
             call("s", lambda: g.scalar.activation(o[0], a[0], f, bias=bi, scale=sc, accum_out=acc[0]), [o, acc], [a] + cs,
                  0.2 + CYCLE * width(a))
 
-    def acti(o, win, off):
-        call("s", lambda: g.scalar.activation(o[0], win[0].indirect(off[0]), F_.Copy), [o], [win, off], 0.065 + GATHER * width(o))
+    def acti(o, win, off, f=F_.Copy, scale=1.0, bias=0.0):
+        call("s", lambda: g.scalar.activation(o[0], win[0].indirect(off[0]), f, bias=bias, scale=scale), [o], [win, off], 0.065 + GATHER * width(o))
 
     def mm(o, l, r, start=False, stop=False):
         call("p", lambda: g.tensor.matmul(o[0], l[0], r[0], start, stop), [o], [l, r], COLUMN * max(min(64, width(l)), width(r)))
@@ -244,21 +296,25 @@ def rank_program(g, core, T, topo):
     def store(q, out, a, sem):
         call(q, lambda: Q[q].dma_start(out, a[0]), [], [a], 0.05, DMALAT + nbytes(a) / DMABW, "dma", sem, 16)
 
-    def send(d, o, a, sem, also=()):
+    def send(d, o, a, sem, also=(), other=None):
         dst, src = T.cores[(rank + d) % n], T.cores[(rank - d) % n]
         rid, pid = topo.addr(dst, core)
-        call("g", lambda: g.remote_dma(o[0], a[0], T.sem[sem], T.sem.snd, pid, rid, topo.mask(core, dst)), [], [a] + list(also),
-             0.4, 0.4 + HOPLAT + nbytes(a) / LINK, "send", sem, len(topo.engines(core, dst)))
+        if other is None:
+            f = lambda: g.remote_dma(o[0], a[0], T.sem[sem], T.sem.snd, pid, rid, topo.mask(core, dst))
+        else:
+            also = [other]
+            f = lambda: g.remote_dma_fused([RemoteDMATransfer(dst_ids=[DstId(rid=rid, pnc=pid)], dma_engine_mask=topo.mask(core, dst),
+                                                              remote_sem=T.sem[sem], srcs=[a[0], other[0]], dsts=[o[0]], alu_op=2)],
+                                           local_sem=T.sem.snd)
+        call("g", f, [], [a] + list(also), 0.4, 0.4 + HOPLAT + nbytes(a) / LINK, "send", sem, len(topo.engines(core, dst)))
         call("rem", None, [o], [], 0.0, 0.0, "land", sem, len(topo.engines(src, core)))
-
-    def in_turn():
-        calls[-1]["kind"] = "gather"
 
     def mat(name, k):
         return view(name, 128 * k, 128 * k + 128)
 
-    def state(t, buf="ST"):
-        return [view(buf, 448 * t, 448 * t + 256)] + [view(buf, 448 * t + 256 + 64 * x, 448 * t + 320 + 64 * x) for x in range(3)]
+    def state(t):
+        return (view("ST", 320 * t, 320 * t + 256), view("ST", 320 * t + 256, 320 * t + 320),
+                view("UF", 128 * t, 128 * t + 64), view("UF", 128 * t + 64, 128 * t + 128))
 
     def record(t):
         return view("AC") if t else view("AR", 0, 256)
@@ -276,88 +332,124 @@ def rank_program(g, core, T, topo):
     load("y", SITES, T.x[:], "lx")
     load("s", view("AR", 256, 512), T.r0[:], "lr")
 
+    P0, s0_, U0, p0 = state(0)
+    ONES = view("ONE", 0, 128)
+    hit, miss = pieces(2 ** 17 + 4096 + 32 - FO * 4096 - RO * EYES["I260k"]), pieces((FO + 31) * 4096 + 32)
+    fills = [(view(nm), c) for nm, c in (("LE", 0.0), ("LP", 0.0), ("F25", 0.25), ("TH", 67.0))]
+    for k, (nm, c) in enumerate((("C32k", 32768.0), ("C128", -128.0), (U0, 1.0), (p0, FO + 16.0))):
+        fills += [(view("Fhit", parts=32, p0=32 * k), hit[k]), (view("Fmiss", parts=32, p0=32 * k), miss[k]), (view(nm) if k < 2 else nm, c)]
+    fills += [(view("F32"), 32.0)]
+
+    def fill(count):
+        for _ in range(count):
+            ms(*fills.pop(0))
+
+    turn[0] = -1
+    ms(view("ONE"), 1.0)
     iota(view("ip"), [[0, 16]], 0, 1)
     iota(view("i2"), [[1, 16], [0, 2]], 0, 0)
     iota(view("inn"), [[1, 16]], 0, 0)
-    iota(view("ia"), [[1, 128]], 0, -1)
-    iota(view("w8i", parts=8), [[1, 144]], -15, -16)
-    iota(view("ib"), [[-16, 8], [0, 16]], 0, 1)
-    iota(view("idl", 0, 8), [[1, 8]], 1, 0)
-    for nm, c in (("ONE", 1.0), ("F25", 0.25), ("LE", 0.0), ("LP", 0.0), ("TH", 67.0), ("C32k", 32768.0),
-                  ("Fm", -1.0 / 4096), ("F16", 16.0), ("FRG", 2048.0), ("FQ0", -2032.0)):
-        ms(view(nm), c)
-    for nm, c in (("Fhit", 3072.0), ("Fmiss", 960.0)):
-        ms(view(nm), 32.5)
-        ms(view(nm, parts=64), c)
+    select(view("Ib"), ONES, [[-1, 128]], A_.is_equal, 0.0)
+    select(view("BM"), ONES, [[-16, 8], [0, 16]], A_.is_ge, 0.0)
+    select(view("W8", parts=8), view("ONE", 0, 144, parts=8), [[1, 144]], A_.is_equal, 0.0, -15, -16)
+    select(view("BM"), view("BM"), [[16, 8], [0, 16]], A_.is_ge, 0.0, 15, -1)
+    iota(view("R1"), [[1, 16], [0, 16]], RO, 0)
+    iota(view("D"), [[1, 128]], 0, -1)
+    select(view("LOW"), ONES, [[-1, 128]], A_.is_gt, 0.0)
+    iota(view("i8"), [[1, 16], [0, 8]], 0, 0)
+    iota(view("td"), [[1, 8]], 1, 0)
+    iota(view("te"), [[-1, 8]], 15, 0)
+    fill(3)
     ts(view("q15"), view("ip"), 15, A_.bitwise_and)
     ts(view("q31i"), view("ip"), 31, A_.bitwise_and)
+    fill(2)
     cp(col("p16"), col("q15"))
     cp(col("q31"), col("q31i"))
+    cp(view("REP"), view("q15"))
+    fill(1)
     ts(col("c3"), col("p16"), 31, A_.mult, col("q31"), A_.add)
-    ts(col("p256"), col("p16"), 16, A_.mult)
-    ts(col("dum"), col("p16"), 2048, A_.add)
-    ts(col("dun"), col("p16"), 2064, A_.add)
+    ts(view("DUP1"), view("i2"), 16, A_.mult, col("p16"), A_.add)
+    ts(col("pa"), col("p16"), RO, A_.add)
+    fill(1)
+    ts(view("UN1"), view("inn"), col("c3"), A_.add)
+    fill(len(fills) - 1)
+    cp(view("S16", parts=8), view("SI", parts=8))
+    cp(col("kf"), view("KA"))
+    for i in range(16):
+        mm(view("E0", 0, 16), view("W8", 15 - i, 143 - i, parts=8), view("S16", i, 256, 16, parts=8), i == 0, i == 15)
+    for nm in EYES:
+        act(view(nm), view("Ib"), scale=EYES[nm])
+        if nm == "NI":
+            act(view("BM16"), view("BM"), scale=16.0)
+            act(view("LE", 15, 143, 16), view("BM", 0, 128, 16), scale=-BIG)
+            act(view("LP", 15, 143, 16), view("BM", 0, 128, 16), scale=BIG)
+        if nm == "NI":
+            acti(view("TA", 256, 512), view("PI"), view("DUP1", 16, 32))
+            act(view("s1"), view("E0", 0, 16))
+    cpi(view("TA", 0, 256), view("PI"), view("DUP1", 0, 16))
+    ts(view("KTa"), view("R1"), col("pa"), A_.is_equal, col("kf"), A_.mult)
+    turn32(view("TB", 0, 256), view("TA", 0, 256))
+    cpi(s0_, view("s1"), view("REP", 0, 4))
+    turn32(view("TB", 256, 512), view("TA", 256, 512))
+    for a, b in HALVES:
+        cpi(part(P0, a, b), view("TB"), view("UN1", a // 16, b // 16))
+    mm(view("RG", 0, 128), view("Ib"), view("D"), True)
+    mm(view("RG", 0, 128), view("I16"), view("LOW"))
+    mm(view("RG", 0, 128), view("N4k"), view("BM"), False, True)
+    act(view("J"), view("RG", 0, 128), F_.Identity, bias=4096.0)
+    for k in range(8):
+        act(mat("KI", k), view("Ib"), scale=k + 0.5)
+    turn[0] = 0
+    fill(len(fills))
     ts(view("q7"), view("ip"), 7, A_.bitwise_and)
     ts(view("EV"), view("q7"), 2, A_.mult)
     ts(view("OD"), view("q7"), 2, A_.mult, 1, A_.add)
-    iota(view("i8"), [[1, 16], [0, 8]], 0, 0)
-    ts(view("SEL"), view("i8"), col("p16"), A_.is_equal)
-    ts(view("DUP1"), view("i2"), 16, A_.mult, col("p16"), A_.add)
-    ts(view("UN1"), view("inn"), col("c3"), A_.add)
-    ts(view("DUP2"), view("i2"), col("p256"), A_.add)
+    for nm, m, c in (("pb", -1, RO + 15), ("dum", 1, 2048), ("dun", 1, 2064), ("p128", 1, 128), ("p112", 1, 112), ("p256", 16, 0)):
+        ts(col(nm), col("p16"), m, A_.mult, c, A_.add)
     ts(view("UN2"), view("inn"), 32, A_.mult, col("q31"), A_.add)
-    cp(view("RK"), view("inn"))
-    ts(view("RVK"), view("inn"), -1, A_.mult, 15, A_.add)
-    ts(view("RVP"), view("RVK"), 16, A_.mult, col("p16"), A_.add)
-    cp(view("REP"), view("q15"))
-    ts(view("LT"), view("inn"), 16, A_.mult, col("p16"), A_.add)
-    ts(view("LT"), view("LT"), 128, A_.add)
-    ts(view("Ib"), view("ia"), 0, A_.is_equal)
-    for nm in EYES:
-        act(view(nm), view("Ib"), scale=EYES[nm])
-    ts(view("I1057"), view("Ib"), 1057, A_.mult)
-    for k in range(16):
-        act(mat("KI", k), view("Ib"), scale=7.5 - k)
-    ts(view("W8", parts=8), view("w8i", parts=8), 0, A_.is_equal)
-    ts(view("jb"), view("ib"), -16, A_.bitwise_and)
-    ts(view("BM"), view("jb"), 0, A_.is_equal)
-    ts(view("LE", 15, 143, 16), view("BM", 0, 128, 16), -BIG, A_.mult)
-    ts(view("LP", 15, 143, 16), view("BM", 0, 128, 16), BIG, A_.mult)
-    ts(view("jm"), view("ia"), 15, A_.bitwise_and)
-    tt(view("J"), view("jm"), view("jb"), A_.add)
-    ts(view("tg"), view("idl", 0, 8), col("p16"), A_.is_gt)
-    ts(view("te"), view("idl", 0, 8), -1, A_.mult, 16, A_.add)
+    ts(view("LT"), view("inn"), 16, A_.mult, col("p128"), A_.add)
+    ts(view("RVP"), view("inn"), -16, A_.mult, col("p112"), A_.add)
+    ts(view("DUP2"), view("i2"), col("p256"), A_.add)
+    def differences(d):
+        two = view("SH", 128 * d, 128 * d + 256)
+        for x in (d, d + 1):
+            ts(mat("SH", x), view("J"), x + 1, A_.is_equal)
+        select(two, two, [[0, 2], [-1, 128]], A_.not_equal, -1.0)
+
+    ts(view("SEL"), view("i8"), col("p16"), A_.is_equal)
+    ts(view("tg"), view("td"), col("p16"), A_.is_gt)
     tt(view("tc"), view("tg"), view("te"), A_.mult)
     for d in range(1, 9):
-        ts(mat("SH", d - 1), view("J"), d, A_.is_equal)
         ts(mat("RD", d - 1), view("J"), view("tc", d - 1, d), A_.is_equal, 4096, A_.mult)
-    cp(col("kf"), view("KA"))
-    ts(view("rk"), view("inn"), col("p16"), A_.is_equal, col("kf"), A_.mult)
-    mm(view("Q1", 0, 16), view("BM"), view("rk"), True, True)
-    cp(view("KC"), view("Q1", 0, 16))
-    cpi(view("KTa"), view("KC"), view("RK"))
-    cpi(view("KTb"), view("KC"), view("RVK"))
-    tt(view("KD"), view("KTa", 0, 256, 16), view("KTb", 0, 256, 16), A_.subtract)
+    ts(view("KTb"), view("R1"), col("pb"), A_.is_equal, col("kf"), A_.mult)
+    tt(view("rk"), view("KTa", 0, 256, 16), view("KTb", 0, 256, 16), A_.subtract)
+    mm(view("DB", 0, 16), view("BM"), view("rk"), True, True)
+    act(view("KD"), view("DB", 0, 16))
     for k in range(16):
         ts(mat("DG", k), view("I16"), view("KD", k, k + 1), A_.mult)
-    P0, s0_, U0, p0 = state(0)
-    cpi(view("TA"), view("PI"), view("DUP1"))
-    turn32(view("TB"), view("TA"))
-    cpi(P0, view("TB"), view("UN1"))
-    cp(view("S16", parts=8), view("SI", parts=8))
-    for i in range(16):
-        mm(view("E0", 0, 16), view("W8", 15 - i, 143 - i, parts=8), view("S16", i, 256, 16, parts=8), i == 0, i == 15)
-    for k in range(4):
-        cp(part(s0_, 16 * k, 16 * k + 16), view("E0", 0, 16))
-    ms(U0, 1.0)
-    ms(p0, -7.5)
+    for k in range(8, 16):
+        act(mat("KI", k), view("Ib"), scale=k + 0.5)
+
+    def choice(t):
+        return view("W", 16 * t, 16 * t + 16)
+
+    def unpack(t, w):
+        _, s_, U, F = state(t)
+        named("low hr U F s")
+        low, wide = view("low", 0, 16), 4 if t == HOPS else 1
+        ts(low, w, 2 ** 17 - 1, A_.bitwise_and)
+        tsi(view("hr"), w, view("REP", 0, 4), 4095, A_.bitwise_and)
+        acti(part(U, 0, 16 * wide), low, view("REP", 0, wide), F_.Sign, bias=0.5 - 2 ** 16)
+        acti(F, low, view("REP", 0, 4), F_.Identity, 2.0 ** -12, FO - 0.25)
+        ts(s_, view("hr"), -32, A_.add)
 
     def site_numbers(t, half, step):
-        a, b = HALVES[half]
+        a, b = ((0, 64), (64, 128), (128, 256))[half]
+        named("uyz"[half] + str(step))
         if step == 0:
-            tt(view("Z", a, b), part(state(t)[0], a, b), view("ZB", a, b), A_.mult)
+            tt(view("Z", a, b), part(state(t)[0], a, b), view("E0", 256 + a, 256 + b), A_.mult)
         elif step == 1:
-            tt(view("ZI", a, b), view("Z", a, b), view("ZB", 256 + a, 256 + b), A_.add)
+            tt(view("ZI", a, b), view("Z", a, b), view("E1" if a >= 128 else "ZB", a, b), A_.add)
         elif step == 2:
             ts(view("HI", a, b), view("ZI", a, b), 5, A_.arith_shift_right, 2047, A_.bitwise_and)
         else:
@@ -368,80 +460,98 @@ def rank_program(g, core, T, topo):
         U1 = part(U, 0, 16)
         d = t % n
         if t:
-            mm(view("E1", 128, 144), view("Ib"), view("LT"), True)
-            mm(view("E1", 128, 144), view("N128"), U1, False, True)
-            cp(view("AO"), view("E1", 128, 144))
+            unpack(t, view("WL", 16 * t, 16 * t + 16))
+        tensor("32.")
+        mm(view("E0", 256, 512), view("F25"), view("ONE"), True)
+        tensor("s.")
+        spread("E0", 256, "Ib", s_, stop=True)
+        for bank, (a, b) in zip(("ZB", "E1"), HALVES):
+            tensor("keys" + bank)
+            mm(view(bank, a, b), view("BM16"), view("KTa", a, b), True)
+            mm(view(bank, a, b), view("BM16"), view("KTb" if t else "KTa", a, b))
+            if t and not a:
+                mm(view("ZB", 128, 144), view("Ib"), view("LT"))
+            tensor("sU" + bank)
+            if t and not a:
+                mm(view("ZB", 128, 144), view("N128"), U1)
+            for x in (a, a + 64):
+                mm(view(bank, x, x + 64), view("I1184"), s_, False, not t and x > a)
+            for x in range(a, b if t else a, 16):
+                mm(view(bank, x, x + 16), mat("DG", x // 16), U1, False, x == b - 16)
+        if t:
+            named("AO AC")
+            cp(view("AO"), view("ZB", 128, 144))
             acti(record(t), view("AR", 512 * d, 512 * d + 512), view("AO"))
-            in_turn()
-        mm(view("ZB", 0, 256), view("F25"), view("ONE"), True)
-        mm(view("ZB", 256, 512), view("I16"), view("KTa"))
-        mm(view("ZB", 256, 512), view("I16"), view("KTb" if t else "KTa"))
-        spread("ZB", 0, "Ib", s_)
-        spread("ZB", 256, "I1184", s_, stop=not t)
-        if t:
-            for k in range(16):
-                mm(view("ZB", 256 + 16 * k, 272 + 16 * k), mat("DG", k), U1, False, k == 15)
+        turn[0] -= not t
         for step in range(4):
-            site_numbers(t, 0, step)
+            if not t:
+                differences(2 * step)
+            for piece in range(3):
+                site_numbers(t, piece, step)
+        turn[0] += not t
         if t:
+            tensor("SA.")
             for k in range(16):
                 mm(view("Q1", 256 + 16 * k, 272 + 16 * k), mat("KI", k), U1, k == 0)
-            spread("Q1", 256, "Ib", pc, stop=True)
-            act(view("A1"), view("Q1", 256, 512), F_.Abs, 4096.0)
-            in_turn()
-            act(view("T2"), view("Q1", 256, 512), F_.Relu, -4096.0)
-            in_turn()
-        else:
-            iota(view("A1"), [[4096, 16], [0, 16]], 0, 0)
-            act(view("T2"), view("A1"))
-        act(view("RG", 256, 512), view("A1"), F_.Relu, -1.0, 1.0)
-        in_turn()
+            spread("Q1", 256, "NI", pc, stop=True)
+            for nm, f, c in (("SA", F_.Sign, 0.5), ("SB", F_.Sign, -0.5), ("R1", F_.Identity, RO)):
+                named(nm)
+                act(view(nm), view("Q1", 256, 512), f, bias=FO + 15.5 + c)
+            tensor("PR.")
+            mm(view("DB", 256, 512), view("Ih"), view("SA"), True)
+            mm(view("DB", 256, 512), view("Nh"), view("SB"), False, True)
+        tensor("pay.")
         mm(view("CB", 0, 256), view("Fhit"), view("ONE"), True)
         mm(view("CB", 240, 256), view("N64k"), view("ONE", 0, 16))
+        tensor("payF.")
         spread("CB", 0, "I4k", pc)
-        spread("CB", 0, "I32k", U)
         mm(view("CB", 240, 256), view("N64k"), U1)
-        mm(view("CB", 0, 256), view("N1k"), view("A1"))
-        mm(view("CB", 0, 256), view("I1057"), view("T2"), False, True)
+        tensor("HK.")
+        mm(view("CB", 0, 256), view("I260k"), view("R1"), False, True)
+        tensor("mask.")
+        masks(t, 0)
+
+    def masks(t, half):
+        a, b = HALVES[half]
+        for x, r, s in ((0, "I4k", "N32k"), (128, "N4k", "I34k")):
+            mm(view(MASKS[half], x, x + 128), view(r), view("R1", a, b), not x)
+            mm(view(MASKS[half], x, x + 128), view(s), view("SA" if t else "ONE", a, b))
 
     def row_p(t):
-        P, s_, U, pc = state(t)
-        tt(view("PR"), view("HI"), view("RG", 256, 512), A_.mult)
-        in_turn()
+        named("PR HK" if t else "HK")
+        if t:
+            tt(view("PR"), view("HI"), view("DB", 256, 512), A_.mult)
         tt(view("HK"), view("HI"), view("CB", 0, 256), A_.add)
-        in_turn()
-        for k in range(16):
-            mm(view("CB", 320, 336), view("Ib"), view("PR", 16 * k, 16 * k + 16), k == 0, k == 15)
+        tensor("hp.")
+        for k in range(16 if t else 0):
+            mm(view("CB", 272, 288), view("Ib"), view("PR", 16 * k, 16 * k + 16), k == 0, k == 15)
 
     def pairs_open(t):
         P, s_, U, pc = state(t)
-        cp(view("hp"), view("CB", 320, 336))
-        in_turn()
-        cp(view("hu"), view("CB", 320, 336))
-        in_turn()
-        act(view("hf"), view("CB", 320, 336))
+        hp = view("CB", 272, 288) if t else view("HI", 0, 16)
+        named("hp hu hf Mm HO HE" if t else "hp Mm HO HE")
+        cp(view("hp"), hp)
+        if t:
+            cp(view("hu"), hp)
+            act(view("hf"), hp)
         o = view("CB", 256, 272)
+        tensor("Mm.")
         mm(o, view("Fmiss"), view("ONE", 0, 16), True)
         mm(o, view("N4k"), part(pc, 0, 16))
-        mm(o, view("N32k"), part(U, 0, 16))
         mm(o, view("Ib"), view("hp"), False, True)
+        act(view("M", 80, 96), o)
+        tensor("pairs.")
         for d in range(8):
-            o = view("DB", 16 * d, 16 * d + 16)
-            mm(o, mat("SH", d), view("hp"), d == 0)
-            mm(o, view("NI"), view("hp"))
-
-    def columns_open():
-        acti(view("HE"), view("hf"), view("EV", 0, 8))
-        tti(view("HO"), view("hf"), view("OD", 0, 8), view("SEL"), A_.mult)
-        mm(view("CB", 384, 512), view("BM"), view("HO"), True)
-
-    def fold(o, nm, rows):
-        if rows == 4:
-            a = 32 * (nm == "M")
-            tt(view("fa", a, a + 32), view(nm, 0, 32), view(nm, 32, 64), A_.max)
-            tt(o, view("fa", a, a + 16), view("fa", a + 16, a + 32), A_.max)
-        else:
-            tt(o, view(nm, 0, 16), view(nm, 16, 32), A_.max)
+            mm(view("DB", 16 * d, 16 * d + 16), mat("SH", d), view("hp"), d == 0)
+        tti(view("HO"), view("hf") if t else hp, view("OD", 0, 8), view("SEL"), A_.mult)
+        o = view("CB", 384, 512)
+        tensor("HE.")
+        mm(o, view("Fmiss"), view("ONE", 0, 128), True)
+        for k in range(4):
+            mm(part(o, 32 * k, 32 * k + 32), view("N4k"), view(pc[1], pc[2], pc[3], 2))
+        mm(view("CB", 288, 352), view("Ib"), s_)
+        mm(o, view("BM"), view("HO"), False, True)
+        act(view("HE"), o)
 
     def distances(t):
         kind, pairs = "".join(CHUNKS), [0]
@@ -455,32 +565,34 @@ def rank_program(g, core, T, topo):
                 acti(span("DR", k), SITES, off)
             else:
                 tti(span("DR", k), SITES, off, record(t), A_.subtract)
-            in_turn()
 
         def size(k, m):
             if kind[k] == "S":
                 q = "Q%d" % (pairs[0] % 2)
                 pairs[0] += 1
-                mm(view(q, 0, 256 * m), view("Ib"), span("DR", k, m), True)
+                tensor("A%x." % k)
                 for x in range(m):
-                    mm(view(q, 256 * x, 256 * x + 256), view("NI"), record(t), False, x == m - 1)
+                    mm(view(q, 256 * x, 256 * x + 256), view("NI"), record(t), x == 0)
+                tensor("X%x." % k)
+                mm(view(q, 0, 256 * m), view("Ib"), span("DR", k, m), False, True)
                 act(span("DA", k, m), view(q, 0, 256 * m), F_.Abs)
             elif kind[k] == "A":
                 act(span("DA", k, m), span("DR", k, m), F_.Abs)
             else:
                 ts(span("DA", k, m), span("DR", k, m), 0.0, A_.max, 2.0, A_.mult)
-            in_turn()
 
         def decide(c):
             kinds, k0 = CHUNKS[c], len("".join(CHUNKS[:c]))
             rows = len(kinds)
             bank = BANKS[c]
             e = view(bank, 0, 16 * rows)
+            tensor("D%d." % c)
             mm(e, view("TH"), view("C32k", 0, 16 * rows), True)
             if "R" in kinds:
                 a, b = kinds.index("R"), kinds.rindex("R") + 1
                 for i in range(16):
                     mm(view(bank, 16 * a, 16 * b), view("LP", 15 - i, 143 - i), view("DR", 256 * (k0 + a) + i, 256 * (k0 + b), 16))
+            tensor("E%d." % c)
             for i in range(16):
                 mm(e, view("LE", 15 - i, 143 - i), view("DA", 256 * k0 + i, 256 * (k0 + rows), 16), False, i == 15)
 
@@ -488,33 +600,38 @@ def rank_program(g, core, T, topo):
             k0, rows = len("".join(CHUNKS[:c])), len(CHUNKS[c])
             e, hk = view(BANKS[c], 0, 16 * rows), view("HK", 16 * k0, 16 * (k0 + rows))
             if step == "m":
-                tt(e if c else view("M"), e, hk, A_.min)
-                in_turn()
+                tt(e if c else view("M", 0, 16 * rows), e, hk, A_.min)
             elif step == "x":
-                m = view("M", 0, 16 * rows if c else 16)
-                tt(m, e if c else view("CB", 256, 272), m, A_.max)
-                in_turn()
+                tt(view("M", 0, 16 * rows), e, view("M", 0, 16 * rows), A_.max)
             else:
-                fold(view("fb"), "M", 4)
-                cpi(view("M4"), view("fb"), view("REP", 0, 4))
-                if rows == 1:
-                    tt(view("fc"), e, hk, A_.min)
-                else:
-                    tt(view("M2", 0, 16 * rows), e, hk, A_.min)
-                    fold(view("fc"), "M2", rows)
-                tti(view("W"), view("fc"), view("REP", 0, 4), view("M4"), A_.max)
+                tt(view("M2", 0, 16 * rows), e, hk, A_.min)
+                tt(view("fa", 0, 32), view("M2", 0, 32), view("M2", 32, 64), A_.max)
+                tt(choice(t), view("fa", 0, 16), view("fa", 16, 32), A_.max)
+
+        def fold(k):
+            if k == 0:
+                tt(view("M", 0, 32), view("M", 0, 32), view("M", 64, 96), A_.max)
+            elif k == 1 and len(CHUNKS[3]) == 1:
+                tt(view("M2", 16, 64), view("M", 0, 48), view("M", 48, 96), A_.max)
+            elif k == 1:
+                tt(view("fa" if len(CHUNKS[3]) == 3 else "M2", 32, 64), view("M", 0, 32), view("M", 32, 64), A_.max)
+            else:
+                tt(view("M2", 48, 64), view("fa", 32, 48), view("fa", 48, 64), A_.max)
 
         for step in STEPS.split():
             k = int(step[1], 16)
+            if step[0] in "gabcfm":
+                named(step)
+            elif step[0] in "xw":
+                named(step + "m" if step[0] == "x" else "w0 w1 w2")
             if step[0] == "g":
                 gather(k)
             elif step[0] == "d":
                 decide(k)
+            elif step[0] == "f":
+                fold(k)
             elif step[0] in "mxw":
                 choose(k, step[0])
-            elif step[0] == "z":
-                site_numbers(t, 1, k)
-                in_turn()
             elif step[0] == "h":
                 row_p(t)
             elif step[0] == "p":
@@ -523,84 +640,104 @@ def rank_program(g, core, T, topo):
                 size(k, " abc".index(step[0]))
 
     def writes(t):
-        acti(view("old"), SITES, view("hu"))
+        if t:
+            named("old")
+            acti(view("old"), SITES, view("hu"))
+        named("n1")
+        tensor("n1.")
         mm(view("E1", 256, 512), view("Ib"), record(t), True)
-        mm(view("E1", 256, 512), view("Ib"), view("old"), False, True)
+        if t:
+            mm(view("E1", 256, 512), view("Ib"), view("old"), False, True)
+        else:
+            mm(view("E1", 256, 512), view("Ib"), record(t))
+            mm(view("E1", 256, 512), view("Ib"), view("DR", 0, 256), False, True)
         act(view("n1"), view("E1", 256, 512), F_.Identity, 0.5, 127.75)
-        act(view("nv"), view("n1"), F_.Identity, bias=-128.0)
-        ts(view("hit"), view("W"), 2 ** 17, A_.is_ge, 4096, A_.mult)
-        columns_open()
-        for k in range(4):
-            mm(view("CB", 384 + 32 * k, 416 + 32 * k), view("Ib"), view("hit", 0, 64, 2), False, k == 3)
-        tt(view("ex"), view("CB", 384, 512), view("HE"), A_.is_equal)
-        for d in range(8):
-            mm(view("DB", 16 * d, 16 * d + 16), mat("SH", d), view("hit", 0, 16))
-        mm(view("DB", 0, 64), view("Ib"), view("hit"))
-        mm(view("DB", 64, 128), view("Ib"), view("hit"), False, True)
+        tensor("maskb.")
+        masks(t, 1)
+        tensor("hq.")
         mm(view("Q1", 0, 16), view("Ib"), view("hp"), True)
-        mm(view("Q1", 0, 16), view("Ib"), view("hit", 0, 16))
+        turn[0] += 1
+        named("G4 ex eq fo fp x7 x6 x5 x4 x3 x2 x1 x0")
+        acti(view("G4"), choice(t), view("REP", 0, 4), F_.Identity, 2.0 ** -5, (GO - 0.4925) * 4096)
+        tti(view("ex"), choice(t), view("EV", 0, 8), view("HE"), A_.is_equal)
+        tensor("eq.")
+        for d in range(8):
+            mm(view("DB", 16 * d, 16 * d + 16), mat("SH", d), view("G4", 0, 16), False, d == 7)
+        tensor("ex.")
+        mm(view("Q1", 0, 16), view("Ib"), view("G4", 0, 16))
         ts(view("eq"), view("DB", 0, 128), 0, A_.is_equal)
         for i in range(16):
             mm(view("Q1", 1, 16, 2), view("LP", 15 - i, 143 - i), view("ex", 8 * i, 8 * i + 8))
+        tensor("fo.")
         for d in range(8):
             mm(view("Q1", 0, 16), mat("RD", d), view("eq", 16 * d, 16 * d + 16), False, d == 7)
-        ts(view("fo", 0, 16, 2), view("Q1", 0, 16, 2), col("dum"), A_.min)
+        ts(view("fo", 0, 16, 2), view("Q1", 0, 16, 2), -4096 * GO, A_.add, col("dum"), A_.min)
         odd = (view("fo", 1, 16, 2)[0], "fp", 0, 16)
-        ts(odd, view("Q1", 1, 16, 2), col("dun"), A_.min)
+        ts(odd, view("Q1", 1, 16, 2), -4096 * GO, A_.add, col("dun"), A_.min)
         for j in range(14, -1, -2):
-            scat(view("X"), view("fo", j, j + 2), view("nv", 16 * j, 16 * j + 32))
+            scat(view("X"), view("fo", j, j + 2), view("n1", 16 * j, 16 * j + 32), view("C128"))
             calls[-1]["ins"].append(odd)
 
     def limit():
-        mm(view("E1", 64, 80), view("Fm"), view("hit", 0, 16), True, True)
-        act(view("jk"), view("E1", 64, 80), F_.Identity, bias=2040.5 / 16, acc=col("mc"))
+        named("mis jk l1 l2 l3 TH")
+        act(view("mis"), view("G4", 0, 16), F_.Relu, -1.0 / 4096, GO + 1.0)
+        tensor("jk.")
+        mm(view("E1", 64, 80), view("ONE", 0, 128), view("mis"), True, True)
+        act(view("jk"), view("E1", 64, 80), F_.Identity, bias=-7.5 / 16, acc=col("mc"))
         act(col("m1"), col("mc"), F_.Identity, bias=ROUND16)
         act(col("m2"), col("m1"), F_.Identity, -1.0, ROUND16)
         act(col("m3"), col("m2"), F_.Identity, bias=74.5)
         act(view("TH"), view("ONE", 0, 128), F_.Identity, col("mc"), col("m3"))
 
-    def become(t, names):
-        P, s_, U, pc = state(t)
-        _, sn, Un, pn_ = state(t, "CO")
-        w = view("W")
-        for bank, sign in (("RG", "IN"), ("Q0", "NI")):
-            mm(view(bank, 0, 256), view("F" + bank), view("ONE"), True)
-            mm(view(bank, 0, 256), view(sign[0] + "2k"), view("A1"))
-            mm(view(bank, 0, 256), view(sign[1] + "1984"), view("T2"))
-        ts(view("hs"), w, 4095, A_.bitwise_and)
-        ts(view("hk"), w, 2.0 ** -17, A_.mult, 1.0, A_.max)
-        ts(view("ub"), w, 16, A_.arith_shift_right, 1, A_.bitwise_and)
-        ts(view("pi"), w, 12, A_.arith_shift_right, 15, A_.bitwise_and)
-        tt(view("sh" if t == 0 else "sf"), s_, view("hs"), A_.mult)
+    def become(t, names_):
+        P = state(t)[0]
+        named("hs sf sh bq" if t else "hs sf bq")
+        tsi(view("hs"), choice(t), view("REP", 0, 4), 4095, A_.bitwise_and)
+        tt(view("sh" if t == 0 else "sf"), view("CB", 288, 352), view("hs"), A_.mult)
         if t:
             ts(view("sh"), view("sf"), 25952 * t, A_.add)
-        ts(sn, view("hs"), -32, A_.add)
-        ts(Un, view("ub"), 2, A_.mult, -1, A_.add)
-        ts(pn_, view("pi"), -7.5, A_.add)
         ts(view("bq"), view("sh"), 5, A_.arith_shift_right, 2047, A_.bitwise_and)
-        for bank, sign in (("RG", "IN"), ("Q0", "NI")):
-            spread(bank, 0, sign[1] + "256k", view("hk"), stop=True)
+        for bank, h in zip(MASKS, "ab"):
+            tensor("P%s." % h)
+            for x in range(0, 256, 64):
+                mm(view(bank, x, x + 64), view("Ih" if x >= 128 else "Nh"), view("G4"), False, x == 192)
+        tensor(None)
+        fold = FOLD and t < HOPS - 1
         for a, b in HALVES:
-            tt(view("RG", a, b), part(P, a, b), view("RG", a, b), A_.min)
+            named(("Pb t2 t3" if a else "Pa t0 t1") + ("" if fold else " Nb" if a else " Na"))
+            bank = MASKS[a // 128]
+            tt(part(names_, a, b) if fold else view(bank, 0, 128), part(P, a, b), view(bank, 0, 128), A_.min)
             for x in range(a, b, 64):
-                tt(view("tP", x, x + 64), view("bq"), view("Q0", x, x + 64), A_.min)
-            tt(part(names, a, b), view("tP", a, b), view("RG", a, b), A_.max)
+                tt(view("CP", 256 * t + x, 256 * t + x + 64) if fold else view("tP", x, x + 64), view("bq"), view(bank, 128 + x - a, 192 + x - a), A_.min)
+            if not fold:
+                tt(part(names_, a, b), view("tP", a, b), view(bank, 0, 128), A_.max)
 
     def finish():
-        _, sn, Un, pn_ = state(HOPS - 1, "CO")
-        acti(view("Pv"), view("Pf"), view("RVP"))
-        mm(view("ZB", 256, 512), view("F16"), view("ONE"), True)
-        spread("ZB", 256, "N2k", Un, stop=True)
-        tt(view("yb"), view("Pf"), view("ZB", 256, 512), A_.subtract)
-        tt(view("ZB", 256, 512), view("Pv"), view("ZB", 256, 512), A_.min)
-        tt(view("yo"), view("ZB", 256, 512), view("yb"), A_.max)
-        acti(view("TA"), view("yo"), view("DUP2"))
-        turn32(view("TB"), view("TA"))
+        unpack(HOPS, choice(HOPS - 1))
+        _, sn, Un, pn_ = state(HOPS)
+        tensor("U.")
+        mm(view("ZB", 256, 512), view("F32"), view("ONE"), True)
+        spread("ZB", 256, "N4k", Un, stop=True)
+        for (a, b), h in zip(HALVES, "ab"):
+            named("V%s b%s" % (h, h))
+            acti(view("Pv", 256 - b, 256 - a), view("Pf", a, b), view("RVP", 0, 8))
+            tt(view("yb", a, b), view("Pf", a, b), view("ZB", 256 + a, 256 + b), A_.subtract)
+        for (a, b), h in zip(HALVES, "ab"):
+            named("m%s o%s" % (h, h))
+            tt(view("ZB", 256 + a, 256 + b), view("Pv", a, b), view("ZB", 256 + a, 256 + b), A_.min)
+            tt(view("yo", a, b), view("ZB", 256 + a, 256 + b), view("yb", a, b), A_.max)
+        for a, h in zip((0, 256), "ab"):
+            named("D%s T%s" % (h, h))
+            acti(view("TA", a, a + 256), view("yo"), view("DUP2", a // 16, a // 16 + 16))
+            turn32(view("TB", a, a + 256), view("TA", a, a + 256))
+        named("Un")
         acti(view("yl"), view("TB"), view("UN2"))
         store("s", T.yn[:], view("yl"), "oz")
-        ts(view("y1"), part(Un, 0, 16), -8.0, A_.mult, 15.5, A_.add)
+        named("y1 sp sq so")
+        ts(view("y1"), part(Un, 0, 16), -16.0, A_.mult, -FO, A_.add)
         cp(view("sp", 0, 16), part(sn, 0, 16))
         tt(view("sp", 16, 32), part(pn_, 0, 16), view("y1"), A_.add)
+        tensor("sp.")
         for i in range(16):
             mm(view("CB", i, 512, 16, parts=8), view("Ib", i, 128, 16), view("sp"), i == 0, i == 15)
         act(view("so", parts=8), view("CB", parts=8))
@@ -616,9 +753,13 @@ def rank_program(g, core, T, topo):
         writes(t)
         if t < HOPS - 1:
             limit()
-            become(t, state(t, "CO")[0])
+            become(t, view("CO", 256 * t, 256 * t + 256))
+            named("ms")
+            send(1, view("WL", 16 * t + 16, 16 * t + 32), choice(t), "ms%d" % t)
             for a, b, sem in PIECES:
-                send(1, view("ST", 448 * t + 448 + a, 448 * t + 448 + b), view("CO", 448 * t + a, 448 * t + b), sem + str(t))
+                named(sem)
+                send(1, part(state(t + 1)[0], a, b), view("CO", 256 * t + a, 256 * t + b), sem + str(t),
+                     other=view("CP", 256 * t + a, 256 * t + b) if FOLD else None)
             sites(t + 1)
         else:
             become(t, view("Pf"))
@@ -656,7 +797,7 @@ def rank_program(g, core, T, topo):
                 d[(q, a, b, wr)] = ev
 
     if not ORDER:
-        ORDER.extend(plan(calls))
+        ORDER.extend(plan(calls, needs(calls)))
     for c in [calls[k] for k in ORDER]:
         q = c["q"]
         if c["kind"] == "land":

@@ -8,24 +8,25 @@ HOPS = 7
 NX = 2080
 BIG = 2.0 ** 22
 ROUND16 = 1.5 * 2 ** 27
-CHUNKS = ("RRRRR", "SSSS", "SSAA", "AAA")
-STEPS = "h0 g0 g1 b0 g2 g3 b2 g4 a4 d0 p0 m0 f0 g5 g6 b5 g7 g8 b7 d1 m1 x1 g9 ga b9 gb gc bb d2 m2 x2 gd ad ge ae gf af d3 f1 f2 w3"
+CHUNKS = ("RRRRR", "SSSS", "SSAA", "RAA")
+STEPS = "h0 G0 b0 G2 b2 g4 a4 d0 p0 m0 f0 G5 b5 G7 b7 d1 m1 x1 G9 b9 Gb bb d2 m2 x2 Gd ad ae gf af d3 w3"
 CYCLE, GATHER, SCATTER, COLUMN, WAKE, HOPLAT, LINK, DMALAT, DMABW = 1.04e-3, 1.3e-3, 3.15e-3, 0.48e-3, 0.19, 1.2, 100e3, 2.0, 200e3
+ACT = 0.06
+ONS = "HO h4"
 PASSES = 4
-BANKS = ("E0", "E1", "ZB", "E0")
+BANKS = ("E0", "E1", "ZB", "Q1")
 ORDER, SPAN = [], []
-TURNS = ("hs ex sf sh bq eq Pa t1 t0 Pb t3 t2 fo fp low hr x7 s x6 x5 x4 x3 AO y0 u0 x2 y1 z0 x1 y2 u1 z1 x0 y3 u2 z2 g4 z3 HK u3 PR "
-         "g2 g0 g3 gc g1 hu hp a4 b0 gb b2 gf gd ge m0 m1 f0 m2 x1m HO x2m f1 w0 f2 w1 w2 "
-         "G4 mis U jk F l1 l2 l3 R1 SA AC TH SB g5 g6 ga g8 g7 b5 g9 b7 hf b9 bb Mm af ad ae old n1 HE "
+TURNS = ("hs low sf ex bq Pa t1 t0 eq t2 t3 Pb fo x7 x6 x5 x4 x3 y0 u0 x2 z0 y1 x1 u1 y2 z1 x0 y3 z2 u2 g4 z3 u3 PR HK "
+         "G0 h4 G2 a4 b0 Gb hu b2 Gd gf m0 ad m1 f0 HO m2 x1m xa xb xc xd wa wb wc w2 "
+         "GW n1 mis jk l1 l2 l3 U s F sc AO TH AC R1 SA SB AD G5 G7 G9 b5 b7 hp b9 bb Mm ae af old HE "
          "ms ma mb "
-         "Pa. eq. Pb. ex. fo. jk. keysZB 32. pay. SA. sUZB s. keysE1 sUE1 payF. A5. HK. A7. D2. PR. D1. X5. hp. mask. X7. A9. X9. D0. Mm. "
-         "E1. E0. E2. pairs. D3. E3. n1. HE. maskb. hq.")
-LAST = ("ex hs sf eq sh low bq hr fp fo s Pb x7 Pa x6 t3 t0 t2 x5 t1 Nb x4 Na y1 x3 bb ba x2 mb ma x1 ob oa x0 sq sp Tb Ta "
-        "G4 F U Vb Va Db Da so Un eq. ex. fo. Pb. Pa. U. sp.")
+         "32. Pa. eq. jk. ex. fo. keysZB keysE1 pay. AO. SA. s. sUZB sUE1 payF. HK. mask. PR. A9. A5. D1. X5. A7. hp. X7. D2. h4. X9. D0. "
+         "E1. Mm. E0. E2. D3. E3. HE. pairs. hq. n1.")
+LAST = ("hs low ex sf eq bq y1 fo t1 x7 t2 Pa x6 t0 Pb x5 Na t3 x4 Nb x3 x2 sp sq x1 x0 Tb Ta Tc Td "
+        "GW F n1 U s Uo Db Da Dc Dd so Un eq. ex. fo. Pa. U. sp.")
 PIECES = ((0, 128, "ma"), (128, 256, "mb"))
 EYES = {"I1184": 1184.0, "I4k": 4096.0, "N64k": -2.0 ** 16, "I260k": 2.0 ** 18 + 4096, "I16": 16.0, "N4k": -4096.0, "NI": -1.0,
-        "N128": -128.0, "N32k": -32768.0, "I34k": 34816.0, "Ih": 0.5, "Nh": -0.5}
-MASKS = ("RG", "Q0")
+        "N128": -128.0, "N32k": -32768.0, "I34k": 34816.0, "Ih": 0.5, "Nh": -0.5, "N2": -2.0}
 FOLD = True
 FO = GO = 192
 RO = GO // 2 + 8
@@ -42,29 +43,31 @@ def _shared(buf, dtype, width, names):
 
 
 _shared("eyes", "bfloat16", 128, ["Ib"] + list(EYES))
-_shared("cols", "float32", 4, ("p16", "q31", "c3", "p256", "dum", "dun", "pa", "pb", "p128", "p112", "kf", "mc", "m1", "m2", "m3"))
-_shared("i64", "int32", 64, ("hs", "low", "hr", "sh", "bq"))
-_shared("f64", "float32", 64, ("M2", "fa", "sf"))
-_shared("u32", "uint16", 32, ("DUP1", "DUP2", "fo"))
-_shared("u16", "uint16", 16, ("UN1", "UN2", "RVP", "AO", "hu", "REP", "EV", "OD"))
+_shared("cols", "float32", 4, ("p16", "q31", "c3", "p256", "q287", "pa", "pb", "p128", "p240", "kf", "mc", "m1", "m2", "m3"))
+_shared("i64", "int32", 64, ("sh", "bq"))
+_shared("f64", "float32", 64, ("fa", "sf"))
+_shared("u32", "uint16", 32, ("DUP1", "fo"))
+_shared("u16", "uint16", 16, ("UN1", "UN2", "AO", "hu", "REP", "EV", "ODD", "R4"))
 _shared("i16", "int32", 16, ("inn", "ip", "q15", "q31i", "q7"))
 _shared("f8", "float32", 8, ("td", "te", "tg", "tc"))
-_shared("b128", "bfloat16", 128, ("BM", "BM16", "D", "LOW", "J", "i8", "SEL", "F25", "F32", "Fhit", "Fmiss", "TH", "eq", "ex"))
+_shared("b128", "bfloat16", 128, ("BM", "BM16", "D", "LOW", "J", "G8", "F25", "Fhit", "Fmiss", "TH", "eq", "ex"))
 for _n, _w, _d in (
     ("X", NX, "bfloat16"), ("AR", 2048, "bfloat16"), ("DR", 4096, "bfloat16"), ("DA", 4096, "bfloat16"),
     ("LE", 144, "bfloat16"), ("LP", 144, "bfloat16"), ("KI", 2048, "bfloat16"), ("DG", 2048, "float16"),
     ("SH", 1024, "bfloat16"), ("RD", 1024, "bfloat16"), ("W8", 144, "bfloat16"),
-    ("ST", 320 * (HOPS + 1), "float16"), ("CO", 256 * HOPS, "float16"), ("CP", 256 * HOPS, "float16"), ("W", 16 * HOPS, "int32"),
-    ("WL", 16 * HOPS, "int32"), ("M", 96, "float32"),
-    ("PI", 256, "int32"), ("SI", 256, "int32"), ("S16", 256, "float16"), ("KA", 1, "int32"), ("TA", 512, "float32"), ("TB", 512, "float32"),
+    ("ST", 320 * (HOPS + 1), "float16"), ("CO", 256 * HOPS, "float16"), ("CP", 256 * HOPS, "float16"), ("W", 112, "int32"), ("K3", 112, "bfloat16"),
+    ("CGO", 16, "bfloat16"), ("DUM", 16, "float32"),
+    ("WS", 48 * HOPS, "int32"), ("WL", 48 * HOPS, "int32"), ("M", 128, "float32"), ("M2", 112, "float32"),
+    ("PI", 256, "int32"), ("SI", 256, "int32"), ("S16", 256, "float16"), ("KA", 1, "int32"), ("TA", 1024, "float32"), ("TB", 1024, "float32"),
+    ("DUP2", 64, "uint16"), ("UNF", 16, "float16"),
     ("i2", 32, "int32"), ("ONE", 256, "bfloat16"), ("C32k", 96, "bfloat16"),
     ("LT", 16, "float16"), ("rk", 16, "float16"), ("s1", 16, "float32"), ("KTa", 256, "float16"), ("KTb", 256, "float16"), ("KD", 16, "float32"),
-    ("AC", 256, "bfloat16"), ("R1", 256, "bfloat16"), ("SA", 256, "bfloat16"), ("SB", 256, "bfloat16"),
+    ("AC", 512, "bfloat16"), ("R1", 256, "bfloat16"), ("SA", 256, "bfloat16"), ("SB", 256, "bfloat16"),
     ("Z", 256, "float32"), ("ZI", 256, "int32"), ("HI", 256, "int32"), ("H16", 256, "uint16"), ("HK", 256, "float32"), ("PR", 256, "float16"),
-    ("hp", 16, "float16"), ("G4", 64, "bfloat16"), ("mis", 16, "bfloat16"), ("C128", 32, "bfloat16"), ("UF", 128 * (HOPS + 1), "bfloat16"),
+    ("hp", 16, "float16"), ("h4", 64, "float16"), ("SC", 32 * HOPS, "float32"), ("G4", 64, "bfloat16"), ("mis", 16, "bfloat16"), ("C128", 32, "bfloat16"), ("UF", 128 * (HOPS + 1), "bfloat16"),
     ("old", 256, "bfloat16"), ("n1", 256, "bfloat16"), ("tP", 256, "float32"),
     ("hf", 16, "float32"), ("HE", 128, "float32"), ("HO", 128, "float16"), ("jk", 16, "float32"),
-    ("Pf", 256, "float32"), ("Pv", 256, "float32"), ("yb", 256, "float32"), ("yo", 256, "float32"), ("yl", 256, "float32"),
+    ("Pf", 256, "float32"), ("yl", 256, "float32"),
     ("y1", 16, "float32"), ("sp", 32, "float16"), ("so", 512, "float32"),
 ):
     SCRATCH[_n] = ("sbuf", [128, _w], _d)
@@ -272,7 +275,7 @@ def rank_program(g, core, T, topo):
         cs = [s for s in (scale, bias) if isinstance(s, tuple)]
         sc, bi = (s[0] if isinstance(s, tuple) else s for s in (scale, bias))
         if acc is None:
-            call("s", lambda: g.scalar.activation(o[0], a[0], f, bias=bi, scale=sc), [o], [a] + cs, 0.06 + CYCLE * width(a))
+            call("s", lambda: g.scalar.activation(o[0], a[0], f, bias=bi, scale=sc), [o], [a] + cs, ACT + CYCLE * width(a))
         else:
             call("s", lambda: g.scalar.activation(o[0], a[0], f, bias=bi, scale=sc, accum_out=acc[0]), [o, acc], [a] + cs,
                  0.2 + CYCLE * width(a))
@@ -317,7 +320,7 @@ def rank_program(g, core, T, topo):
                 view("UF", 128 * t, 128 * t + 64), view("UF", 128 * t + 64, 128 * t + 128))
 
     def record(t):
-        return view("AC") if t else view("AR", 0, 256)
+        return view("AC", 0, 256)
 
     def part(v, a, b):
         return view(v[1], v[2] + a, v[2] + b)
@@ -330,7 +333,7 @@ def rank_program(g, core, T, topo):
     load("s", view("KA"), T.kap[:], "lk")
     load("s", view("AR", 0, 256), T.a0[:], "la")
     load("y", SITES, T.x[:], "lx")
-    load("s", view("AR", 256, 512), T.r0[:], "lr")
+    load("y", view("AR", 256, 512), T.r0[:], "lr")
 
     P0, s0_, U0, p0 = state(0)
     ONES = view("ONE", 0, 128)
@@ -338,7 +341,6 @@ def rank_program(g, core, T, topo):
     fills = [(view(nm), c) for nm, c in (("LE", 0.0), ("LP", 0.0), ("F25", 0.25), ("TH", 67.0))]
     for k, (nm, c) in enumerate((("C32k", 32768.0), ("C128", -128.0), (U0, 1.0), (p0, FO + 16.0))):
         fills += [(view("Fhit", parts=32, p0=32 * k), hit[k]), (view("Fmiss", parts=32, p0=32 * k), miss[k]), (view(nm) if k < 2 else nm, c)]
-    fills += [(view("F32"), 32.0)]
 
     def fill(count):
         for _ in range(count):
@@ -356,9 +358,10 @@ def rank_program(g, core, T, topo):
     iota(view("R1"), [[1, 16], [0, 16]], RO, 0)
     iota(view("D"), [[1, 128]], 0, -1)
     select(view("LOW"), ONES, [[-1, 128]], A_.is_gt, 0.0)
-    iota(view("i8"), [[1, 16], [0, 8]], 0, 0)
     iota(view("td"), [[1, 8]], 1, 0)
     iota(view("te"), [[-1, 8]], 15, 0)
+    iota(view("SC", 1, 32 * HOPS, 2), [[25952, HOPS], [0, 16]], 0, 0)
+    iota(view("KI", 1280, 2048), [[2, 6], [0, 128]], 21, 0)
     fill(3)
     ts(view("q15"), view("ip"), 15, A_.bitwise_and)
     ts(view("q31i"), view("ip"), 31, A_.bitwise_and)
@@ -370,78 +373,103 @@ def rank_program(g, core, T, topo):
     ts(col("c3"), col("p16"), 31, A_.mult, col("q31"), A_.add)
     ts(view("DUP1"), view("i2"), 16, A_.mult, col("p16"), A_.add)
     ts(col("pa"), col("p16"), RO, A_.add)
+    ts(col("pb"), col("p16"), -1, A_.mult, RO + 15, A_.add)
     fill(1)
     ts(view("UN1"), view("inn"), col("c3"), A_.add)
-    fill(len(fills) - 1)
+    fill(len(fills))
     cp(view("S16", parts=8), view("SI", parts=8))
     cp(col("kf"), view("KA"))
     for i in range(16):
         mm(view("E0", 0, 16), view("W8", 15 - i, 143 - i, parts=8), view("S16", i, 256, 16, parts=8), i == 0, i == 15)
-    for nm in EYES:
+    eyes = list(EYES)
+    for nm in eyes[:7]:
         act(view(nm), view("Ib"), scale=EYES[nm])
-        if nm == "NI":
-            act(view("BM16"), view("BM"), scale=16.0)
-            act(view("LE", 15, 143, 16), view("BM", 0, 128, 16), scale=-BIG)
-            act(view("LP", 15, 143, 16), view("BM", 0, 128, 16), scale=BIG)
-        if nm == "NI":
-            acti(view("TA", 256, 512), view("PI"), view("DUP1", 16, 32))
-            act(view("s1"), view("E0", 0, 16))
+    act(view("BM16"), view("BM"), scale=16.0)
+    act(view("LE", 15, 143, 16), view("BM", 0, 128, 16), scale=-BIG)
+    act(view("LP", 15, 143, 16), view("BM", 0, 128, 16), scale=BIG)
+    acti(view("TA", 256, 512), view("PI"), view("DUP1", 16, 32))
+    act(view("s1"), view("E0", 0, 16))
+    act(view("AC", 0, 256), view("AR", 0, 256))
+    acti(s0_, view("s1"), view("REP", 0, 4))
+    act(view("AC", 256, 512), view("AR", 0, 256))
     cpi(view("TA", 0, 256), view("PI"), view("DUP1", 0, 16))
     ts(view("KTa"), view("R1"), col("pa"), A_.is_equal, col("kf"), A_.mult)
     turn32(view("TB", 0, 256), view("TA", 0, 256))
-    cpi(s0_, view("s1"), view("REP", 0, 4))
     turn32(view("TB", 256, 512), view("TA", 256, 512))
-    for a, b in HALVES:
-        cpi(part(P0, a, b), view("TB"), view("UN1", a // 16, b // 16))
+    ts(view("KTb"), view("R1"), col("pb"), A_.is_equal, col("kf"), A_.mult)
+    cpi(part(P0, 0, 128), view("TB", 0, 512), view("UN1", 0, 8))
+    tt(view("rk"), view("KTa", 0, 256, 16), view("KTb", 0, 256, 16), A_.subtract)
+    acti(part(P0, 128, 256), view("TB", 0, 512), view("UN1", 8, 16))
+    turn[0] = 0
     mm(view("RG", 0, 128), view("Ib"), view("D"), True)
     mm(view("RG", 0, 128), view("I16"), view("LOW"))
     mm(view("RG", 0, 128), view("N4k"), view("BM"), False, True)
+    mm(view("RG", 128, 256, parts=8), view("Ib", 0, 128, 16), view("BM"), True, True)
+    turn[0] = -1
     act(view("J"), view("RG", 0, 128), F_.Identity, bias=4096.0)
-    for k in range(8):
-        act(mat("KI", k), view("Ib"), scale=k + 0.5)
+    act(view("G8", parts=8), view("RG", 128, 256, parts=8))
+    for nm in eyes[7:]:
+        turn[0] = -(nm not in ("N128", "N2"))
+        act(view(nm), view("Ib"), scale=EYES[nm])
     turn[0] = 0
-    fill(len(fills))
+    ms(view("WS", 0, 48 * HOPS, 2), 0)
+    turn[0] = -1
+    act(view("SC", 0, 32, 2), view("s1"))
+    turn[0] = 0
+    ts(view("ODD"), view("q15"), 2, A_.mult, 1, A_.add)
     ts(view("q7"), view("ip"), 7, A_.bitwise_and)
-    ts(view("EV"), view("q7"), 2, A_.mult)
-    ts(view("OD"), view("q7"), 2, A_.mult, 1, A_.add)
-    for nm, m, c in (("pb", -1, RO + 15), ("dum", 1, 2048), ("dun", 1, 2064), ("p128", 1, 128), ("p112", 1, 112), ("p256", 16, 0)):
+    ts(view("EV"), view("q7"), 14, A_.mult, 6, A_.add)
+    ts(view("R4"), view("q15"), 7, A_.mult, 6, A_.add)
+    ms(view("K3"), 1.0)
+    ms(view("K3", 0, 112, 7), 0.0)
+    ms(view("CGO"), GO)
+    for nm, m, c in (("p128", 1, 128), ("p240", -16, 240), ("p256", 16, 0)):
         ts(col(nm), col("p16"), m, A_.mult, c, A_.add)
-    ts(view("UN2"), view("inn"), 32, A_.mult, col("q31"), A_.add)
+    iota(view("DUM"), [[0, 8], [16, 2]], 2048, 0)
+    ts(view("DUM"), view("DUM"), col("p16"), A_.add)
+    ts(col("q287"), col("q31"), 256, A_.add)
+    ts(view("UNF"), view("inn"), 32, A_.mult, col("q287"), A_.add)
     ts(view("LT"), view("inn"), 16, A_.mult, col("p128"), A_.add)
-    ts(view("RVP"), view("inn"), -16, A_.mult, col("p112"), A_.add)
-    ts(view("DUP2"), view("i2"), col("p256"), A_.add)
+    ts(view("DUP2", 0, 32), view("i2"), col("p256"), A_.add)
+    ts(view("DUP2", 32, 64), view("i2"), col("p240"), A_.add)
     def differences(d):
         two = view("SH", 128 * d, 128 * d + 256)
         for x in (d, d + 1):
             ts(mat("SH", x), view("J"), x + 1, A_.is_equal)
         select(two, two, [[0, 2], [-1, 128]], A_.not_equal, -1.0)
 
-    ts(view("SEL"), view("i8"), col("p16"), A_.is_equal)
     ts(view("tg"), view("td"), col("p16"), A_.is_gt)
     tt(view("tc"), view("tg"), view("te"), A_.mult)
     for d in range(1, 9):
         ts(mat("RD", d - 1), view("J"), view("tc", d - 1, d), A_.is_equal, 4096, A_.mult)
-    ts(view("KTb"), view("R1"), col("pb"), A_.is_equal, col("kf"), A_.mult)
-    tt(view("rk"), view("KTa", 0, 256, 16), view("KTb", 0, 256, 16), A_.subtract)
-    mm(view("DB", 0, 16), view("BM"), view("rk"), True, True)
-    act(view("KD"), view("DB", 0, 16))
-    for k in range(16):
-        ts(mat("DG", k), view("I16"), view("KD", k, k + 1), A_.mult)
-    for k in range(8, 16):
-        act(mat("KI", k), view("Ib"), scale=k + 0.5)
 
-    def choice(t):
-        return view("W", 16 * t, 16 * t + 16)
+    def key_matrices():
+        tensor(None)
+        mm(view("Q0", 0, 16), view("BM"), view("rk"), True, True)
+        named("old")
+        act(view("KD"), view("Q0", 0, 16))
+        for k in range(16):
+            ts(mat("DG", k), view("I16"), view("KD", k, k + 1), A_.mult)
+
+    for k in range(10):
+        act(mat("KI", k), view("Ib"), scale=2 * k + 1)
+    for k in (10, 13):
+        three = view("KI", 128 * k, 128 * k + 384)
+        select(three, three, [[0, 3], [-1, 128]], A_.is_equal, 0.0)
+
+    def slot(r):
+        return (view("M2", r, 112, 7)[0], "slot%d" % r, 0, 16)
 
     def unpack(t, w):
         _, s_, U, F = state(t)
-        named("low hr U F s")
-        low, wide = view("low", 0, 16), 4 if t == HOPS else 1
-        ts(low, w, 2 ** 17 - 1, A_.bitwise_and)
-        tsi(view("hr"), w, view("REP", 0, 4), 4095, A_.bitwise_and)
-        acti(part(U, 0, 16 * wide), low, view("REP", 0, wide), F_.Sign, bias=0.5 - 2 ** 16)
+        named("U F s")
+        low = part(w, 32, 48)
+        acti(part(U, 0, 16), low, view("REP", 0, 1), F_.Sign, bias=0.5 - 2 ** 16)
         acti(F, low, view("REP", 0, 4), F_.Identity, 2.0 ** -12, FO - 0.25)
-        ts(s_, view("hr"), -32, A_.add)
+        acti(s_, part(w, 0, 32), view("ODD", 0, 4), F_.Identity, bias=-32.0)
+        if t < HOPS:
+            named("sc")
+            act(view("SC", 32 * t, 32 * t + 32, 2), part(s_, 0, 16))
 
     def site_numbers(t, half, step):
         a, b = ((0, 64), (64, 128), (128, 256))[half]
@@ -453,14 +481,14 @@ def rank_program(g, core, T, topo):
         elif step == 2:
             ts(view("HI", a, b), view("ZI", a, b), 5, A_.arith_shift_right, 2047, A_.bitwise_and)
         else:
-            cp(view("H16", a, b), view("HI", a, b))
+            (act if t and "uyz"[half] + "3" in ONS else cp)(view("H16", a, b), view("HI", a, b))
 
     def sites(t):
         P, s_, U, pc = state(t)
         U1 = part(U, 0, 16)
         d = t % n
         if t:
-            unpack(t, view("WL", 16 * t, 16 * t + 16))
+            unpack(t, view("WL", 48 * t, 48 * t + 48))
         tensor("32.")
         mm(view("E0", 256, 512), view("F25"), view("ONE"), True)
         tensor("s.")
@@ -469,37 +497,38 @@ def rank_program(g, core, T, topo):
             tensor("keys" + bank)
             mm(view(bank, a, b), view("BM16"), view("KTa", a, b), True)
             mm(view(bank, a, b), view("BM16"), view("KTb" if t else "KTa", a, b))
-            if t and not a:
-                mm(view("ZB", 128, 144), view("Ib"), view("LT"))
             tensor("sU" + bank)
-            if t and not a:
-                mm(view("ZB", 128, 144), view("N128"), U1)
             for x in (a, a + 64):
                 mm(view(bank, x, x + 64), view("I1184"), s_, False, not t and x > a)
             for x in range(a, b if t else a, 16):
                 mm(view(bank, x, x + 16), mat("DG", x // 16), U1, False, x == b - 16)
         if t:
-            named("AO AC")
-            cp(view("AO"), view("ZB", 128, 144))
+            tensor("AO.")
+            mm(view("Q0", 0, 16), view("Ib"), view("LT"), True)
+            mm(view("Q0", 0, 16), view("N128"), U1, False, True)
+            named("AO AC AD")
+            act(view("AO"), view("Q0", 0, 16))
             acti(record(t), view("AR", 512 * d, 512 * d + 512), view("AO"))
+            act(view("AC", 256, 512), record(t))
         turn[0] -= not t
         for step in range(4):
-            if not t:
-                differences(2 * step)
             for piece in range(3):
                 site_numbers(t, piece, step)
         turn[0] += not t
+        for d, slot in enumerate(("z3", "PR", "h4", "hu") if not t else ()):
+            named("%s %s -" % (slot, slot))
+            differences(2 * d)
         if t:
             tensor("SA.")
             for k in range(16):
                 mm(view("Q1", 256 + 16 * k, 272 + 16 * k), mat("KI", k), U1, k == 0)
-            spread("Q1", 256, "NI", pc, stop=True)
+            spread("Q1", 256, "N2", pc, stop=True)
             for nm, f, c in (("SA", F_.Sign, 0.5), ("SB", F_.Sign, -0.5), ("R1", F_.Identity, RO)):
                 named(nm)
-                act(view(nm), view("Q1", 256, 512), f, bias=FO + 15.5 + c)
+                act(view(nm), view("Q1", 256, 512), f, 0.5, FO + 15.5 + c)
             tensor("PR.")
-            mm(view("DB", 256, 512), view("Ih"), view("SA"), True)
-            mm(view("DB", 256, 512), view("Nh"), view("SB"), False, True)
+            mm(view("ZB", 256, 512), view("Ih"), view("SA"), True)
+            mm(view("ZB", 256, 512), view("Nh"), view("SB"), False, True)
         tensor("pay.")
         mm(view("CB", 0, 256), view("Fhit"), view("ONE"), True)
         mm(view("CB", 240, 256), view("N64k"), view("ONE", 0, 16))
@@ -509,48 +538,49 @@ def rank_program(g, core, T, topo):
         tensor("HK.")
         mm(view("CB", 0, 256), view("I260k"), view("R1"), False, True)
         tensor("mask.")
-        masks(t, 0)
-
-    def masks(t, half):
-        a, b = HALVES[half]
-        for x, r, s in ((0, "I4k", "N32k"), (128, "N4k", "I34k")):
-            mm(view(MASKS[half], x, x + 128), view(r), view("R1", a, b), not x)
-            mm(view(MASKS[half], x, x + 128), view(s), view("SA" if t else "ONE", a, b))
+        for x, r, s in ((0, "I4k", "N32k"), (256, "N4k", "I34k")):
+            mm(view("RG", x, x + 256), view(r), view("R1"), not x)
+            mm(view("RG", x, x + 256), view(s), view("SA" if t else "ONE"))
 
     def row_p(t):
         named("PR HK" if t else "HK")
         if t:
-            tt(view("PR"), view("HI"), view("DB", 256, 512), A_.mult)
+            tt(view("PR"), view("HI"), view("ZB", 256, 512), A_.mult)
         tt(view("HK"), view("HI"), view("CB", 0, 256), A_.add)
         tensor("hp.")
-        for k in range(16 if t else 0):
-            mm(view("CB", 272, 288), view("Ib"), view("PR", 16 * k, 16 * k + 16), k == 0, k == 15)
+        if t:
+            for k in range(4):
+                mm(view("CB", 288, 352), view("Ib"), view("PR", 64 * k, 64 * k + 64), k == 0, k == 3)
+            named("h4")
+            (cp if "h4" in ONS else act)(view("h4"), view("CB", 288, 352))
+            tensor("h4.")
+            for k in range(4):
+                mm(view("CB", 272, 288), view("Ib"), view("h4", 16 * k, 16 * k + 16), k == 0, k == 3)
 
     def pairs_open(t):
         P, s_, U, pc = state(t)
         hp = view("CB", 272, 288) if t else view("HI", 0, 16)
-        named("hp hu hf Mm HO HE" if t else "hp Mm HO HE")
-        cp(view("hp"), hp)
+        named("hp hu Mm HO HE" if t else "hp Mm HO HE")
         if t:
-            cp(view("hu"), hp)
-            act(view("hf"), hp)
+            act(view("hp"), hp)
+            (act if "hu" in ONS else cp)(view("hu"), hp)
+        else:
+            acti(view("hp"), hp, view("REP", 0, 1))
         o = view("CB", 256, 272)
         tensor("Mm.")
         mm(o, view("Fmiss"), view("ONE", 0, 16), True)
         mm(o, view("N4k"), part(pc, 0, 16))
         mm(o, view("Ib"), view("hp"), False, True)
-        act(view("M", 80, 96), o)
-        tensor("pairs.")
-        for d in range(8):
-            mm(view("DB", 16 * d, 16 * d + 16), mat("SH", d), view("hp"), d == 0)
-        tti(view("HO"), view("hf") if t else hp, view("OD", 0, 8), view("SEL"), A_.mult)
+        for i in range(16):
+            mm(view("CB", 8 * i, 8 * i + 8, parts=8), view("Ib", i, 128, 16), view("hp", 1, 16, 2), i == 0, i == 15)
+        act(view("M", 16 * len(CHUNKS[0]), 16 * len(CHUNKS[0]) + 16), o)
+        (cp if "HO" in ONS else act)(view("HO", parts=8), view("CB", 0, 128, parts=8))
         o = view("CB", 384, 512)
         tensor("HE.")
         mm(o, view("Fmiss"), view("ONE", 0, 128), True)
         for k in range(4):
             mm(part(o, 32 * k, 32 * k + 32), view("N4k"), view(pc[1], pc[2], pc[3], 2))
-        mm(view("CB", 288, 352), view("Ib"), s_)
-        mm(o, view("BM"), view("HO"), False, True)
+        mm(o, view("G8", parts=8), view("HO", parts=8), False, True)
         act(view("HE"), o)
 
     def distances(t):
@@ -559,16 +589,16 @@ def rank_program(g, core, T, topo):
         def span(buf, k, m=1):
             return view(buf, 256 * k, 256 * (k + m))
 
-        def gather(k):
-            off = view("H16", 16 * k, 16 * k + 16)
+        def gather(k, m):
+            off = view("H16", 16 * k, 16 * (k + m))
             if kind[k] == "S":
-                acti(span("DR", k), SITES, off)
+                acti(span("DR", k, m), SITES, off)
             else:
-                tti(span("DR", k), SITES, off, record(t), A_.subtract)
+                tti(span("DR", k, m), SITES, off, view("AC", 0, 256 * m), A_.subtract)
 
         def size(k, m):
             if kind[k] == "S":
-                q = "Q%d" % (pairs[0] % 2)
+                q = ("Q0", "Q1", "DB")[pairs[0]]
                 pairs[0] += 1
                 tensor("A%x." % k)
                 for x in range(m):
@@ -601,31 +631,28 @@ def rank_program(g, core, T, topo):
             e, hk = view(BANKS[c], 0, 16 * rows), view("HK", 16 * k0, 16 * (k0 + rows))
             if step == "m":
                 tt(e if c else view("M", 0, 16 * rows), e, hk, A_.min)
+            if step == "x" and c == 1:
+                tt(view("M", 0, 64), e, view("M", 0, 64), A_.max)
             elif step == "x":
-                tt(view("M", 0, 16 * rows), e, view("M", 0, 16 * rows), A_.max)
-            else:
-                tt(view("M2", 0, 16 * rows), e, hk, A_.min)
-                tt(view("fa", 0, 32), view("M2", 0, 32), view("M2", 32, 64), A_.max)
-                tt(choice(t), view("fa", 0, 16), view("fa", 16, 32), A_.max)
+                for r in range(4):
+                    tt(slot(3 + r), part(e, 16 * r, 16 * r + 16), view("M", 16 * r, 16 * r + 16), A_.max)
+            elif step == "w":
+                for r in range(rows):
+                    tt(slot(r), part(e, 16 * r, 16 * r + 16), part(hk, 16 * r, 16 * r + 16), A_.min)
+                call("v", lambda: g.vector.tensor_tensor_scan(T.W[:], T.K3[:], T.M2[:], 0.0, A_.mult, A_.max), [view("W")],
+                     [view("K3")] + [slot(r) for r in range(7)], 112 * CYCLE)
 
         def fold(k):
-            if k == 0:
-                tt(view("M", 0, 32), view("M", 0, 32), view("M", 64, 96), A_.max)
-            elif k == 1 and len(CHUNKS[3]) == 1:
-                tt(view("M2", 16, 64), view("M", 0, 48), view("M", 48, 96), A_.max)
-            elif k == 1:
-                tt(view("fa" if len(CHUNKS[3]) == 3 else "M2", 32, 64), view("M", 0, 32), view("M", 32, 64), A_.max)
-            else:
-                tt(view("M2", 48, 64), view("fa", 32, 48), view("fa", 48, 64), A_.max)
+            tt(view("M", 0, 32), view("M", 0, 32), view("M", 64, 96), A_.max)
 
         for step in STEPS.split():
             k = int(step[1], 16)
-            if step[0] in "gabcfm":
+            if step[0] in "gGabcfm":
                 named(step)
             elif step[0] in "xw":
-                named(step + "m" if step[0] == "x" else "w0 w1 w2")
-            if step[0] == "g":
-                gather(k)
+                named({"x1": "x1m", "x2": "xa xb xc xd", "w3": "wa wb wc w2"}[step])
+            if step[0] in "gG":
+                gather(k, 1 + (step[0] == "G"))
             elif step[0] == "d":
                 decide(k)
             elif step[0] == "f":
@@ -643,7 +670,6 @@ def rank_program(g, core, T, topo):
         if t:
             named("old")
             acti(view("old"), SITES, view("hu"))
-        named("n1")
         tensor("n1.")
         mm(view("E1", 256, 512), view("Ib"), record(t), True)
         if t:
@@ -651,15 +677,17 @@ def rank_program(g, core, T, topo):
         else:
             mm(view("E1", 256, 512), view("Ib"), record(t))
             mm(view("E1", 256, 512), view("Ib"), view("DR", 0, 256), False, True)
-        act(view("n1"), view("E1", 256, 512), F_.Identity, 0.5, 127.75)
-        tensor("maskb.")
-        masks(t, 1)
+        tensor("pairs.")
+        for d in range(8):
+            mm(view("DB", 16 * d, 16 * d + 16), mat("SH", d), view("hp"), d == 0)
         tensor("hq.")
         mm(view("Q1", 0, 16), view("Ib"), view("hp"), True)
+        mm(view("Q1", 0, 16), view("N4k"), view("CGO"))
         turn[0] += 1
-        named("G4 ex eq fo fp x7 x6 x5 x4 x3 x2 x1 x0")
-        acti(view("G4"), choice(t), view("REP", 0, 4), F_.Identity, 2.0 ** -5, (GO - 0.4925) * 4096)
-        tti(view("ex"), choice(t), view("EV", 0, 8), view("HE"), A_.is_equal)
+        named("n1 GW ex eq fo x7 x6 x5 x4 x3 x2 x1 x0")
+        act(view("n1"), view("E1", 256, 512), F_.Identity, 0.5, 127.75)
+        acti(view("G4"), view("W"), view("R4", 0, 4), F_.Identity, 2.0 ** -5, (GO - 0.4925) * 4096)
+        tti(view("ex"), view("W"), view("EV", 0, 8), view("HE"), A_.is_equal)
         tensor("eq.")
         for d in range(8):
             mm(view("DB", 16 * d, 16 * d + 16), mat("SH", d), view("G4", 0, 16), False, d == 7)
@@ -671,12 +699,9 @@ def rank_program(g, core, T, topo):
         tensor("fo.")
         for d in range(8):
             mm(view("Q1", 0, 16), mat("RD", d), view("eq", 16 * d, 16 * d + 16), False, d == 7)
-        ts(view("fo", 0, 16, 2), view("Q1", 0, 16, 2), -4096 * GO, A_.add, col("dum"), A_.min)
-        odd = (view("fo", 1, 16, 2)[0], "fp", 0, 16)
-        ts(odd, view("Q1", 1, 16, 2), -4096 * GO, A_.add, col("dun"), A_.min)
+        tt(view("fo", 0, 16), view("Q1", 0, 16), view("DUM"), A_.min)
         for j in range(14, -1, -2):
             scat(view("X"), view("fo", j, j + 2), view("n1", 16 * j, 16 * j + 32), view("C128"))
-            calls[-1]["ins"].append(odd)
 
     def limit():
         named("mis jk l1 l2 l3 TH")
@@ -691,44 +716,37 @@ def rank_program(g, core, T, topo):
 
     def become(t, names_):
         P = state(t)[0]
-        named("hs sf sh bq" if t else "hs sf bq")
-        tsi(view("hs"), choice(t), view("REP", 0, 4), 4095, A_.bitwise_and)
-        tt(view("sh" if t == 0 else "sf"), view("CB", 288, 352), view("hs"), A_.mult)
-        if t:
-            ts(view("sh"), view("sf"), 25952 * t, A_.add)
-        ts(view("bq"), view("sh"), 5, A_.arith_shift_right, 2047, A_.bitwise_and)
-        for bank, h in zip(MASKS, "ab"):
-            tensor("P%s." % h)
-            for x in range(0, 256, 64):
-                mm(view(bank, x, x + 64), view("Ih" if x >= 128 else "Nh"), view("G4"), False, x == 192)
+        named("hs low sf bq")
+        ts(view("WS", 48 * t + 1, 48 * t + 32, 2), view("W", 6, 112, 7), 4095, A_.bitwise_and)
+        ts(view("WS", 48 * t + 32, 48 * t + 48), view("W", 6, 112, 7), 2 ** 17 - 1, A_.bitwise_and)
+        o, d0, d1 = view("sh", 0, 32), view("WS", 48 * t, 48 * t + 32), view("SC", 32 * t, 32 * t + 32)
+        call("v", lambda: g.vector.tensor_tensor_scan(o[0], d0[0], d1[0], 0.0, A_.mult, A_.add), [o], [d0, d1], 64 * CYCLE)
+        tsi(view("bq"), o, view("ODD", 0, 4), 5, A_.arith_shift_right, 2047, A_.bitwise_and)
+        tensor("Pa.")
+        spread("RG", 0, "Nh", view("G4"))
+        spread("RG", 256, "Ih", view("G4"), stop=True)
         tensor(None)
         fold = FOLD and t < HOPS - 1
         for a, b in HALVES:
             named(("Pb t2 t3" if a else "Pa t0 t1") + ("" if fold else " Nb" if a else " Na"))
-            bank = MASKS[a // 128]
-            tt(part(names_, a, b) if fold else view(bank, 0, 128), part(P, a, b), view(bank, 0, 128), A_.min)
+            tt(part(names_, a, b) if fold else view("RG", a, b), part(P, a, b), view("RG", a, b), A_.min)
             for x in range(a, b, 64):
-                tt(view("CP", 256 * t + x, 256 * t + x + 64) if fold else view("tP", x, x + 64), view("bq"), view(bank, 128 + x - a, 192 + x - a), A_.min)
+                tt(view("CP", 256 * t + x, 256 * t + x + 64) if fold else view("tP", x, x + 64), view("bq"), view("RG", 256 + x, 320 + x), A_.min)
             if not fold:
-                tt(part(names_, a, b), view("tP", a, b), view(bank, 0, 128), A_.max)
+                tt(part(names_, a, b), view("tP", a, b), view("RG", a, b), A_.max)
 
     def finish():
-        unpack(HOPS, choice(HOPS - 1))
+        unpack(HOPS, view("WS", 48 * HOPS - 48, 48 * HOPS))
         _, sn, Un, pn_ = state(HOPS)
         tensor("U.")
-        mm(view("ZB", 256, 512), view("F32"), view("ONE"), True)
-        spread("ZB", 256, "N4k", Un, stop=True)
-        for (a, b), h in zip(HALVES, "ab"):
-            named("V%s b%s" % (h, h))
-            acti(view("Pv", 256 - b, 256 - a), view("Pf", a, b), view("RVP", 0, 8))
-            tt(view("yb", a, b), view("Pf", a, b), view("ZB", 256 + a, 256 + b), A_.subtract)
-        for (a, b), h in zip(HALVES, "ab"):
-            named("m%s o%s" % (h, h))
-            tt(view("ZB", 256 + a, 256 + b), view("Pv", a, b), view("ZB", 256 + a, 256 + b), A_.min)
-            tt(view("yo", a, b), view("ZB", 256 + a, 256 + b), view("yb", a, b), A_.max)
-        for a, h in zip((0, 256), "ab"):
+        mm(view("ZB", 0, 16), view("Ib"), view("UNF"), True)
+        mm(view("ZB", 0, 16), view("N128"), part(Un, 0, 16))
+        mm(view("ZB", 0, 16), view("N128"), part(Un, 0, 16), False, True)
+        named("Uo")
+        act(view("UN2"), view("ZB", 0, 16))
+        for a, h in zip(range(0, 1024, 256), "abcd"):
             named("D%s T%s" % (h, h))
-            acti(view("TA", a, a + 256), view("yo"), view("DUP2", a // 16, a // 16 + 16))
+            acti(view("TA", a, a + 256), view("Pf"), view("DUP2", a // 16, a // 16 + 16))
             turn32(view("TB", a, a + 256), view("TA", a, a + 256))
         named("Un")
         acti(view("yl"), view("TB"), view("UN2"))
@@ -750,12 +768,14 @@ def rank_program(g, core, T, topo):
         if t < n - 1:
             send(t + 1, view("AR", 512 * t + 512, 512 * t + 1024), view("AR", 0, 512), "ar%d" % (t + 1), [view("H16", 0, 64)])
         distances(t)
+        if not t:
+            key_matrices()
         writes(t)
         if t < HOPS - 1:
             limit()
             become(t, view("CO", 256 * t, 256 * t + 256))
             named("ms")
-            send(1, view("WL", 16 * t + 16, 16 * t + 32), choice(t), "ms%d" % t)
+            send(1, view("WL", 48 * t + 48, 48 * t + 96), view("WS", 48 * t, 48 * t + 48), "ms%d" % t)
             for a, b, sem in PIECES:
                 named(sem)
                 send(1, part(state(t + 1)[0], a, b), view("CO", 256 * t + a, 256 * t + b), sem + str(t),

@@ -1,4 +1,3 @@
-import math
 from concourse.bass import DstId, RemoteDMATransfer
 from concourse.mybir import AluOpType, ActivationFunctionType
 
@@ -8,28 +7,32 @@ HOPS = 7
 NX = 2080
 BIG = 2.0 ** 22
 ROUND16 = 1.5 * 2 ** 27
-CHUNKS = ("RRRRR", "SSSS", "SSAA", "RAA")
-STEPS = "h0 G0 b0 G2 b2 g4 a4 d0 p0 m0 f0 G5 b5 G7 b7 d1 m1 x1 G9 b9 Gb bb d2 m2 x2 Gd ad ae gf af d3 w3"
-CYCLE, GATHER, SCATTER, COLUMN, WAKE, HOPLAT, LINK, DMALAT, DMABW = 1.04e-3, 1.3e-3, 3.15e-3, 0.48e-3, 0.19, 1.2, 100e3, 2.0, 200e3
-ACT = 0.06
-ONS = "HO h4"
+CHUNKS = ("RRRR", "SSSS", "AASS", "HHHH")
+SLOTS = 9
+STEPS = "h0 G0 G2 c0 d0 p0 m0 G4 b4 G6 b6 d1 m1 x1 G8 b8 Ga ba d2 m2 f2 Gc bc Ge be d3 w3"
+CYCLE, GATHER, SCATTER, COLUMN, HOPLAT, LINK, DMALAT, DMABW = 0.87e-3, 1.15e-3, 2.6e-3, 0.43e-3, 1.5, 150e3, 1.8, 300e3
+ACT, VFIX, WAKE, WSAME = 0.05, 0.04, 0.14, 0.2
+COPIES = {"hu": "g", "Hf": "g", "z3": "g", "sc": "g", "hp": "s", "HO": "s", "h4": "s", "AD": "s"}
+PRS = False
 PASSES = 4
-BANKS = ("E0", "E1", "ZB", "Q1")
+BANKS = ("E0", "E1", "Q1", "Q0")
+PB = "ZB"
 ORDER, SPAN = [], []
-TURNS = ("hs low sf ex bq Pa t1 t0 eq t2 t3 Pb fo x7 x6 x5 x4 x3 y0 u0 x2 z0 y1 x1 u1 y2 z1 x0 y3 z2 u2 g4 z3 u3 PR HK "
-         "G0 h4 G2 a4 b0 Gb hu b2 Gd gf m0 ad m1 f0 HO m2 x1m xa xb xc xd wa wb wc w2 "
-         "GW n1 mis jk l1 l2 l3 U s F sc AO TH AC R1 SA SB AD G5 G7 G9 b5 b7 hp b9 bb Mm ae af old HE "
-         "ms ma mb "
-         "32. Pa. eq. jk. ex. fo. keysZB keysE1 pay. AO. SA. s. sUZB sUE1 payF. HK. mask. PR. A9. A5. D1. X5. A7. hp. X7. D2. h4. X9. D0. "
-         "E1. Mm. E0. E2. D3. E3. HE. pairs. hq. n1.")
-LAST = ("hs low ex sf eq bq y1 fo t1 x7 t2 Pa x6 t0 Pb x5 Na t3 x4 Nb x3 x2 sp sq x1 x0 Tb Ta Tc Td "
-        "GW F n1 U s Uo Db Da Dc Dd so Un eq. ex. fo. Pa. U. sp.")
-PIECES = ((0, 128, "ma"), (128, 256, "mb"))
+TURNS = ("hs low sf ex bq eq Pa t0 t1 t2 t3 Pb fo Nb x7 z0 x6 z1 x5 z2 x4 x3 u0 x2 u1 x1 u2 x0 u3 "
+         "G0 G2 PR G8 c0 Ge Gc re rc m0 m1 xm m2 xa xb xc xd wa wb wc wd w2 "
+         "GW n1 mis sn Un jk l1 l2 U s F l3 AO TH AC R1 SA AD SB G4 G6 Ga b4 b6 h4 b8 ba HK hp be bc HO Mm old sd HE "
+         "ms ma z3 mh mb sc Hf hu "
+         "eq. Pa. jk. ex. fo. 32ZB keysZB keysE1 32E1 sE1 sUE1 AO. sZB SA. sUZB A4. mask. pay. Aa. payF. PR. D1. HK. X4. A6. X6. "
+         "hp. D0. Xa. Hf. E0. h4. D2. E1. D3. L3. E2. Mm. O3. E3. pairs. HE. hq. n1.")
+LAST = ("hs low sf ex bq sp y1 eq sq t0 t1 t2 t3 Pb Pa fo Nb x7 Na x6 x5 x4 x3 x2 Td x1 Tb x0 Ta Tc "
+        "GW s U F n1 so Dd Db Da Dc Uo Un eq. Pa. ex. fo. U. sp.")
 EYES = {"I1184": 1184.0, "I4k": 4096.0, "N64k": -2.0 ** 16, "I260k": 2.0 ** 18 + 4096, "I16": 16.0, "N4k": -4096.0, "NI": -1.0,
-        "N128": -128.0, "N32k": -32768.0, "I34k": 34816.0, "Ih": 0.5, "Nh": -0.5, "N2": -2.0}
-FOLD = True
+        "N128": -128.0, "N32k": -32768.0, "I34k": 34816.0, "Ih": 0.5, "Nh": -0.5, "N2": -2.0, "I9": 9.0, "I17": 17.0, "I25": 25.0,
+        "I2": 2.0, "I4": 4.0, "I6": 6.0}
 FO = GO = 192
 RO = GO // 2 + 8
+HIT, MISS = 2 ** 17 + 4096 + 32 - FO * 4096 - RO * EYES["I260k"], (FO + 31) * 4096 + 32.0
+HIT_SUM = round(HIT / 2 ** 17) * 1024.0
 SIZE = {"float32": 4, "int32": 4, "bfloat16": 2, "float16": 2, "uint16": 2}
 
 SCRATCH = {}
@@ -43,27 +46,29 @@ def _shared(buf, dtype, width, names):
 
 
 _shared("eyes", "bfloat16", 128, ["Ib"] + list(EYES))
-_shared("cols", "float32", 4, ("p16", "q31", "c3", "p256", "q287", "pa", "pb", "p128", "p240", "kf", "mc", "m1", "m2", "m3"))
+_shared("cols", "float32", 4, ("p16", "c3", "c4", "p256", "q287", "pa", "pb", "p128", "p240", "kf", "pc", "mc", "m1", "m2", "m3"))
+_shared("LL", "bfloat16", 144, ("LE", "LP"))
 _shared("i64", "int32", 64, ("sh", "bq"))
 _shared("f64", "float32", 64, ("fa", "sf"))
 _shared("u32", "uint16", 32, ("DUP1", "fo"))
-_shared("u16", "uint16", 16, ("UN1", "UN2", "AO", "hu", "REP", "EV", "ODD", "R4"))
-_shared("i16", "int32", 16, ("inn", "ip", "q15", "q31i", "q7"))
-_shared("f8", "float32", 8, ("td", "te", "tg", "tc"))
-_shared("b128", "bfloat16", 128, ("BM", "BM16", "D", "LOW", "J", "G8", "F25", "Fhit", "Fmiss", "TH", "eq", "ex"))
+_shared("u16", "uint16", 16, ("UN1", "UN2", "AO", "hu", "REP", "R32", "EV", "ODD", "R4"))
+_shared("i16", "int32", 16, ("inn", "ip", "q15", "q31i", "q7", "qo", "qv", "qw", "qe"))
+_shared("f8", "float32", 8, ("td", "te", "tg", "tc", "tw", "th"))
+_shared("b128", "bfloat16", 128, ("BM", "BM16", "D", "G8", "F25", "Fhit", "TH", "eq", "ex"))
 for _n, _w, _d in (
     ("X", NX, "bfloat16"), ("AR", 2048, "bfloat16"), ("DR", 4096, "bfloat16"), ("DA", 4096, "bfloat16"),
-    ("LE", 144, "bfloat16"), ("LP", 144, "bfloat16"), ("KI", 2048, "bfloat16"), ("DG", 2048, "float16"),
-    ("SH", 1024, "bfloat16"), ("RD", 1024, "bfloat16"), ("W8", 144, "bfloat16"),
-    ("ST", 320 * (HOPS + 1), "float16"), ("CO", 256 * HOPS, "float16"), ("CP", 256 * HOPS, "float16"), ("W", 112, "int32"), ("K3", 112, "bfloat16"),
+    ("SH", 1024, "bfloat16"), ("RD", 1024, "bfloat16"),
+    ("KD", 16, "float32"), ("rk", 16, "float16"), ("DG", 2048, "float16"),
+    ("ST", 320 * (HOPS + 1), "float16"), ("CO", 256 * HOPS, "float16"), ("CP", 256 * HOPS, "float16"), ("W", 16 * SLOTS, "int32"), ("K3", 16 * SLOTS, "bfloat16"),
     ("CGO", 16, "bfloat16"), ("DUM", 16, "float32"),
-    ("WS", 48 * HOPS, "int32"), ("WL", 48 * HOPS, "int32"), ("M", 128, "float32"), ("M2", 112, "float32"),
-    ("PI", 256, "int32"), ("SI", 256, "int32"), ("S16", 256, "float16"), ("KA", 1, "int32"), ("TA", 1024, "float32"), ("TB", 1024, "float32"),
+    ("WS", 48 * HOPS, "int32"), ("WL", 48 * HOPS, "int32"), ("M", 64, "float32"), ("M2", 16 * SLOTS, "float32"),
+    ("PI", 272, "int32"), ("PT", 512, "int32"), ("SI", 32, "int32"), ("SJ", 32, "int32"), ("KA", 1, "int32"), ("TA", 1024, "float32"), ("TB", 1024, "float32"),
     ("DUP2", 64, "uint16"), ("UNF", 16, "float16"),
-    ("i2", 32, "int32"), ("ONE", 256, "bfloat16"), ("C32k", 96, "bfloat16"),
-    ("LT", 16, "float16"), ("rk", 16, "float16"), ("s1", 16, "float32"), ("KTa", 256, "float16"), ("KTb", 256, "float16"), ("KD", 16, "float32"),
+    ("i2", 32, "int32"), ("ONE", 256, "bfloat16"), ("C32k", 64, "bfloat16"),
+    ("LT", 16, "float16"), ("KTa", 256, "float16"), ("KS", 272, "float16"), ("KN", 144, "float16"), ("RS", 256, "bfloat16"), ("kb", 16, "float16"),
+    ("HS", 128 * HOPS, "uint16"), ("sn", 64, "float16"), ("Un", 16, "bfloat16"),
     ("AC", 512, "bfloat16"), ("R1", 256, "bfloat16"), ("SA", 256, "bfloat16"), ("SB", 256, "bfloat16"),
-    ("Z", 256, "float32"), ("ZI", 256, "int32"), ("HI", 256, "int32"), ("H16", 256, "uint16"), ("HK", 256, "float32"), ("PR", 256, "float16"),
+    ("Z", 256, "float32"), ("ZI", 256, "int32"), ("HI", 256, "int32"), ("H16", 256 * HOPS, "uint16"), ("HK", 256, "float32"), ("PR", 256, "float16"), ("Hf", 256, "float16"),
     ("hp", 16, "float16"), ("h4", 64, "float16"), ("SC", 32 * HOPS, "float32"), ("G4", 64, "bfloat16"), ("mis", 16, "bfloat16"), ("C128", 32, "bfloat16"), ("UF", 128 * (HOPS + 1), "bfloat16"),
     ("old", 256, "bfloat16"), ("n1", 256, "bfloat16"), ("tP", 256, "float32"),
     ("hf", 16, "float32"), ("HE", 128, "float32"), ("HO", 128, "float16"), ("jk", 16, "float32"),
@@ -76,7 +81,7 @@ for _n in PS:
     SCRATCH[_n] = ("psum", [128, 512], "float32")
 
 SEMAPHORES = (["qv", "qs", "qp", "qg", "snd", "lx", "la", "lr", "lk", "lz", "lp", "oy", "oz"]
-              + [m + str(t) for m in ("ma", "mb", "ms") for t in range(HOPS - 1)] + ["ar%d" % d for d in (1, 2, 3)])
+              + [m + str(t) for m in ("ma", "mb", "ms", "mh") for t in range(HOPS - 1)] + ["ar%d" % d for d in (1, 2, 3)] + ["kn"])
 
 
 def needs(calls):
@@ -84,7 +89,7 @@ def needs(calls):
     log, bank, sender = {}, {}, {}
     for k, c in enumerate(calls):
         def after(j, wait=True):
-            gap = calls[j]["done"] + WAKE if wait else 0.0
+            gap = calls[j]["done"] + (WSAME if calls[j]["q"] == c["q"] else WAKE) if wait else 0.0
             pre[k][j] = max(pre[k].get(j, 0.0), gap)
         if c["kind"] == "send":
             sender[c["sem"]] = k
@@ -166,7 +171,7 @@ def plan(calls, pre):
             left[j] -= 1
             if not left[j]:
                 todo.append(j)
-    assert len(todo) == n
+    assert len(todo) == n, [calls[k]["name"] for k in range(n) if left[k]][-40:]
     best = None
     for _ in range(PASSES):
         out, end = run(ahead, [0.0] * n, rest)
@@ -223,11 +228,11 @@ def rank_program(g, core, T, topo):
 
     def vcost(o, a):
         half = SIZE[SCRATCH[a[1]][2]] == 2 and SIZE[SCRATCH[o[1]][2]] == 2
-        return CYCLE * max(64, width(a) * (0.5 if half else 1))
+        return VFIX + CYCLE * max(64, width(a) * (0.5 if half else 1))
 
     def tt(o, a, b, op):
         call("v", lambda: g.vector.tensor_tensor(o[0], a[0], b[0], op), [o], [a, b],
-             CYCLE * max(64, width(a) * (1 if a[1] in PS or b[1] in PS else 2)))
+             VFIX + CYCLE * max(64, width(a) * (1 if a[1] in PS or b[1] in PS else 2)))
 
     def tti(o, win, off, b, op):
         call("v", lambda: g.vector.tensor_tensor(o[0], win[0].indirect(off[0]), b[0], op), [o], [win, off, b], 0.05 + GATHER * width(o))
@@ -254,14 +259,6 @@ def rank_program(g, core, T, topo):
     def scat(win, off, a, b):
         call("v", lambda: g.vector.tensor_tensor(win[0].indirect(off[0]), a[0], b[0], A_.add), [win], [off, a, b], 0.05 + SCATTER * width(a))
 
-    def pieces(total):
-        left, out = total / 32, []
-        for k in range(4):
-            unit = 2.0 ** (math.frexp(left)[1] - 8)
-            out.append(round(left / unit) * unit)
-            left -= out[-1]
-        return out
-
     def select(o, a, pattern, op, fill, base=0, step=1):
         call("g", lambda: g.affine_select(o[0], a[0], pattern, op, fill, base, step), [o], [a], 0.17 + 2 * CYCLE * width(o))
 
@@ -282,6 +279,13 @@ def rank_program(g, core, T, topo):
 
     def acti(o, win, off, f=F_.Copy, scale=1.0, bias=0.0):
         call("s", lambda: g.scalar.activation(o[0], win[0].indirect(off[0]), f, bias=bias, scale=scale), [o], [win, off], 0.065 + GATHER * width(o))
+
+    def copy(name, o, a):
+        q = COPIES.get(name, "v")
+        if q == "g":
+            select(o, a, [[0, width(o)]], A_.is_equal, 0.0, 0, 0)
+        else:
+            (cp if q == "v" else act)(o, a)
 
     def mm(o, l, r, start=False, stop=False):
         call("p", lambda: g.tensor.matmul(o[0], l[0], r[0], start, stop), [o], [l, r], COLUMN * max(min(64, width(l)), width(r)))
@@ -328,8 +332,8 @@ def rank_program(g, core, T, topo):
     SITES = view("X", 0, 2048)
     HALVES = ((0, 128), (128, 256))
 
-    load("y", view("PI"), T.pn[:], "lp")
-    load("s", view("SI", parts=8), T.s0[:], "lz")
+    load("y", view("PI", 0, 256), T.pn[:], "lp")
+    load("s", view("SI", 0, 16), T.s0[:], "lz")
     load("s", view("KA"), T.kap[:], "lk")
     load("s", view("AR", 0, 256), T.a0[:], "la")
     load("y", SITES, T.x[:], "lx")
@@ -337,151 +341,215 @@ def rank_program(g, core, T, topo):
 
     P0, s0_, U0, p0 = state(0)
     ONES = view("ONE", 0, 128)
-    hit, miss = pieces(2 ** 17 + 4096 + 32 - FO * 4096 - RO * EYES["I260k"]), pieces((FO + 31) * 4096 + 32)
-    fills = [(view(nm), c) for nm, c in (("LE", 0.0), ("LP", 0.0), ("F25", 0.25), ("TH", 67.0))]
-    for k, (nm, c) in enumerate((("C32k", 32768.0), ("C128", -128.0), (U0, 1.0), (p0, FO + 16.0))):
-        fills += [(view("Fhit", parts=32, p0=32 * k), hit[k]), (view("Fmiss", parts=32, p0=32 * k), miss[k]), (view(nm) if k < 2 else nm, c)]
-
-    def fill(count):
-        for _ in range(count):
-            ms(*fills.pop(0))
-
     turn[0] = -1
     ms(view("ONE"), 1.0)
     iota(view("ip"), [[0, 16]], 0, 1)
-    iota(view("i2"), [[1, 16], [0, 2]], 0, 0)
     iota(view("inn"), [[1, 16]], 0, 0)
-    select(view("Ib"), ONES, [[-1, 128]], A_.is_equal, 0.0)
-    select(view("BM"), ONES, [[-16, 8], [0, 16]], A_.is_ge, 0.0)
-    select(view("W8", parts=8), view("ONE", 0, 144, parts=8), [[1, 144]], A_.is_equal, 0.0, -15, -16)
-    select(view("BM"), view("BM"), [[16, 8], [0, 16]], A_.is_ge, 0.0, 15, -1)
-    iota(view("R1"), [[1, 16], [0, 16]], RO, 0)
     iota(view("D"), [[1, 128]], 0, -1)
-    select(view("LOW"), ONES, [[-1, 128]], A_.is_gt, 0.0)
     iota(view("td"), [[1, 8]], 1, 0)
-    iota(view("te"), [[-1, 8]], 15, 0)
-    iota(view("SC", 1, 32 * HOPS, 2), [[25952, HOPS], [0, 16]], 0, 0)
-    iota(view("KI", 1280, 2048), [[2, 6], [0, 128]], 21, 0)
-    fill(3)
+    select(view("BM"), ONES, [[-16, 8], [0, 16]], A_.is_ge, 0.0)
+    iota(view("R1"), [[1, 16], [0, 16]], RO, 0)
+    select(view("BM"), view("BM"), [[16, 8], [0, 16]], A_.is_ge, 0.0, 15, -1)
     ts(view("q15"), view("ip"), 15, A_.bitwise_and)
     ts(view("q31i"), view("ip"), 31, A_.bitwise_and)
-    fill(2)
-    cp(col("p16"), col("q15"))
-    cp(col("q31"), col("q31i"))
-    cp(view("REP"), view("q15"))
-    fill(1)
-    ts(col("c3"), col("p16"), 31, A_.mult, col("q31"), A_.add)
-    ts(view("DUP1"), view("i2"), 16, A_.mult, col("p16"), A_.add)
-    ts(col("pa"), col("p16"), RO, A_.add)
-    ts(col("pb"), col("p16"), -1, A_.mult, RO + 15, A_.add)
-    fill(1)
-    ts(view("UN1"), view("inn"), col("c3"), A_.add)
-    fill(len(fills))
-    cp(view("S16", parts=8), view("SI", parts=8))
-    cp(col("kf"), view("KA"))
-    for i in range(16):
-        mm(view("E0", 0, 16), view("W8", 15 - i, 143 - i, parts=8), view("S16", i, 256, 16, parts=8), i == 0, i == 15)
-    eyes = list(EYES)
-    for nm in eyes[:7]:
-        act(view(nm), view("Ib"), scale=EYES[nm])
+    ts(view("qo"), view("ip"), 4, A_.arith_shift_right, 1, A_.bitwise_and)
+    ms(view("LL"), 0.0)
+    act(view("F25"), ONES, scale=0.25)
+    act(view("TH"), ONES, scale=67.0)
+    for nm, m, c in (("p16", 1, 0), ("pb", -1, 15), ("pa", 1, RO)):
+        act(col(nm), col("q15"), F_.Identity, float(m), float(c))
+    act(col("pc"), col("q15"), F_.Abs, 2.0, -15.0)
+    act(col("p128"), col("q15"), F_.Identity, 1.0, 128.0)
+    tt(view("qv"), view("q31i"), view("qo"), A_.subtract)
+    ts(view("Ib"), view("D"), 0, A_.is_equal)
+    cp(view("R32"), view("q31i"))
+    ts(view("qw"), view("qv"), 15, A_.bitwise_and)
+    ts(view("qe"), view("qv"), 1, A_.bitwise_and)
+    ts(view("tw"), view("td"), col("pb"), A_.is_gt, -16, A_.mult)
+    ts(view("I1184"), view("Ib"), EYES["I1184"], A_.mult)
+    tt(view("qv"), view("qw"), view("qo"), A_.add)
+    ts(col("c3"), col("qe"), 15, A_.mult)
+    tt(view("th"), view("tw"), view("td"), A_.add)
+    ms(view("C32k"), 32768.0)
+    ts(col("c4"), col("qv"), col("c3"), A_.add, 16, A_.mult)
+
+    def shifts(a, b):
+        for d in range(a, b):
+            ts(mat("SH", d), view("D"), view("th", d, d + 1), A_.is_equal)
+
+    def eyes(text):
+        for nm in text.split():
+            act(view(nm), view("Ib"), scale=EYES[nm])
+
+    def diagonal(text):
+        for nm in text.split():
+            select(view(nm), view("Ib"), [[-1, 128]], A_.not_equal, EYES[nm])
+
+    iota(view("RS", 0, 128), [[-2, 8], [0, 16]], 15, 0)
+    iota(view("RS", 128, 256), [[2, 8], [0, 16]], 1, 0)
+    iota(view("te"), [[-1, 8]], 15, 0)
+    eyes("NI N64k I4k I260k")
+    shifts(0, 2)
+    ts(view("UN1"), view("inn"), col("c4"), A_.add)
+    shifts(2, 4)
+    act(view("SI", 16, 32), view("SI", 0, 16))
+    act(col("kf"), view("KA"))
     act(view("BM16"), view("BM"), scale=16.0)
+    turn32(view("SJ"), view("SI"))
+    shifts(4, 5)
+    ts(view("KTa"), view("R1"), col("pa"), A_.is_equal, col("kf"), A_.mult)
+    acti(s0_, view("SJ"), view("R32", 0, 4))
+    shifts(5, 6)
+    act(view("PI", 256, 272), view("PI", 0, 16))
+    act(view("AC", 0, 256), view("AR", 0, 256))
+    act(view("AC", 256, 512), view("AR", 0, 256))
+    turn32(view("PT", 0, 256), view("PI", 0, 256))
+    turn32(view("PT", 256, 512), view("PI", 16, 272))
+    shifts(6, 8)
+    ts(view("kb"), view("inn"), col("pb"), A_.is_equal, col("kf"), A_.mult)
+    cpi(part(P0, 0, 128), view("PT"), view("UN1", 0, 8))
+    acti(part(P0, 128, 256), view("PT"), view("UN1", 8, 16))
+    tt(view("rk"), view("KTa", 0, 256, 16), view("kb"), A_.subtract)
+    ts(view("q7"), view("ip"), 7, A_.bitwise_and)
+    ts(view("KS", 0, 256), view("RS"), col("pc"), A_.is_equal, col("kf"), A_.mult)
+    for half in range(2):
+        four = view("SH", 512 * half, 512 * half + 512)
+        select(four, four, [[0, 4], [-1, 128]], A_.not_equal, -1.0)
     act(view("LE", 15, 143, 16), view("BM", 0, 128, 16), scale=-BIG)
     act(view("LP", 15, 143, 16), view("BM", 0, 128, 16), scale=BIG)
-    acti(view("TA", 256, 512), view("PI"), view("DUP1", 16, 32))
-    act(view("s1"), view("E0", 0, 16))
-    act(view("AC", 0, 256), view("AR", 0, 256))
-    acti(s0_, view("s1"), view("REP", 0, 4))
-    act(view("AC", 256, 512), view("AR", 0, 256))
-    cpi(view("TA", 0, 256), view("PI"), view("DUP1", 0, 16))
-    ts(view("KTa"), view("R1"), col("pa"), A_.is_equal, col("kf"), A_.mult)
-    turn32(view("TB", 0, 256), view("TA", 0, 256))
-    turn32(view("TB", 256, 512), view("TA", 256, 512))
-    ts(view("KTb"), view("R1"), col("pb"), A_.is_equal, col("kf"), A_.mult)
-    cpi(part(P0, 0, 128), view("TB", 0, 512), view("UN1", 0, 8))
-    tt(view("rk"), view("KTa", 0, 256, 16), view("KTb", 0, 256, 16), A_.subtract)
-    acti(part(P0, 128, 256), view("TB", 0, 512), view("UN1", 8, 16))
+    for o, c in ((U0, 1.0), (p0, FO + 16.0), (view("Fhit"), HIT_SUM)):
+        act(o, view("ONE", 0, width(o)), scale=c)
     turn[0] = 0
-    mm(view("RG", 0, 128), view("Ib"), view("D"), True)
-    mm(view("RG", 0, 128), view("I16"), view("LOW"))
-    mm(view("RG", 0, 128), view("N4k"), view("BM"), False, True)
-    mm(view("RG", 128, 256, parts=8), view("Ib", 0, 128, 16), view("BM"), True, True)
+    tensor("A4.")
+    mm(view("Q1", 0, 16), view("BM"), view("rk"), True, True)
     turn[0] = -1
-    act(view("J"), view("RG", 0, 128), F_.Identity, bias=4096.0)
-    act(view("G8", parts=8), view("RG", 128, 256, parts=8))
-    for nm in eyes[7:]:
-        turn[0] = -(nm not in ("N128", "N2"))
-        act(view(nm), view("Ib"), scale=EYES[nm])
+    act(view("KS", 256, 272), view("Q1", 0, 16))
+    act(view("KD", 0, 8), view("Q1", 0, 8))
+    eyes("N4k N32k I34k")
     turn[0] = 0
-    ms(view("WS", 0, 48 * HOPS, 2), 0)
-    turn[0] = -1
-    act(view("SC", 0, 32, 2), view("s1"))
-    turn[0] = 0
-    ts(view("ODD"), view("q15"), 2, A_.mult, 1, A_.add)
-    ts(view("q7"), view("ip"), 7, A_.bitwise_and)
-    ts(view("EV"), view("q7"), 14, A_.mult, 6, A_.add)
-    ts(view("R4"), view("q15"), 7, A_.mult, 6, A_.add)
-    ms(view("K3"), 1.0)
-    ms(view("K3", 0, 112, 7), 0.0)
-    ms(view("CGO"), GO)
-    for nm, m, c in (("p128", 1, 128), ("p240", -16, 240), ("p256", 16, 0)):
-        ts(col(nm), col("p16"), m, A_.mult, c, A_.add)
-    iota(view("DUM"), [[0, 8], [16, 2]], 2048, 0)
-    ts(view("DUM"), view("DUM"), col("p16"), A_.add)
-    ts(col("q287"), col("q31"), 256, A_.add)
-    ts(view("UNF"), view("inn"), 32, A_.mult, col("q287"), A_.add)
-    ts(view("LT"), view("inn"), 16, A_.mult, col("p128"), A_.add)
-    ts(view("DUP2", 0, 32), view("i2"), col("p256"), A_.add)
-    ts(view("DUP2", 32, 64), view("i2"), col("p240"), A_.add)
-    def differences(d):
-        two = view("SH", 128 * d, 128 * d + 256)
-        for x in (d, d + 1):
-            ts(mat("SH", x), view("J"), x + 1, A_.is_equal)
-        select(two, two, [[0, 2], [-1, 128]], A_.not_equal, -1.0)
-
+    named("sd sd sd")
+    for nm, src, m, c in (("R4", "q15", SLOTS, SLOTS - 1), ("EV", "q7", 2 * SLOTS, SLOTS - 1), ("ODD", "q15", 2, 1)):
+        act(view(nm), view(src), F_.Identity, float(m), float(c))
+    named("hp")
+    eyes("I16")
     ts(view("tg"), view("td"), col("p16"), A_.is_gt)
     tt(view("tc"), view("tg"), view("te"), A_.mult)
-    for d in range(1, 9):
-        ts(mat("RD", d - 1), view("J"), view("tc", d - 1, d), A_.is_equal, 4096, A_.mult)
+    named("sd old")
+    act(view("REP"), view("q15"))
+    act(view("LT"), view("inn"), F_.Identity, 16.0, col("p128"))
+    named("mb " * 8)
+    select(view("K3"), view("ONE", 0, 16 * SLOTS), [[0, 16], [1, SLOTS]], A_.not_equal, 0.0, 0, 0)
+    select(view("G8", parts=8), view("ONE", 0, 128, parts=8), [[1, 8], [0, 16]], A_.is_equal, 0.0, 0, -1)
+    iota(view("CGO"), [[0, 16]], GO, 0)
+    iota(view("DUM"), [[0, 8], [16, 2]], 2048, 0)
+    iota(view("WS", 0, 48 * HOPS, 2), [[0, 24 * HOPS]], 0, 0)
+    iota(view("SC", 1, 32 * HOPS, 2), [[25952, HOPS], [0, 16]], 0, 0)
+    iota(view("C128"), [[0, 32]], -128, 0)
+    iota(view("i2"), [[1, 16], [0, 2]], 0, 0)
+    named("hu " * 6)
+    diagonal("Nh Ih N128 N2 I9 I17")
+    turn[0] = 1
+    named("z3 " * 3)
+    diagonal("I25 I2 I4")
+    named("x6")
+    ts(view("I6"), view("Ib"), EYES["I6"], A_.mult)
+    turn[0] = 0
+    named("sd sd")
+    act(view("SC", 0, 32, 2), part(s0_, 0, 16))
+    act(view("DUM"), view("DUM"), F_.Identity, 1.0, col("p16"))
+    turn[0] = 2
+    named("l1 l1 l2 l2 l3 l3")
+    act(col("p240"), col("p16"), F_.Identity, -16.0, 240.0)
+    act(col("p256"), col("p16"), F_.Identity, 16.0)
+    act(col("q287"), col("q31i"), F_.Identity, 1.0, 256.0)
+    act(view("DUP2", 0, 32), view("i2"), F_.Identity, 1.0, col("p256"))
+    act(view("DUP2", 32, 64), view("i2"), F_.Identity, 1.0, col("p240"))
+    act(view("UNF"), view("inn"), F_.Identity, 32.0, col("q287"))
+    turn[0] = 0
 
-    def key_matrices():
-        tensor(None)
-        mm(view("Q0", 0, 16), view("BM"), view("rk"), True, True)
-        named("old")
-        act(view("KD"), view("Q0", 0, 16))
-        for k in range(16):
-            ts(mat("DG", k), view("I16"), view("KD", k, k + 1), A_.mult)
+    def key_differences():
+        def diagonals(k0, slots, by_scalar):
+            for k, slot in enumerate(slots.split(), k0):
+                named(slot)
+                if by_scalar:
+                    act(mat("DG", k), view("I16"), F_.Identity, view("KD", k, k + 1))
+                else:
+                    ts(mat("DG", k), view("I16"), view("KD", k, k + 1), A_.mult)
 
-    for k in range(10):
-        act(mat("KI", k), view("Ib"), scale=2 * k + 1)
-    for k in (10, 13):
-        three = view("KI", 128 * k, 128 * k + 384)
-        select(three, three, [[0, 3], [-1, 128]], A_.is_equal, 0.0)
+        diagonals(0, "old old old", True)
+        turn[0] += 1
+        named("mis")
+        act(view("KD", 8, 16), view("KN", 136, 144))
+        diagonals(8, "jk jk jk jk", True)
+        diagonals(12, "Nb Nb x7 x7", False)
+        diagonals(3, "l1 l2", True)
+        diagonals(5, "x5 x4 x4", False)
+        turn[0] -= 1
+
+    def differences():
+        for d in range(8):
+            named("")
+            ts(mat("RD", d), view("D"), view("tc", d, d + 1), A_.is_equal, 4096, A_.mult)
 
     def slot(r):
-        return (view("M2", r, 112, 7)[0], "slot%d" % r, 0, 16)
+        return (view("M2", r, None, SLOTS)[0], "slot%d" % r, 0, 16)
 
     def unpack(t, w):
         _, s_, U, F = state(t)
         named("U F s")
         low = part(w, 32, 48)
-        acti(part(U, 0, 16), low, view("REP", 0, 1), F_.Sign, bias=0.5 - 2 ** 16)
+        acti(U, low, view("REP", 0, 4), F_.Sign, bias=0.5 - 2 ** 16)
         acti(F, low, view("REP", 0, 4), F_.Identity, 2.0 ** -12, FO - 0.25)
         acti(s_, part(w, 0, 32), view("ODD", 0, 4), F_.Identity, bias=-32.0)
         if t < HOPS:
             named("sc")
-            act(view("SC", 32 * t, 32 * t + 32, 2), part(s_, 0, 16))
+            copy("sc", view("SC", 32 * t, 32 * t + 32, 2), part(s_, 0, 16))
 
-    def site_numbers(t, half, step):
-        a, b = ((0, 64), (64, 128), (128, 256))[half]
-        named("uyz"[half] + str(step))
+    def sites_of(t):
+        return view("H16", 256 * t, 256 * t + 256)
+
+    def site_numbers(t, piece, step, P, H):
+        a, b = ((0, 64), (64, 128), (128, 256), (0, 128))[piece]
+        named("uyzu"[piece] + str(step))
         if step == 0:
-            tt(view("Z", a, b), part(state(t)[0], a, b), view("E0", 256 + a, 256 + b), A_.mult)
+            tt(view("Z", a, b), part(P, a, b), view("DB" if a else "E0", 256 + a, 256 + b), A_.mult)
         elif step == 1:
             tt(view("ZI", a, b), view("Z", a, b), view("E1" if a >= 128 else "ZB", a, b), A_.add)
         elif step == 2:
             ts(view("HI", a, b), view("ZI", a, b), 5, A_.arith_shift_right, 2047, A_.bitwise_and)
         else:
-            (act if t and "uyz"[half] + "3" in ONS else cp)(view("H16", a, b), view("HI", a, b))
+            copy("uyzu"[piece] + "3" if t else "hp" if a else "", part(H, a, b), view("HI", a, b))
+
+    def spreads(t, half, s_, U1):
+        a, b = HALVES[half]
+        bank = ("ZB", "E1")[half]
+        tensor("32" + bank)
+        mm(view(("E0", "DB")[half], 256 + a, 256 + b), view("F25"), view("ONE", 0, 128), True)
+        tensor("s" + bank)
+        for x in (a, a + 64):
+            mm(view(("E0", "DB")[half], 256 + x, 320 + x), view("Ib"), s_, False, x > a)
+        tensor("keys" + bank)
+        mm(view(bank, a, b), view("BM16"), view(("KS", "KN")[half], 0, 128) if t else view("KTa", a, b), True)
+        if not t:
+            mm(view(bank, a, b), view("BM16"), view("KTa", a, b))
+        tensor("sU" + bank)
+        for x in (a, a + 64):
+            mm(view(bank, x, x + 64), view("I1184"), s_, False, not t and x > a)
+        for x in range(a, b if t else a, 16):
+            mm(view(bank, x, x + 16), mat("DG", x // 16), U1, False, x == b - 16)
+
+    def sites_ahead(t):
+        w, names_ = view("WS", 48 * t, 48 * t + 48), view("CO", 256 * t, 256 * t + 256)
+        named("sn Un")
+        acti(view("sn"), part(w, 0, 32), view("ODD", 0, 4), F_.Identity, bias=-32.0)
+        acti(view("Un"), part(w, 32, 48), view("REP", 0, 1), F_.Sign, bias=0.5 - 2 ** 16)
+        spreads(t + 1, 1, view("sn"), view("Un"))
+        for step in range(4):
+            site_numbers(t + 1, 2, step, names_, view("HS", 128 * t - 128, 128 * t + 128))
+        named("mh")
+        send(1, part(sites_of(t + 1), 128, 256), view("HS", 128 * t, 128 * t + 128), "mh%d" % t)
+        named("mb")
+        send(1, part(state(t + 1)[0], 128, 256), part(names_, 128, 256), "mb%d" % t)
 
     def sites(t):
         P, s_, U, pc = state(t)
@@ -489,19 +557,9 @@ def rank_program(g, core, T, topo):
         d = t % n
         if t:
             unpack(t, view("WL", 48 * t, 48 * t + 48))
-        tensor("32.")
-        mm(view("E0", 256, 512), view("F25"), view("ONE"), True)
-        tensor("s.")
-        spread("E0", 256, "Ib", s_, stop=True)
-        for bank, (a, b) in zip(("ZB", "E1"), HALVES):
-            tensor("keys" + bank)
-            mm(view(bank, a, b), view("BM16"), view("KTa", a, b), True)
-            mm(view(bank, a, b), view("BM16"), view("KTb" if t else "KTa", a, b))
-            tensor("sU" + bank)
-            for x in (a, a + 64):
-                mm(view(bank, x, x + 64), view("I1184"), s_, False, not t and x > a)
-            for x in range(a, b if t else a, 16):
-                mm(view(bank, x, x + 16), mat("DG", x // 16), U1, False, x == b - 16)
+        turn[0] -= not t
+        for half in range(1 if t else 2):
+            spreads(t, half, s_, U1)
         if t:
             tensor("AO.")
             mm(view("Q0", 0, 16), view("Ib"), view("LT"), True)
@@ -509,26 +567,30 @@ def rank_program(g, core, T, topo):
             named("AO AC AD")
             act(view("AO"), view("Q0", 0, 16))
             acti(record(t), view("AR", 512 * d, 512 * d + 512), view("AO"))
-            act(view("AC", 256, 512), record(t))
-        turn[0] -= not t
+            copy("AD", view("AC", 256, 512), record(t))
         for step in range(4):
-            for piece in range(3):
-                site_numbers(t, piece, step)
+            for piece in (3,) if t else (3, 2):
+                site_numbers(t, piece, step, P, sites_of(t))
         turn[0] += not t
-        for d, slot in enumerate(("z3", "PR", "h4", "hu") if not t else ()):
-            named("%s %s -" % (slot, slot))
-            differences(2 * d)
+        if not t:
+            differences()
         if t:
             tensor("SA.")
-            for k in range(16):
-                mm(view("Q1", 256 + 16 * k, 272 + 16 * k), mat("KI", k), U1, k == 0)
-            spread("Q1", 256, "N2", pc, stop=True)
-            for nm, f, c in (("SA", F_.Sign, 0.5), ("SB", F_.Sign, -0.5), ("R1", F_.Identity, RO)):
+            spread("Q1", 256, "N2", pc, True)
+            for k, eye in enumerate(("Ib", "I9", "I17", "I25")):
+                mm(view("Q1", 256 + 64 * k, 320 + 64 * k), view(eye), U)
+            for x in range(256, 512, 16):
+                if x % 64:
+                    mm(view("Q1", x, x + 16), view(("I2", "I4", "I6")[x % 64 // 16 - 1]), U1, False, x == 496)
+            for nm, f, c in (("SA", F_.Sign, 0.5), ("SB", F_.Abs, 0.0) if PRS else ("SB", F_.Sign, -0.5), ("R1", F_.Identity, RO)):
                 named(nm)
                 act(view(nm), view("Q1", 256, 512), f, 0.5, FO + 15.5 + c)
             tensor("PR.")
-            mm(view("ZB", 256, 512), view("Ih"), view("SA"), True)
-            mm(view("ZB", 256, 512), view("Nh"), view("SB"), False, True)
+            if PRS:
+                mm(view("ZB", 256, 512), view("N4k"), view("SB"), True)
+            else:
+                mm(view("ZB", 256, 512), view("Ih"), view("SA"), True)
+                mm(view("ZB", 256, 512), view("Nh"), view("SB"), False, True)
         tensor("pay.")
         mm(view("CB", 0, 256), view("Fhit"), view("ONE"), True)
         mm(view("CB", 240, 256), view("N64k"), view("ONE", 0, 16))
@@ -536,52 +598,55 @@ def rank_program(g, core, T, topo):
         spread("CB", 0, "I4k", pc)
         mm(view("CB", 240, 256), view("N64k"), U1)
         tensor("HK.")
-        mm(view("CB", 0, 256), view("I260k"), view("R1"), False, True)
+        mm(view("CB", 0, 256), view("I260k"), view("R1"))
         tensor("mask.")
         for x, r, s in ((0, "I4k", "N32k"), (256, "N4k", "I34k")):
             mm(view("RG", x, x + 256), view(r), view("R1"), not x)
             mm(view("RG", x, x + 256), view(s), view("SA" if t else "ONE"))
 
     def row_p(t):
-        named("PR HK" if t else "HK")
-        if t:
-            tt(view("PR"), view("HI"), view("ZB", 256, 512), A_.mult)
-        tt(view("HK"), view("HI"), view("CB", 0, 256), A_.add)
+        named("Hf PR HK" if t else "c0 HK")
+        copy("Hf" if t else "", view("Hf"), sites_of(t))
+        if t and PRS:
+            tensor("PS.")
+            mm(view("ZB", 256, 512), view("Ib"), view("Hf"), False, True)
+            act(view("PR"), view("ZB", 256, 512), F_.Relu)
+        elif t:
+            tt(view("PR"), sites_of(t), view("ZB", 256, 512), A_.mult)
+        tensor("Hf.")
+        mm(view("CB", 0, 256), view("Ib"), view("Hf"), False, True)
+        act(view("HK"), view("CB", 0, 256), F_.Identity, bias=HIT - 128 * HIT_SUM)
         tensor("hp.")
         if t:
             for k in range(4):
-                mm(view("CB", 288, 352), view("Ib"), view("PR", 64 * k, 64 * k + 64), k == 0, k == 3)
+                mm(view(PB, 288, 352), view("Ib"), view("PR", 64 * k, 64 * k + 64), k == 0, k == 3)
             named("h4")
-            (cp if "h4" in ONS else act)(view("h4"), view("CB", 288, 352))
+            copy("h4", view("h4"), view(PB, 288, 352))
             tensor("h4.")
             for k in range(4):
-                mm(view("CB", 272, 288), view("Ib"), view("h4", 16 * k, 16 * k + 16), k == 0, k == 3)
+                mm(view(PB, 272, 288), view("Ib"), view("h4", 16 * k, 16 * k + 16), k == 0, k == 3)
 
     def pairs_open(t):
         P, s_, U, pc = state(t)
-        hp = view("CB", 272, 288) if t else view("HI", 0, 16)
+        hp = view(PB, 272, 288) if t else view("H16", 0, 16)
         named("hp hu Mm HO HE" if t else "hp Mm HO HE")
+        copy("hp", view("hp"), hp)
         if t:
-            act(view("hp"), hp)
-            (act if "hu" in ONS else cp)(view("hu"), hp)
-        else:
-            acti(view("hp"), hp, view("REP", 0, 1))
-        o = view("CB", 256, 272)
+            copy("hu", view("hu"), view("hp") if COPIES.get("hu") == "g" else hp)
+        o = view(PB, 256, 272)
         tensor("Mm.")
-        mm(o, view("Fmiss"), view("ONE", 0, 16), True)
-        mm(o, view("N4k"), part(pc, 0, 16))
+        mm(o, view("N4k"), part(pc, 0, 16), True)
         mm(o, view("Ib"), view("hp"), False, True)
         for i in range(16):
-            mm(view("CB", 8 * i, 8 * i + 8, parts=8), view("Ib", i, 128, 16), view("hp", 1, 16, 2), i == 0, i == 15)
-        act(view("M", 16 * len(CHUNKS[0]), 16 * len(CHUNKS[0]) + 16), o)
-        (cp if "HO" in ONS else act)(view("HO", parts=8), view("CB", 0, 128, parts=8))
-        o = view("CB", 384, 512)
+            mm(view(PB, 8 * i, 8 * i + 8, parts=8), view("Ib", i, 128, 16), view("hp", 1, 16, 2), i == 0, i == 15)
+        act(slot(8), o, F_.Identity, bias=MISS)
+        copy("HO", view("HO", parts=8), view(PB, 0, 128, parts=8))
+        o = view(PB, 384, 512)
         tensor("HE.")
-        mm(o, view("Fmiss"), view("ONE", 0, 128), True)
         for k in range(4):
-            mm(part(o, 32 * k, 32 * k + 32), view("N4k"), view(pc[1], pc[2], pc[3], 2))
+            mm(part(o, 32 * k, 32 * k + 32), view("N4k"), view(pc[1], pc[2], pc[3], 2), k == 0)
         mm(o, view("G8", parts=8), view("HO", parts=8), False, True)
-        act(view("HE"), o)
+        act(view("HE"), o, F_.Identity, bias=MISS)
 
     def distances(t):
         kind, pairs = "".join(CHUNKS), [0]
@@ -590,7 +655,7 @@ def rank_program(g, core, T, topo):
             return view(buf, 256 * k, 256 * (k + m))
 
         def gather(k, m):
-            off = view("H16", 16 * k, 16 * (k + m))
+            off = part(sites_of(t), 16 * k, 16 * (k + m))
             if kind[k] == "S":
                 acti(span("DR", k, m), SITES, off)
             else:
@@ -608,63 +673,72 @@ def rank_program(g, core, T, topo):
                 act(span("DA", k, m), view(q, 0, 256 * m), F_.Abs)
             elif kind[k] == "A":
                 act(span("DA", k, m), span("DR", k, m), F_.Abs)
+            elif kind[k] == "H":
+                k0, rows = kind.index("H"), kind.count("H")
+                a = 256 * k0 + 128 * (k - k0)
+                act(view("DA", a, a + 128 * m), view("DR", 256 * k, 256 * (k + m), 2), F_.Abs)
+                a += 128 * rows
+                named("r%x" % k)
+                ts(view("DA", a, a + 128 * m), view("DR", 256 * k + 1, 256 * (k + m), 2), 0.0, A_.max, 2.0, A_.mult)
             else:
                 ts(span("DA", k, m), span("DR", k, m), 0.0, A_.max, 2.0, A_.mult)
 
         def decide(c):
             kinds, k0 = CHUNKS[c], len("".join(CHUNKS[:c]))
             rows = len(kinds)
-            bank = BANKS[c]
-            e = view(bank, 0, 16 * rows)
+            e = view(BANKS[c], 0, 64)
             tensor("D%d." % c)
-            mm(e, view("TH"), view("C32k", 0, 16 * rows), True)
-            if "R" in kinds:
+            mm(e, view("TH"), view("C32k"), True)
+            for i in range(16 if "R" in kinds else 0):
                 a, b = kinds.index("R"), kinds.rindex("R") + 1
-                for i in range(16):
-                    mm(view(bank, 16 * a, 16 * b), view("LP", 15 - i, 143 - i), view("DR", 256 * (k0 + a) + i, 256 * (k0 + b), 16))
+                mm(part(e, 16 * a, 16 * b), view("LP", 15 - i, 143 - i), view("DR", 256 * (k0 + a) + i, 256 * (k0 + b), 16))
+            if "H" in kinds:
+                tensor("L%d." % c)
+                for i in range(1, 16, 2):
+                    mm(e, view("LP", 15 - i, 143 - i), view("DR", 256 * k0 + i, 256 * (k0 + rows), 16))
+                for odd in (1, 0):
+                    tensor("EO"[odd] + "%d." % c)
+                    a = 256 * k0 + 128 * rows * odd
+                    for i in range(odd, 16, 2):
+                        mm(e, view("LE", 15 - i, 143 - i), view("DA", a + i // 2, a + 128 * rows, 8), False, i == 14)
+                return
             tensor("E%d." % c)
             for i in range(16):
                 mm(e, view("LE", 15 - i, 143 - i), view("DA", 256 * k0 + i, 256 * (k0 + rows), 16), False, i == 15)
 
         def choose(c, step):
-            k0, rows = len("".join(CHUNKS[:c])), len(CHUNKS[c])
-            e, hk = view(BANKS[c], 0, 16 * rows), view("HK", 16 * k0, 16 * (k0 + rows))
+            rows, e, hk = 4, view(BANKS[c], 0, 64), view("HK", 64 * c, 64 * c + 64)
             if step == "m":
-                tt(e if c else view("M", 0, 16 * rows), e, hk, A_.min)
-            if step == "x" and c == 1:
-                tt(view("M", 0, 64), e, view("M", 0, 64), A_.max)
+                tt(e if c else view("M"), e, hk, A_.min)
             elif step == "x":
-                for r in range(4):
-                    tt(slot(3 + r), part(e, 16 * r, 16 * r + 16), view("M", 16 * r, 16 * r + 16), A_.max)
-            elif step == "w":
+                tt(view("M"), e, view("M"), A_.max)
+            elif step == "f":
+                for r in range(rows):
+                    tt(slot(4 + r), part(e, 16 * r, 16 * r + 16), view("M", 16 * r, 16 * r + 16), A_.max)
+            else:
                 for r in range(rows):
                     tt(slot(r), part(e, 16 * r, 16 * r + 16), part(hk, 16 * r, 16 * r + 16), A_.min)
                 call("v", lambda: g.vector.tensor_tensor_scan(T.W[:], T.K3[:], T.M2[:], 0.0, A_.mult, A_.max), [view("W")],
-                     [view("K3")] + [slot(r) for r in range(7)], 112 * CYCLE)
-
-        def fold(k):
-            tt(view("M", 0, 32), view("M", 0, 32), view("M", 64, 96), A_.max)
+                     [view("K3")] + [slot(r) for r in range(SLOTS)], 16 * SLOTS * CYCLE)
 
         for step in STEPS.split():
             k = int(step[1], 16)
-            if step[0] in "gGabcfm":
+            if step[0] in "GHbcm":
                 named(step)
-            elif step[0] in "xw":
-                named({"x1": "x1m", "x2": "xa xb xc xd", "w3": "wa wb wc w2"}[step])
-            if step[0] in "gG":
-                gather(k, 1 + (step[0] == "G"))
+            elif step[0] in "xwf":
+                named({"x": "xm", "f": "xa xb xc xd", "w": "wa wb wc wd w2"}[step[0]])
+            if step[0] in "GH":
+                gather(k, 2 if step[0] == "G" else 4)
             elif step[0] == "d":
                 decide(k)
-            elif step[0] == "f":
-                fold(k)
-            elif step[0] in "mxw":
+            elif step[0] in "mfxw":
                 choose(k, step[0])
             elif step[0] == "h":
                 row_p(t)
             elif step[0] == "p":
                 pairs_open(t)
             else:
-                size(k, " abc".index(step[0]))
+                size(k, 2 if step[0] == "b" else 4)
 
     def writes(t):
         if t:
@@ -675,7 +749,8 @@ def rank_program(g, core, T, topo):
         if t:
             mm(view("E1", 256, 512), view("Ib"), view("old"), False, True)
         else:
-            mm(view("E1", 256, 512), view("Ib"), record(t))
+            if CHUNKS[0][0] != "S":
+                mm(view("E1", 256, 512), view("Ib"), record(t))
             mm(view("E1", 256, 512), view("Ib"), view("DR", 0, 256), False, True)
         tensor("pairs.")
         for d in range(8):
@@ -707,8 +782,8 @@ def rank_program(g, core, T, topo):
         named("mis jk l1 l2 l3 TH")
         act(view("mis"), view("G4", 0, 16), F_.Relu, -1.0 / 4096, GO + 1.0)
         tensor("jk.")
-        mm(view("E1", 64, 80), view("ONE", 0, 128), view("mis"), True, True)
-        act(view("jk"), view("E1", 64, 80), F_.Identity, bias=-7.5 / 16, acc=col("mc"))
+        mm(view("Q0", 64, 80), view("ONE", 0, 128), view("mis"), True, True)
+        act(view("jk"), view("Q0", 64, 80), F_.Identity, bias=-7.5 / 16, acc=col("mc"))
         act(col("m1"), col("mc"), F_.Identity, bias=ROUND16)
         act(col("m2"), col("m1"), F_.Identity, -1.0, ROUND16)
         act(col("m3"), col("m2"), F_.Identity, bias=74.5)
@@ -717,8 +792,8 @@ def rank_program(g, core, T, topo):
     def become(t, names_):
         P = state(t)[0]
         named("hs low sf bq")
-        ts(view("WS", 48 * t + 1, 48 * t + 32, 2), view("W", 6, 112, 7), 4095, A_.bitwise_and)
-        ts(view("WS", 48 * t + 32, 48 * t + 48), view("W", 6, 112, 7), 2 ** 17 - 1, A_.bitwise_and)
+        ts(view("WS", 48 * t + 1, 48 * t + 32, 2), view("W", SLOTS - 1, None, SLOTS), 4095, A_.bitwise_and)
+        ts(view("WS", 48 * t + 32, 48 * t + 48), view("W", SLOTS - 1, None, SLOTS), 2 ** 17 - 1, A_.bitwise_and)
         o, d0, d1 = view("sh", 0, 32), view("WS", 48 * t, 48 * t + 32), view("SC", 32 * t, 32 * t + 32)
         call("v", lambda: g.vector.tensor_tensor_scan(o[0], d0[0], d1[0], 0.0, A_.mult, A_.add), [o], [d0, d1], 64 * CYCLE)
         tsi(view("bq"), o, view("ODD", 0, 4), 5, A_.arith_shift_right, 2047, A_.bitwise_and)
@@ -726,8 +801,8 @@ def rank_program(g, core, T, topo):
         spread("RG", 0, "Nh", view("G4"))
         spread("RG", 256, "Ih", view("G4"), stop=True)
         tensor(None)
-        fold = FOLD and t < HOPS - 1
         for a, b in HALVES:
+            fold = t < HOPS - 1 and not a
             named(("Pb t2 t3" if a else "Pa t0 t1") + ("" if fold else " Nb" if a else " Na"))
             tt(part(names_, a, b) if fold else view("RG", a, b), part(P, a, b), view("RG", a, b), A_.min)
             for x in range(a, b, 64):
@@ -764,22 +839,24 @@ def rank_program(g, core, T, topo):
         store("y", T.yx[:], SITES, "oy")
 
     sites(0)
+    named("ms")
+    send(-1, view("KN"), view("KS", 128, 272), "kn", [SITES])
     for t in range(HOPS):
         if t < n - 1:
-            send(t + 1, view("AR", 512 * t + 512, 512 * t + 1024), view("AR", 0, 512), "ar%d" % (t + 1), [view("H16", 0, 64)])
+            named("" if t else "ma")
+            send(t + 1, view("AR", 512 * t + 512, 512 * t + 1024), view("AR", 0, 512), "ar%d" % (t + 1), [part(sites_of(t), 0, 64)])
         distances(t)
         if not t:
-            key_matrices()
+            key_differences()
         writes(t)
         if t < HOPS - 1:
             limit()
             become(t, view("CO", 256 * t, 256 * t + 256))
             named("ms")
             send(1, view("WL", 48 * t + 48, 48 * t + 96), view("WS", 48 * t, 48 * t + 48), "ms%d" % t)
-            for a, b, sem in PIECES:
-                named(sem)
-                send(1, part(state(t + 1)[0], a, b), view("CO", 256 * t + a, 256 * t + b), sem + str(t),
-                     other=view("CP", 256 * t + a, 256 * t + b) if FOLD else None)
+            named("ma")
+            send(1, part(state(t + 1)[0], 0, 128), view("CO", 256 * t, 256 * t + 128), "ma%d" % t, other=view("CP", 256 * t, 256 * t + 128))
+            sites_ahead(t)
             sites(t + 1)
         else:
             become(t, view("Pf"))

from concourse.bass import DstId, RemoteDMATransfer
from concourse.mybir import AluOpType, ActivationFunctionType

A_ = AluOpType
F_ = ActivationFunctionType
HOPS = 7
NX = 2080
BIG = 2.0 ** 22
ROUND16 = 1.5 * 2 ** 27
CHUNKS = ("RRRR", "SSSS", "AASS", "HHHH")
SLOTS = 9
STEPS = "h0 G0 G2 c0 d0 p0 m0 G4 b4 G6 b6 d1 m1 x1 G8 b8 Ga ba d2 m2 f2 Gc bc Ge be d3 w3"
CYCLE, GATHER, SCATTER, COLUMN, HOPLAT, LINK, DMALAT, DMABW = 0.87e-3, 1.15e-3, 2.6e-3, 0.43e-3, 1.5, 150e3, 1.8, 300e3
ACT, VFIX, WAKE, WSAME = 0.05, 0.04, 0.14, 0.2
COPIES = {"hu": "g", "Hf": "g", "z3": "g", "sc": "g", "hp": "s", "HO": "s", "h4": "s", "AD": "s"}
PRS = False
PASSES = 4
BANKS = ("E0", "E1", "Q1", "Q0")
PB = "ZB"
ORDER, SPAN = [], []
TURNS = ("hs low sf ex bq eq Pa t0 t1 t2 t3 Pb fo Nb x7 z0 x6 z1 x5 z2 x4 x3 u0 x2 u1 x1 u2 x0 u3 "
         "G0 G2 PR G8 c0 Ge Gc re rc m0 m1 xm m2 xa xb xc xd wa wb wc wd w2 "
         "GW n1 mis sn Un jk l1 l2 U s F l3 AO TH AC R1 SA AD SB G4 G6 Ga b4 b6 h4 b8 ba HK hp be bc HO Mm old sd HE "
         "ms ma z3 mh mb sc Hf hu "
         "eq. Pa. jk. ex. fo. 32ZB keysZB keysE1 32E1 sE1 sUE1 AO. sZB SA. sUZB A4. mask. pay. Aa. payF. PR. D1. HK. X4. A6. X6. "
         "hp. D0. Xa. Hf. E0. h4. D2. E1. D3. L3. E2. Mm. O3. E3. pairs. HE. hq. n1.")
LAST = ("hs low sf ex bq sp y1 eq sq t0 t1 t2 t3 Pb Pa fo Nb x7 Na x6 x5 x4 x3 x2 Td x1 Tb x0 Ta Tc "
        "GW s U F n1 so Dd Db Da Dc Uo Un eq. Pa. ex. fo. U. sp.")
EYES = {"I1184": 1184.0, "I4k": 4096.0, "N64k": -2.0 ** 16, "I260k": 2.0 ** 18 + 4096, "I16": 16.0, "N4k": -4096.0, "NI": -1.0,
        "N128": -128.0, "N32k": -32768.0, "I34k": 34816.0, "Ih": 0.5, "Nh": -0.5, "N2": -2.0, "I9": 9.0, "I17": 17.0, "I25": 25.0,
        "I2": 2.0, "I4": 4.0, "I6": 6.0}
FO = GO = 192
RO = GO // 2 + 8
HIT, MISS = 2 ** 17 + 4096 + 32 - FO * 4096 - RO * EYES["I260k"], (FO + 31) * 4096 + 32.0
HIT_SUM = round(HIT / 2 ** 17) * 1024.0
SIZE = {"float32": 4, "int32": 4, "bfloat16": 2, "float16": 2, "uint16": 2}

SCRATCH = {}
PART = {}


def _shared(buf, dtype, width, names):
    SCRATCH[buf] = ("sbuf", [128, width * len(names)], dtype)
    for k, n in enumerate(names):
        PART[n] = (buf, width * k, width)


_shared("eyes", "bfloat16", 128, ["Ib"] + list(EYES))
_shared("cols", "float32", 4, ("p16", "c3", "c4", "p256", "q287", "pa", "pb", "p128", "p240", "kf", "pc", "mc", "m1", "m2", "m3"))
_shared("LL", "bfloat16", 144, ("LE", "LP"))
_shared("i64", "int32", 64, ("sh", "bq"))
_shared("f64", "float32", 64, ("fa", "sf"))
_shared("u32", "uint16", 32, ("DUP1", "fo"))
_shared("u16", "uint16", 16, ("UN1", "UN2", "AO", "hu", "REP", "R32", "EV", "ODD", "R4"))
_shared("i16", "int32", 16, ("inn", "ip", "q15", "q31i", "q7", "qo", "qv", "qw", "qe"))
_shared("f8", "float32", 8, ("td", "te", "tg", "tc", "tw", "th"))
_shared("b128", "bfloat16", 128, ("BM", "BM16", "D", "G8", "F25", "Fhit", "TH", "eq", "ex"))
for _n, _w, _d in (
    ("X", NX, "bfloat16"), ("AR", 2048, "bfloat16"), ("DR", 4096, "bfloat16"), ("DA", 4096, "bfloat16"),
    ("SH", 1024, "bfloat16"), ("RD", 1024, "bfloat16"),
    ("KD", 16, "float32"), ("rk", 16, "float16"), ("DG", 2048, "float16"),
    ("ST", 320 * (HOPS + 1), "float16"), ("CO", 256 * HOPS, "float16"), ("CP", 256 * HOPS, "float16"), ("W", 16 * SLOTS, "int32"), ("K3", 16 * SLOTS, "bfloat16"),
    ("CGO", 16, "bfloat16"), ("DUM", 16, "float32"),
    ("WS", 48 * HOPS, "int32"), ("WL", 48 * HOPS, "int32"), ("M", 64, "float32"), ("M2", 16 * SLOTS, "float32"),
    ("PI", 272, "int32"), ("PT", 512, "int32"), ("SI", 32, "int32"), ("SJ", 32, "int32"), ("KA", 1, "int32"), ("TA", 1024, "float32"), ("TB", 1024, "float32"),
    ("DUP2", 64, "uint16"), ("UNF", 16, "float16"),
    ("i2", 32, "int32"), ("ONE", 256, "bfloat16"), ("C32k", 64, "bfloat16"),
    ("LT", 16, "float16"), ("KTa", 256, "float16"), ("KS", 272, "float16"), ("KN", 144, "float16"), ("RS", 256, "bfloat16"), ("kb", 16, "float16"),
    ("HS", 128 * HOPS, "uint16"), ("sn", 64, "float16"), ("Un", 16, "bfloat16"),
    ("AC", 512, "bfloat16"), ("R1", 256, "bfloat16"), ("SA", 256, "bfloat16"), ("SB", 256, "bfloat16"),
    ("Z", 256, "float32"), ("ZI", 256, "int32"), ("HI", 256, "int32"), ("H16", 256 * HOPS, "uint16"), ("HK", 256, "float32"), ("PR", 256, "float16"), ("Hf", 256, "float16"),
    ("hp", 16, "float16"), ("h4", 64, "float16"), ("SC", 32 * HOPS, "float32"), ("G4", 64, "bfloat16"), ("mis", 16, "bfloat16"), ("C128", 32, "bfloat16"), ("UF", 128 * (HOPS + 1), "bfloat16"),
    ("old", 256, "bfloat16"), ("n1", 256, "bfloat16"), ("tP", 256, "float32"),
    ("hf", 16, "float32"), ("HE", 128, "float32"), ("HO", 128, "float16"), ("jk", 16, "float32"),
    ("Pf", 256, "float32"), ("yl", 256, "float32"),
    ("y1", 16, "float32"), ("sp", 32, "float16"), ("so", 512, "float32"),
):
    SCRATCH[_n] = ("sbuf", [128, _w], _d)
PS = ("E0", "E1", "Q0", "Q1", "ZB", "CB", "RG", "DB")
for _n in PS:
    SCRATCH[_n] = ("psum", [128, 512], "float32")

SEMAPHORES = (["qv", "qs", "qp", "qg", "snd", "lx", "la", "lr", "lk", "lz", "lp", "oy", "oz"]
              + [m + str(t) for m in ("ma", "mb", "ms", "mh") for t in range(HOPS - 1)] + ["ar%d" % d for d in (1, 2, 3)] + ["kn"])


def needs(calls):
    pre = [dict() for _ in calls]
    log, bank, sender = {}, {}, {}
    for k, c in enumerate(calls):
        def after(j, wait=True):
            gap = calls[j]["done"] + (WSAME if calls[j]["q"] == c["q"] else WAKE) if wait else 0.0
            pre[k][j] = max(pre[k].get(j, 0.0), gap)
        if c["kind"] == "send":
            sender[c["sem"]] = k
        if c["kind"] == "land":
            pre[k][sender[c["sem"]]] = calls[sender[c["sem"]]]["done"]
        for vs, wr in ((c["ins"], False), (c["outs"], True)):
            for _, nm, a, b in vs:
                for a2, b2, w2, j in log.get(nm, []):
                    if j != k and a < b2 and a2 < b and (wr or w2):
                        after(j, not calls[j]["q"] == c["q"] == "p")
                if nm in PS:
                    old, cur = bank.get(nm, ([], []))
                    if cur and calls[cur[0]]["q"] != c["q"]:
                        old, cur = cur, []
                    for j in old:
                        after(j)
                    if c["q"] == "p" and cur and cur[-1] != k:
                        after(cur[-1], False)
                    bank[nm] = (old, cur + [k])
        for vs, wr in ((c["ins"], False), (c["outs"], True)):
            for _, nm, a, b in vs:
                keep = [e for e in log.get(nm, []) if not (wr and a <= e[0] and e[1] <= b)]
                log[nm] = keep + [(a, b, wr, k)]
    return pre


def plan(calls, pre):
    n = len(calls)
    place = {nm: x for x, nm in enumerate(["first"] + TURNS.split() + [x + "!" for x in LAST.split()])}
    for q in "vsgp":
        named = sorted((c["name"][0], place[c["name"][1]], k) for k, c in enumerate(calls) if c["q"] == q and c["name"] and c["name"][1] in place)
        for (_, _, j), (_, _, k) in zip(named, named[1:]):
            pre[k][j] = max(pre[k].get(j, 0.0), calls[j]["hold"])
    hold, queue = [c["hold"] for c in calls], [c["q"] for c in calls]
    tail = [c["done"] - c["hold"] for c in calls]
    ahead, back = [[] for _ in calls], [[] for _ in calls]
    for k in range(n):
        for j, gap in pre[k].items():
            ahead[j].append((k, gap))
            back[k].append((j, gap + hold[k] - hold[j]))

    def run(post, first, rest):
        left, start, free, out = [0] * n, list(first), {}, []
        for k in range(n):
            for j, _ in post[k]:
                left[j] += 1
        ready = {q: [k for k in range(n) if queue[k] == q and not left[k]] for q in set(queue)}
        head = {}

        def at(k):
            return max(start[k], free.get(queue[k], 0.0))
        while len(out) < n:
            for q in ready:
                if q not in head and ready[q]:
                    head[q] = min((at(k), -rest[k], k) for k in ready[q])
            a = min(head.values())[2]
            for b in ready[queue[a]]:
                if rest[b] > rest[a] and at(b) < at(a) + hold[a]:
                    if max(at(b) + rest[b], at(b) + hold[b] + rest[a]) < max(at(a) + rest[a], at(a) + hold[a] + rest[b]):
                        a = b
            ready[queue[a]].remove(a)
            del head[queue[a]]
            start[a] = at(a)
            free[queue[a]] = start[a] + hold[a]
            out.append(a)
            for j, gap in post[a]:
                start[j] = max(start[j], start[a] + gap)
                left[j] -= 1
                if not left[j]:
                    ready[queue[j]].append(j)
                    head.pop(queue[j], None)
        return out, [start[k] + hold[k] for k in range(n)]

    rest, left = [0.0] * n, [len(a) for a in ahead]
    todo = [k for k in range(n) if not left[k]]
    for k in todo:
        rest[k] = max([calls[k]["done"]] + [max(gap, hold[k]) + rest[j] for j, gap in ahead[k]])
        for j, _ in back[k]:
            left[j] -= 1
            if not left[j]:
                todo.append(j)
    assert len(todo) == n, [calls[k]["name"] for k in range(n) if left[k]][-40:]
    best = None
    for _ in range(PASSES):
        out, end = run(ahead, [0.0] * n, rest)
        span = max(end[k] + tail[k] for k in range(n))
        if best is None or span < best[0]:
            best = (span, out)
        rest = run(back, tail, end)[1]
    SPAN[:] = [best[0]]
    return best[1]


def rank_program(g, core, T, topo):
    rank = T.rank_of(core)
    if rank is None:
        return
    n = len(T.cores)
    nxt, prv = T.cores[(rank + 1) % n], T.cores[(rank - 1) % n]
    Q = {"v": g.vector, "s": g.scalar, "p": g.tensor, "g": g, "y": g.sync}
    QS = {"v": "qv", "s": "qs", "p": "qp", "g": "qg"}
    calls, names, block, turn = [], [], [None], [0]

    def view(name, a=0, b=None, st=1, parts=128, p0=0):
        if name in PART:
            name, o, w = PART[name]
            a, b = o + a, o + (w if b is None else b)
        b = SCRATCH[name][1][1] if b is None else b
        ap = T[name][p0:p0 + parts, a:b] if st == 1 else T[name][p0:p0 + parts, a:b:st]
        return (ap, name, a, b)

    def col(name):
        return view(name, 0, 1)

    def width(v):
        return v[0].shape[1]

    def nbytes(v):
        return v[0].shape[0] * width(v) * SIZE[SCRATCH[v[1]][2]]

    def call(q, fn, outs, ins, hold, done=None, kind="compute", sem=None, count=0):
        name = (turn[0], names.pop(0)) if names and q in "vsg" else (turn[0], block[0]) if q == "p" else None
        if turn[0] < 0:
            name = (-1, "first")
        if turn[0] == HOPS and name:
            name = (HOPS, "%s!" % name[1])
        calls.append(dict(q=q, fn=fn, outs=outs, ins=ins, hold=hold, done=hold if done is None else done, kind=kind, sem=sem, count=count,
                          name=name))

    def named(text):
        assert not names
        names.extend(text.split())

    def tensor(name):
        block[0] = name

    def vcost(o, a):
        half = SIZE[SCRATCH[a[1]][2]] == 2 and SIZE[SCRATCH[o[1]][2]] == 2
        return VFIX + CYCLE * max(64, width(a) * (0.5 if half else 1))

    def tt(o, a, b, op):
        call("v", lambda: g.vector.tensor_tensor(o[0], a[0], b[0], op), [o], [a, b],
             VFIX + CYCLE * max(64, width(a) * (1 if a[1] in PS or b[1] in PS else 2)))

    def tti(o, win, off, b, op):
        call("v", lambda: g.vector.tensor_tensor(o[0], win[0].indirect(off[0]), b[0], op), [o], [win, off, b], 0.05 + GATHER * width(o))

    def ts(o, a, s1, op0, s2=None, op1=None):
        cs = [s for s in (s1, s2) if isinstance(s, tuple)]
        x1, x2 = (s[0] if isinstance(s, tuple) else s for s in (s1, s2))
        if op1 is None:
            f = lambda: g.vector.tensor_scalar(o[0], a[0], x1, None, op0)
        else:
            f = lambda: g.vector.tensor_scalar(o[0], a[0], x1, x2, op0, op1)
        call("v", f, [o], [a] + cs, vcost(o, a))

    def cp(o, a):
        call("v", lambda: g.vector.tensor_copy(o[0], a[0]), [o], [a], vcost(o, a))

    def cpi(o, win, off):
        call("v", lambda: g.vector.tensor_copy(o[0], win[0].indirect(off[0])), [o], [win, off], 0.05 + GATHER * width(o))

    def tsi(o, win, off, s1, op0, s2=None, op1=None):
        more = () if op1 is None else (op1,)
        call("v", lambda: g.vector.tensor_scalar(o[0], win[0].indirect(off[0]), s1, s2, op0, *more), [o], [win, off], 0.05 + GATHER * width(o))

    def scat(win, off, a, b):
        call("v", lambda: g.vector.tensor_tensor(win[0].indirect(off[0]), a[0], b[0], A_.add), [win], [off, a, b], 0.05 + SCATTER * width(a))

    def select(o, a, pattern, op, fill, base=0, step=1):
        call("g", lambda: g.affine_select(o[0], a[0], pattern, op, fill, base, step), [o], [a], 0.17 + 2 * CYCLE * width(o))

    def turn32(o, a):
        call("v", lambda: g.vector.transpose(o[0], a[0]), [o], [a], vcost(o, a))

    def ms(o, c):
        call("v", lambda: g.vector.memset(o[0], c), [o], [], vcost(o, o))

    def act(o, a, f=F_.Copy, scale=1.0, bias=0.0, acc=None):
        cs = [s for s in (scale, bias) if isinstance(s, tuple)]
        sc, bi = (s[0] if isinstance(s, tuple) else s for s in (scale, bias))
        if acc is None:
            call("s", lambda: g.scalar.activation(o[0], a[0], f, bias=bi, scale=sc), [o], [a] + cs, ACT + CYCLE * width(a))
        else:
            call("s", lambda: g.scalar.activation(o[0], a[0], f, bias=bi, scale=sc, accum_out=acc[0]), [o, acc], [a] + cs,
                 0.2 + CYCLE * width(a))

    def acti(o, win, off, f=F_.Copy, scale=1.0, bias=0.0):
        call("s", lambda: g.scalar.activation(o[0], win[0].indirect(off[0]), f, bias=bias, scale=scale), [o], [win, off], 0.065 + GATHER * width(o))

    def copy(name, o, a):
        q = COPIES.get(name, "v")
        if q == "g":
            select(o, a, [[0, width(o)]], A_.is_equal, 0.0, 0, 0)
        else:
            (cp if q == "v" else act)(o, a)

    def mm(o, l, r, start=False, stop=False):
        call("p", lambda: g.tensor.matmul(o[0], l[0], r[0], start, stop), [o], [l, r], COLUMN * max(min(64, width(l)), width(r)))

    def spread(bank, a, l, r, start=False, stop=False):
        for k in range(4):
            mm(view(bank, a + 64 * k, a + 64 * k + 64), view(l), r, start and k == 0, stop and k == 3)

    def iota(o, pat, base, cm):
        call("g", lambda: g.iota(o[0], pat, base, cm, allow_small_or_imprecise_dtypes=True), [o], [], 0.13 + 2 * CYCLE * width(o))

    def load(q, o, src, sem):
        call(q, lambda: Q[q].dma_start(o[0], src), [o], [], 0.05, DMALAT + nbytes(o) / DMABW, "dma", sem, 16)

    def store(q, out, a, sem):
        call(q, lambda: Q[q].dma_start(out, a[0]), [], [a], 0.05, DMALAT + nbytes(a) / DMABW, "dma", sem, 16)

    def send(d, o, a, sem, also=(), other=None):
        dst, src = T.cores[(rank + d) % n], T.cores[(rank - d) % n]
        rid, pid = topo.addr(dst, core)
        if other is None:
            f = lambda: g.remote_dma(o[0], a[0], T.sem[sem], T.sem.snd, pid, rid, topo.mask(core, dst))
        else:
            also = [other]
            f = lambda: g.remote_dma_fused([RemoteDMATransfer(dst_ids=[DstId(rid=rid, pnc=pid)], dma_engine_mask=topo.mask(core, dst),
                                                              remote_sem=T.sem[sem], srcs=[a[0], other[0]], dsts=[o[0]], alu_op=2)],
                                           local_sem=T.sem.snd)
        call("g", f, [], [a] + list(also), 0.4, 0.4 + HOPLAT + nbytes(a) / LINK, "send", sem, len(topo.engines(core, dst)))
        call("rem", None, [o], [], 0.0, 0.0, "land", sem, len(topo.engines(src, core)))

    def mat(name, k):
        return view(name, 128 * k, 128 * k + 128)

    def state(t):
        return (view("ST", 320 * t, 320 * t + 256), view("ST", 320 * t + 256, 320 * t + 320),
                view("UF", 128 * t, 128 * t + 64), view("UF", 128 * t + 64, 128 * t + 128))

    def record(t):
        return view("AC", 0, 256)

    def part(v, a, b):
        return view(v[1], v[2] + a, v[2] + b)

    SITES = view("X", 0, 2048)
    HALVES = ((0, 128), (128, 256))

    load("y", view("PI", 0, 256), T.pn[:], "lp")
    load("s", view("SI", 0, 16), T.s0[:], "lz")
    load("s", view("KA"), T.kap[:], "lk")
    load("s", view("AR", 0, 256), T.a0[:], "la")
    load("y", SITES, T.x[:], "lx")
    load("y", view("AR", 256, 512), T.r0[:], "lr")

    P0, s0_, U0, p0 = state(0)
    ONES = view("ONE", 0, 128)
    turn[0] = -1
    ms(view("ONE"), 1.0)
    iota(view("ip"), [[0, 16]], 0, 1)
    iota(view("inn"), [[1, 16]], 0, 0)
    iota(view("D"), [[1, 128]], 0, -1)
    iota(view("td"), [[1, 8]], 1, 0)
    select(view("BM"), ONES, [[-16, 8], [0, 16]], A_.is_ge, 0.0)
    iota(view("R1"), [[1, 16], [0, 16]], RO, 0)
    select(view("BM"), view("BM"), [[16, 8], [0, 16]], A_.is_ge, 0.0, 15, -1)
    ts(view("q15"), view("ip"), 15, A_.bitwise_and)
    ts(view("q31i"), view("ip"), 31, A_.bitwise_and)
    ts(view("qo"), view("ip"), 4, A_.arith_shift_right, 1, A_.bitwise_and)
    ms(view("LL"), 0.0)
    act(view("F25"), ONES, scale=0.25)
    act(view("TH"), ONES, scale=67.0)
    for nm, m, c in (("p16", 1, 0), ("pb", -1, 15), ("pa", 1, RO)):
        act(col(nm), col("q15"), F_.Identity, float(m), float(c))
    act(col("pc"), col("q15"), F_.Abs, 2.0, -15.0)
    act(col("p128"), col("q15"), F_.Identity, 1.0, 128.0)
    tt(view("qv"), view("q31i"), view("qo"), A_.subtract)
    ts(view("Ib"), view("D"), 0, A_.is_equal)
    cp(view("R32"), view("q31i"))
    ts(view("qw"), view("qv"), 15, A_.bitwise_and)
    ts(view("qe"), view("qv"), 1, A_.bitwise_and)
    ts(view("tw"), view("td"), col("pb"), A_.is_gt, -16, A_.mult)
    ts(view("I1184"), view("Ib"), EYES["I1184"], A_.mult)
    tt(view("qv"), view("qw"), view("qo"), A_.add)
    ts(col("c3"), col("qe"), 15, A_.mult)
    tt(view("th"), view("tw"), view("td"), A_.add)
    ms(view("C32k"), 32768.0)
    ts(col("c4"), col("qv"), col("c3"), A_.add, 16, A_.mult)

    def shifts(a, b):
        for d in range(a, b):
            ts(mat("SH", d), view("D"), view("th", d, d + 1), A_.is_equal)

    def eyes(text):
        for nm in text.split():
            act(view(nm), view("Ib"), scale=EYES[nm])

    def diagonal(text):
        for nm in text.split():
            select(view(nm), view("Ib"), [[-1, 128]], A_.not_equal, EYES[nm])

    iota(view("RS", 0, 128), [[-2, 8], [0, 16]], 15, 0)
    iota(view("RS", 128, 256), [[2, 8], [0, 16]], 1, 0)
    iota(view("te"), [[-1, 8]], 15, 0)
    eyes("NI N64k I4k I260k")
    shifts(0, 2)
    ts(view("UN1"), view("inn"), col("c4"), A_.add)
    shifts(2, 4)
    act(view("SI", 16, 32), view("SI", 0, 16))
    act(col("kf"), view("KA"))
    act(view("BM16"), view("BM"), scale=16.0)
    turn32(view("SJ"), view("SI"))
    shifts(4, 5)
    ts(view("KTa"), view("R1"), col("pa"), A_.is_equal, col("kf"), A_.mult)
    acti(s0_, view("SJ"), view("R32", 0, 4))
    shifts(5, 6)
    act(view("PI", 256, 272), view("PI", 0, 16))
    act(view("AC", 0, 256), view("AR", 0, 256))
    act(view("AC", 256, 512), view("AR", 0, 256))
    turn32(view("PT", 0, 256), view("PI", 0, 256))
    turn32(view("PT", 256, 512), view("PI", 16, 272))
    shifts(6, 8)
    ts(view("kb"), view("inn"), col("pb"), A_.is_equal, col("kf"), A_.mult)
    cpi(part(P0, 0, 128), view("PT"), view("UN1", 0, 8))
    acti(part(P0, 128, 256), view("PT"), view("UN1", 8, 16))
    tt(view("rk"), view("KTa", 0, 256, 16), view("kb"), A_.subtract)
    ts(view("q7"), view("ip"), 7, A_.bitwise_and)
    ts(view("KS", 0, 256), view("RS"), col("pc"), A_.is_equal, col("kf"), A_.mult)
    for half in range(2):
        four = view("SH", 512 * half, 512 * half + 512)
        select(four, four, [[0, 4], [-1, 128]], A_.not_equal, -1.0)
    act(view("LE", 15, 143, 16), view("BM", 0, 128, 16), scale=-BIG)
    act(view("LP", 15, 143, 16), view("BM", 0, 128, 16), scale=BIG)
    for o, c in ((U0, 1.0), (p0, FO + 16.0), (view("Fhit"), HIT_SUM)):
        act(o, view("ONE", 0, width(o)), scale=c)
    turn[0] = 0
    tensor("A4.")
    mm(view("Q1", 0, 16), view("BM"), view("rk"), True, True)
    turn[0] = -1
    act(view("KS", 256, 272), view("Q1", 0, 16))
    act(view("KD", 0, 8), view("Q1", 0, 8))
    eyes("N4k N32k I34k")
    turn[0] = 0
    named("sd sd sd")
    for nm, src, m, c in (("R4", "q15", SLOTS, SLOTS - 1), ("EV", "q7", 2 * SLOTS, SLOTS - 1), ("ODD", "q15", 2, 1)):
        act(view(nm), view(src), F_.Identity, float(m), float(c))
    named("hp")
    eyes("I16")
    ts(view("tg"), view("td"), col("p16"), A_.is_gt)
    tt(view("tc"), view("tg"), view("te"), A_.mult)
    named("sd old")
    act(view("REP"), view("q15"))
    act(view("LT"), view("inn"), F_.Identity, 16.0, col("p128"))
    named("mb " * 8)
    select(view("K3"), view("ONE", 0, 16 * SLOTS), [[0, 16], [1, SLOTS]], A_.not_equal, 0.0, 0, 0)
    select(view("G8", parts=8), view("ONE", 0, 128, parts=8), [[1, 8], [0, 16]], A_.is_equal, 0.0, 0, -1)
    iota(view("CGO"), [[0, 16]], GO, 0)
    iota(view("DUM"), [[0, 8], [16, 2]], 2048, 0)
    iota(view("WS", 0, 48 * HOPS, 2), [[0, 24 * HOPS]], 0, 0)
    iota(view("SC", 1, 32 * HOPS, 2), [[25952, HOPS], [0, 16]], 0, 0)
    iota(view("C128"), [[0, 32]], -128, 0)
    iota(view("i2"), [[1, 16], [0, 2]], 0, 0)
    named("hu " * 6)
    diagonal("Nh Ih N128 N2 I9 I17")
    turn[0] = 1
    named("z3 " * 3)
    diagonal("I25 I2 I4")
    named("x6")
    ts(view("I6"), view("Ib"), EYES["I6"], A_.mult)
    turn[0] = 0
    named("sd sd")
    act(view("SC", 0, 32, 2), part(s0_, 0, 16))
    act(view("DUM"), view("DUM"), F_.Identity, 1.0, col("p16"))
    turn[0] = 2
    named("l1 l1 l2 l2 l3 l3")
    act(col("p240"), col("p16"), F_.Identity, -16.0, 240.0)
    act(col("p256"), col("p16"), F_.Identity, 16.0)
    act(col("q287"), col("q31i"), F_.Identity, 1.0, 256.0)
    act(view("DUP2", 0, 32), view("i2"), F_.Identity, 1.0, col("p256"))
    act(view("DUP2", 32, 64), view("i2"), F_.Identity, 1.0, col("p240"))
    act(view("UNF"), view("inn"), F_.Identity, 32.0, col("q287"))
    turn[0] = 0

    def key_differences():
        def diagonals(k0, slots, by_scalar):
            for k, slot in enumerate(slots.split(), k0):
                named(slot)
                if by_scalar:
                    act(mat("DG", k), view("I16"), F_.Identity, view("KD", k, k + 1))
                else:
                    ts(mat("DG", k), view("I16"), view("KD", k, k + 1), A_.mult)

        diagonals(0, "old old old", True)
        turn[0] += 1
        named("mis")
        act(view("KD", 8, 16), view("KN", 136, 144))
        diagonals(8, "jk jk jk jk", True)
        diagonals(12, "Nb Nb x7 x7", False)
        diagonals(3, "l1 l2", True)
        diagonals(5, "x5 x4 x4", False)
        turn[0] -= 1

    def differences():
        for d in range(8):
            named("")
            ts(mat("RD", d), view("D"), view("tc", d, d + 1), A_.is_equal, 4096, A_.mult)

    def slot(r):
        return (view("M2", r, None, SLOTS)[0], "slot%d" % r, 0, 16)

    def unpack(t, w):
        _, s_, U, F = state(t)
        named("U F s")
        low = part(w, 32, 48)
        acti(U, low, view("REP", 0, 4), F_.Sign, bias=0.5 - 2 ** 16)
        acti(F, low, view("REP", 0, 4), F_.Identity, 2.0 ** -12, FO - 0.25)
        acti(s_, part(w, 0, 32), view("ODD", 0, 4), F_.Identity, bias=-32.0)
        if t < HOPS:
            named("sc")
            copy("sc", view("SC", 32 * t, 32 * t + 32, 2), part(s_, 0, 16))

    def sites_of(t):
        return view("H16", 256 * t, 256 * t + 256)

    def site_numbers(t, piece, step, P, H):
        a, b = ((0, 64), (64, 128), (128, 256), (0, 128))[piece]
        named("uyzu"[piece] + str(step))
        if step == 0:
            tt(view("Z", a, b), part(P, a, b), view("DB" if a else "E0", 256 + a, 256 + b), A_.mult)
        elif step == 1:
            tt(view("ZI", a, b), view("Z", a, b), view("E1" if a >= 128 else "ZB", a, b), A_.add)
        elif step == 2:
            ts(view("HI", a, b), view("ZI", a, b), 5, A_.arith_shift_right, 2047, A_.bitwise_and)
        else:
            copy("uyzu"[piece] + "3" if t else "hp" if a else "", part(H, a, b), view("HI", a, b))

    def spreads(t, half, s_, U1):
        a, b = HALVES[half]
        bank = ("ZB", "E1")[half]
        tensor("32" + bank)
        mm(view(("E0", "DB")[half], 256 + a, 256 + b), view("F25"), view("ONE", 0, 128), True)
        tensor("s" + bank)
        for x in (a, a + 64):
            mm(view(("E0", "DB")[half], 256 + x, 320 + x), view("Ib"), s_, False, x > a)
        tensor("keys" + bank)
        mm(view(bank, a, b), view("BM16"), view(("KS", "KN")[half], 0, 128) if t else view("KTa", a, b), True)
        if not t:
            mm(view(bank, a, b), view("BM16"), view("KTa", a, b))
        tensor("sU" + bank)
        for x in (a, a + 64):
            mm(view(bank, x, x + 64), view("I1184"), s_, False, not t and x > a)
        for x in range(a, b if t else a, 16):
            mm(view(bank, x, x + 16), mat("DG", x // 16), U1, False, x == b - 16)

    def sites_ahead(t):
        w, names_ = view("WS", 48 * t, 48 * t + 48), view("CO", 256 * t, 256 * t + 256)
        named("sn Un")
        acti(view("sn"), part(w, 0, 32), view("ODD", 0, 4), F_.Identity, bias=-32.0)
        acti(view("Un"), part(w, 32, 48), view("REP", 0, 1), F_.Sign, bias=0.5 - 2 ** 16)
        spreads(t + 1, 1, view("sn"), view("Un"))
        for step in range(4):
            site_numbers(t + 1, 2, step, names_, view("HS", 128 * t - 128, 128 * t + 128))
        named("mh")
        send(1, part(sites_of(t + 1), 128, 256), view("HS", 128 * t, 128 * t + 128), "mh%d" % t)
        named("mb")
        send(1, part(state(t + 1)[0], 128, 256), part(names_, 128, 256), "mb%d" % t)

    def sites(t):
        P, s_, U, pc = state(t)
        U1 = part(U, 0, 16)
        d = t % n
        if t:
            unpack(t, view("WL", 48 * t, 48 * t + 48))
        turn[0] -= not t
        for half in range(1 if t else 2):
            spreads(t, half, s_, U1)
        if t:
            tensor("AO.")
            mm(view("Q0", 0, 16), view("Ib"), view("LT"), True)
            mm(view("Q0", 0, 16), view("N128"), U1, False, True)
            named("AO AC AD")
            act(view("AO"), view("Q0", 0, 16))
            acti(record(t), view("AR", 512 * d, 512 * d + 512), view("AO"))
            copy("AD", view("AC", 256, 512), record(t))
        for step in range(4):
            for piece in (3,) if t else (3, 2):
                site_numbers(t, piece, step, P, sites_of(t))
        turn[0] += not t
        if not t:
            differences()
        if t:
            tensor("SA.")
            spread("Q1", 256, "N2", pc, True)
            for k, eye in enumerate(("Ib", "I9", "I17", "I25")):
                mm(view("Q1", 256 + 64 * k, 320 + 64 * k), view(eye), U)
            for x in range(256, 512, 16):
                if x % 64:
                    mm(view("Q1", x, x + 16), view(("I2", "I4", "I6")[x % 64 // 16 - 1]), U1, False, x == 496)
            for nm, f, c in (("SA", F_.Sign, 0.5), ("SB", F_.Abs, 0.0) if PRS else ("SB", F_.Sign, -0.5), ("R1", F_.Identity, RO)):
                named(nm)
                act(view(nm), view("Q1", 256, 512), f, 0.5, FO + 15.5 + c)
            tensor("PR.")
            if PRS:
                mm(view("ZB", 256, 512), view("N4k"), view("SB"), True)
            else:
                mm(view("ZB", 256, 512), view("Ih"), view("SA"), True)
                mm(view("ZB", 256, 512), view("Nh"), view("SB"), False, True)
        tensor("pay.")
        mm(view("CB", 0, 256), view("Fhit"), view("ONE"), True)
        mm(view("CB", 240, 256), view("N64k"), view("ONE", 0, 16))
        tensor("payF.")
        spread("CB", 0, "I4k", pc)
        mm(view("CB", 240, 256), view("N64k"), U1)
        tensor("HK.")
        mm(view("CB", 0, 256), view("I260k"), view("R1"))
        tensor("mask.")
        for x, r, s in ((0, "I4k", "N32k"), (256, "N4k", "I34k")):
            mm(view("RG", x, x + 256), view(r), view("R1"), not x)
            mm(view("RG", x, x + 256), view(s), view("SA" if t else "ONE"))

    def row_p(t):
        named("Hf PR HK" if t else "c0 HK")
        copy("Hf" if t else "", view("Hf"), sites_of(t))
        if t and PRS:
            tensor("PS.")
            mm(view("ZB", 256, 512), view("Ib"), view("Hf"), False, True)
            act(view("PR"), view("ZB", 256, 512), F_.Relu)
        elif t:
            tt(view("PR"), sites_of(t), view("ZB", 256, 512), A_.mult)
        tensor("Hf.")
        mm(view("CB", 0, 256), view("Ib"), view("Hf"), False, True)
        act(view("HK"), view("CB", 0, 256), F_.Identity, bias=HIT - 128 * HIT_SUM)
        tensor("hp.")
        if t:
            for k in range(4):
                mm(view(PB, 288, 352), view("Ib"), view("PR", 64 * k, 64 * k + 64), k == 0, k == 3)
            named("h4")
            copy("h4", view("h4"), view(PB, 288, 352))
            tensor("h4.")
            for k in range(4):
                mm(view(PB, 272, 288), view("Ib"), view("h4", 16 * k, 16 * k + 16), k == 0, k == 3)

    def pairs_open(t):
        P, s_, U, pc = state(t)
        hp = view(PB, 272, 288) if t else view("H16", 0, 16)
        named("hp hu Mm HO HE" if t else "hp Mm HO HE")
        copy("hp", view("hp"), hp)
        if t:
            copy("hu", view("hu"), view("hp") if COPIES.get("hu") == "g" else hp)
        o = view(PB, 256, 272)
        tensor("Mm.")
        mm(o, view("N4k"), part(pc, 0, 16), True)
        mm(o, view("Ib"), view("hp"), False, True)
        for i in range(16):
            mm(view(PB, 8 * i, 8 * i + 8, parts=8), view("Ib", i, 128, 16), view("hp", 1, 16, 2), i == 0, i == 15)
        act(slot(8), o, F_.Identity, bias=MISS)
        copy("HO", view("HO", parts=8), view(PB, 0, 128, parts=8))
        o = view(PB, 384, 512)
        tensor("HE.")
        for k in range(4):
            mm(part(o, 32 * k, 32 * k + 32), view("N4k"), view(pc[1], pc[2], pc[3], 2), k == 0)
        mm(o, view("G8", parts=8), view("HO", parts=8), False, True)
        act(view("HE"), o, F_.Identity, bias=MISS)

    def distances(t):
        kind, pairs = "".join(CHUNKS), [0]

        def span(buf, k, m=1):
            return view(buf, 256 * k, 256 * (k + m))

        def gather(k, m):
            off = part(sites_of(t), 16 * k, 16 * (k + m))
            if kind[k] == "S":
                acti(span("DR", k, m), SITES, off)
            else:
                tti(span("DR", k, m), SITES, off, view("AC", 0, 256 * m), A_.subtract)

        def size(k, m):
            if kind[k] == "S":
                q = ("Q0", "Q1", "DB")[pairs[0]]
                pairs[0] += 1
                tensor("A%x." % k)
                for x in range(m):
                    mm(view(q, 256 * x, 256 * x + 256), view("NI"), record(t), x == 0)
                tensor("X%x." % k)
                mm(view(q, 0, 256 * m), view("Ib"), span("DR", k, m), False, True)
                act(span("DA", k, m), view(q, 0, 256 * m), F_.Abs)
            elif kind[k] == "A":
                act(span("DA", k, m), span("DR", k, m), F_.Abs)
            elif kind[k] == "H":
                k0, rows = kind.index("H"), kind.count("H")
                a = 256 * k0 + 128 * (k - k0)
                act(view("DA", a, a + 128 * m), view("DR", 256 * k, 256 * (k + m), 2), F_.Abs)
                a += 128 * rows
                named("r%x" % k)
                ts(view("DA", a, a + 128 * m), view("DR", 256 * k + 1, 256 * (k + m), 2), 0.0, A_.max, 2.0, A_.mult)
            else:
                ts(span("DA", k, m), span("DR", k, m), 0.0, A_.max, 2.0, A_.mult)

        def decide(c):
            kinds, k0 = CHUNKS[c], len("".join(CHUNKS[:c]))
            rows = len(kinds)
            e = view(BANKS[c], 0, 64)
            tensor("D%d." % c)
            mm(e, view("TH"), view("C32k"), True)
            for i in range(16 if "R" in kinds else 0):
                a, b = kinds.index("R"), kinds.rindex("R") + 1
                mm(part(e, 16 * a, 16 * b), view("LP", 15 - i, 143 - i), view("DR", 256 * (k0 + a) + i, 256 * (k0 + b), 16))
            if "H" in kinds:
                tensor("L%d." % c)
                for i in range(1, 16, 2):
                    mm(e, view("LP", 15 - i, 143 - i), view("DR", 256 * k0 + i, 256 * (k0 + rows), 16))
                for odd in (1, 0):
                    tensor("EO"[odd] + "%d." % c)
                    a = 256 * k0 + 128 * rows * odd
                    for i in range(odd, 16, 2):
                        mm(e, view("LE", 15 - i, 143 - i), view("DA", a + i // 2, a + 128 * rows, 8), False, i == 14)
                return
            tensor("E%d." % c)
            for i in range(16):
                mm(e, view("LE", 15 - i, 143 - i), view("DA", 256 * k0 + i, 256 * (k0 + rows), 16), False, i == 15)

        def choose(c, step):
            rows, e, hk = 4, view(BANKS[c], 0, 64), view("HK", 64 * c, 64 * c + 64)
            if step == "m":
                tt(e if c else view("M"), e, hk, A_.min)
            elif step == "x":
                tt(view("M"), e, view("M"), A_.max)
            elif step == "f":
                for r in range(rows):
                    tt(slot(4 + r), part(e, 16 * r, 16 * r + 16), view("M", 16 * r, 16 * r + 16), A_.max)
            else:
                for r in range(rows):
                    tt(slot(r), part(e, 16 * r, 16 * r + 16), part(hk, 16 * r, 16 * r + 16), A_.min)
                call("v", lambda: g.vector.tensor_tensor_scan(T.W[:], T.K3[:], T.M2[:], 0.0, A_.mult, A_.max), [view("W")],
                     [view("K3")] + [slot(r) for r in range(SLOTS)], 16 * SLOTS * CYCLE)

        for step in STEPS.split():
            k = int(step[1], 16)
            if step[0] in "GHbcm":
                named(step)
            elif step[0] in "xwf":
                named({"x": "xm", "f": "xa xb xc xd", "w": "wa wb wc wd w2"}[step[0]])
            if step[0] in "GH":
                gather(k, 2 if step[0] == "G" else 4)
            elif step[0] == "d":
                decide(k)
            elif step[0] in "mfxw":
                choose(k, step[0])
            elif step[0] == "h":
                row_p(t)
            elif step[0] == "p":
                pairs_open(t)
            else:
                size(k, 2 if step[0] == "b" else 4)

    def writes(t):
        if t:
            named("old")
            acti(view("old"), SITES, view("hu"))
        tensor("n1.")
        mm(view("E1", 256, 512), view("Ib"), record(t), True)
        if t:
            mm(view("E1", 256, 512), view("Ib"), view("old"), False, True)
        else:
            if CHUNKS[0][0] != "S":
                mm(view("E1", 256, 512), view("Ib"), record(t))
            mm(view("E1", 256, 512), view("Ib"), view("DR", 0, 256), False, True)
        tensor("pairs.")
        for d in range(8):
            mm(view("DB", 16 * d, 16 * d + 16), mat("SH", d), view("hp"), d == 0)
        tensor("hq.")
        mm(view("Q1", 0, 16), view("Ib"), view("hp"), True)
        mm(view("Q1", 0, 16), view("N4k"), view("CGO"))
        turn[0] += 1
        named("n1 GW ex eq fo x7 x6 x5 x4 x3 x2 x1 x0")
        act(view("n1"), view("E1", 256, 512), F_.Identity, 0.5, 127.75)
        acti(view("G4"), view("W"), view("R4", 0, 4), F_.Identity, 2.0 ** -5, (GO - 0.4925) * 4096)
        tti(view("ex"), view("W"), view("EV", 0, 8), view("HE"), A_.is_equal)
        tensor("eq.")
        for d in range(8):
            mm(view("DB", 16 * d, 16 * d + 16), mat("SH", d), view("G4", 0, 16), False, d == 7)
        tensor("ex.")
        mm(view("Q1", 0, 16), view("Ib"), view("G4", 0, 16))
        ts(view("eq"), view("DB", 0, 128), 0, A_.is_equal)
        for i in range(16):
            mm(view("Q1", 1, 16, 2), view("LP", 15 - i, 143 - i), view("ex", 8 * i, 8 * i + 8))
        tensor("fo.")
        for d in range(8):
            mm(view("Q1", 0, 16), mat("RD", d), view("eq", 16 * d, 16 * d + 16), False, d == 7)
        tt(view("fo", 0, 16), view("Q1", 0, 16), view("DUM"), A_.min)
        for j in range(14, -1, -2):
            scat(view("X"), view("fo", j, j + 2), view("n1", 16 * j, 16 * j + 32), view("C128"))

    def limit():
        named("mis jk l1 l2 l3 TH")
        act(view("mis"), view("G4", 0, 16), F_.Relu, -1.0 / 4096, GO + 1.0)
        tensor("jk.")
        mm(view("Q0", 64, 80), view("ONE", 0, 128), view("mis"), True, True)
        act(view("jk"), view("Q0", 64, 80), F_.Identity, bias=-7.5 / 16, acc=col("mc"))
        act(col("m1"), col("mc"), F_.Identity, bias=ROUND16)
        act(col("m2"), col("m1"), F_.Identity, -1.0, ROUND16)
        act(col("m3"), col("m2"), F_.Identity, bias=74.5)
        act(view("TH"), view("ONE", 0, 128), F_.Identity, col("mc"), col("m3"))

    def become(t, names_):
        P = state(t)[0]
        named("hs low sf bq")
        ts(view("WS", 48 * t + 1, 48 * t + 32, 2), view("W", SLOTS - 1, None, SLOTS), 4095, A_.bitwise_and)
        ts(view("WS", 48 * t + 32, 48 * t + 48), view("W", SLOTS - 1, None, SLOTS), 2 ** 17 - 1, A_.bitwise_and)
        o, d0, d1 = view("sh", 0, 32), view("WS", 48 * t, 48 * t + 32), view("SC", 32 * t, 32 * t + 32)
        call("v", lambda: g.vector.tensor_tensor_scan(o[0], d0[0], d1[0], 0.0, A_.mult, A_.add), [o], [d0, d1], 64 * CYCLE)
        tsi(view("bq"), o, view("ODD", 0, 4), 5, A_.arith_shift_right, 2047, A_.bitwise_and)
        tensor("Pa.")
        spread("RG", 0, "Nh", view("G4"))
        spread("RG", 256, "Ih", view("G4"), stop=True)
        tensor(None)
        for a, b in HALVES:
            fold = t < HOPS - 1 and not a
            named(("Pb t2 t3" if a else "Pa t0 t1") + ("" if fold else " Nb" if a else " Na"))
            tt(part(names_, a, b) if fold else view("RG", a, b), part(P, a, b), view("RG", a, b), A_.min)
            for x in range(a, b, 64):
                tt(view("CP", 256 * t + x, 256 * t + x + 64) if fold else view("tP", x, x + 64), view("bq"), view("RG", 256 + x, 320 + x), A_.min)
            if not fold:
                tt(part(names_, a, b), view("tP", a, b), view("RG", a, b), A_.max)

    def finish():
        unpack(HOPS, view("WS", 48 * HOPS - 48, 48 * HOPS))
        _, sn, Un, pn_ = state(HOPS)
        tensor("U.")
        mm(view("ZB", 0, 16), view("Ib"), view("UNF"), True)
        mm(view("ZB", 0, 16), view("N128"), part(Un, 0, 16))
        mm(view("ZB", 0, 16), view("N128"), part(Un, 0, 16), False, True)
        named("Uo")
        act(view("UN2"), view("ZB", 0, 16))
        for a, h in zip(range(0, 1024, 256), "abcd"):
            named("D%s T%s" % (h, h))
            acti(view("TA", a, a + 256), view("Pf"), view("DUP2", a // 16, a // 16 + 16))
            turn32(view("TB", a, a + 256), view("TA", a, a + 256))
        named("Un")
        acti(view("yl"), view("TB"), view("UN2"))
        store("s", T.yn[:], view("yl"), "oz")
        named("y1 sp sq so")
        ts(view("y1"), part(Un, 0, 16), -16.0, A_.mult, -FO, A_.add)
        cp(view("sp", 0, 16), part(sn, 0, 16))
        tt(view("sp", 16, 32), part(pn_, 0, 16), view("y1"), A_.add)
        tensor("sp.")
        for i in range(16):
            mm(view("CB", i, 512, 16, parts=8), view("Ib", i, 128, 16), view("sp"), i == 0, i == 15)
        act(view("so", parts=8), view("CB", parts=8))
        store("y", T.ys[:], view("so", 0, 256, parts=8), "oy")
        store("y", T.yp[:], view("so", 256, 512, parts=8), "oy")
        store("y", T.yx[:], SITES, "oy")

    sites(0)
    named("ms")
    send(-1, view("KN"), view("KS", 128, 272), "kn", [SITES])
    for t in range(HOPS):
        if t < n - 1:
            named("" if t else "ma")
            send(t + 1, view("AR", 512 * t + 512, 512 * t + 1024), view("AR", 0, 512), "ar%d" % (t + 1), [part(sites_of(t), 0, 64)])
        distances(t)
        if not t:
            key_differences()
        writes(t)
        if t < HOPS - 1:
            limit()
            become(t, view("CO", 256 * t, 256 * t + 256))
            named("ms")
            send(1, view("WL", 48 * t + 48, 48 * t + 96), view("WS", 48 * t, 48 * t + 48), "ms%d" % t)
            named("ma")
            send(1, part(state(t + 1)[0], 0, 128), view("CO", 256 * t, 256 * t + 128), "ma%d" % t, other=view("CP", 256 * t, 256 * t + 128))
            sites_ahead(t)
            sites(t + 1)
        else:
            become(t, view("Pf"))
            finish()

    cnt = {q: 0 for q in QS}
    seen = {q: {} for q in Q}
    log, total = {}, {"snd": 0}

    def need(q, ev):
        if seen[q].get(ev[0], 0) < ev[1]:
            seen[q][ev[0]] = ev[1]
            Q[q].wait_ge(T.sem[ev[0]], ev[1])

    def order(q, outs, ins):
        todo = {}
        for vs, wr in ((ins, False), (outs, True)):
            for _, nm, a, b in vs:
                ps = nm in PS
                for (q2, a2, b2, w2), ev in log.get(nm, {}).items():
                    hitx = a < b2 and a2 < b
                    dep = (hitx and (wr or w2) and not q == q2 == "p") or (q2 != q and ps)
                    if dep and todo.get(ev[0], 0) < ev[1]:
                        todo[ev[0]] = ev[1]
        for k in sorted(todo):
            need(q, (k, todo[k]))

    def note(q, outs, ins, ev):
        for vs, wr in ((ins, False), (outs, True)):
            for _, nm, a, b in vs:
                d = log.setdefault(nm, {})
                if wr and nm not in PS:
                    for k in [k for k in d if a <= k[1] and k[2] <= b]:
                        del d[k]
                d[(q, a, b, wr)] = ev

    if not ORDER:
        ORDER.extend(plan(calls, needs(calls)))
    for c in [calls[k] for k in ORDER]:
        q = c["q"]
        if c["kind"] == "land":
            note(q, c["outs"], [], (c["sem"], c["count"]))
            continue
        order(q, c["outs"], c["ins"])
        if c["kind"] == "send":
            c["fn"]()
            total["snd"] += c["count"]
        elif c["kind"] == "dma":
            c["fn"]().then_inc(T.sem[c["sem"]], 16)
            total[c["sem"]] = total.get(c["sem"], 0) + 16
            note("dma", c["outs"], [], (c["sem"], 16))
        else:
            cnt[q] += 1
            c["fn"]().then_inc(T.sem[QS[q]], 1)
            note(q, c["outs"], c["ins"], (QS[q], cnt[q]))
    for q in QS:
        need("g", (QS[q], cnt[q]))
    for sem in total:
        need("g", (sem, total[sem]))
